import numpy as np
import ml_dtypes


def mxq(x, axis, fmt="e4m3"):
    dtype, down = {"e4m3": (ml_dtypes.float8_e4m3fn, 7), "e5m2": (ml_dtypes.float8_e5m2, 14)}[fmt]
    v = np.moveaxis(np.asarray(x, np.float32).astype(ml_dtypes.bfloat16).astype(np.float64), axis, -1)
    blocks = v.reshape(v.shape[:-1] + (-1, 32))
    amax = np.abs(blocks).max(-1, keepdims=True)
    byte = np.maximum(np.where(amax > 0, np.frexp(amax)[1] - 1 + 127, 0) - down, 1)
    scale = np.exp2(byte - 127.0)
    codes = (blocks / scale).astype(np.float32).astype(dtype).astype(np.float64)
    return np.moveaxis((codes * scale).reshape(v.shape), -1, axis)


WIDE = False


def mx_kscale(k):
    if not WIDE:
        return np.ones(k)
    levels = np.array([10, -10, 5, -5, 0])
    if k % 512:
        return np.exp2(np.random.permutation(np.resize(levels, k // 32))).repeat(32)
    a = np.empty((k // 512, 16))
    for p in range(k // 512):
        a[p, :8] = np.random.permutation(np.resize(levels, 8))
        for g in range(8):
            far = levels[np.abs(levels - a[p, g]) >= 10]
            a[p, g + 8] = far[np.random.randint(len(far))]
    return np.exp2(a.ravel()).repeat(32)


def f64(x):
    return np.asarray(x).astype(np.float64)


def striped(idx):
    return np.tile(idx.reshape(-1, 16).T, (8, 1)).astype(np.uint16)


def unstriped(offs):
    return offs[:16].T.reshape(-1).astype(np.int64)


def silu(v):
    return v / (1.0 + np.exp(-np.maximum(v, -700.0)))


K, T, D, S, V, H, N = 512, 2048, 2, 1024, 512, 512, 128
P = 2 ** 7


def setup_inputs():
    n = np.random.standard_normal
    s = mx_kscale(K)[:, None]
    u = mx_kscale(H)
    q = np.random.permutation(S)
    return {
        "xT": (n((K, T)) * s).astype(np.float32),
        "w1": (n((K, H)) / np.sqrt(K) / s * u).astype(np.float32),
        "w2": (n((H, N)) / np.sqrt(H) / u[:, None]).astype(np.float32),
        "gate": np.tile(np.random.uniform(0.2, 1.0, (D, 1, V)) / np.sqrt(D), (1, P, 1)).astype(np.float32),
        "offs": striped(np.random.permutation(T)[:S]),
        "pos1": striped(q[:V]),
        "pos2": striped(q[V:]),
    }


def reference(xT, w1, w2, gate, offs, pos1, pos2):
    h = silu(mxq(f64(w1), 0, "e4m3").T @ mxq(f64(xT)[:, unstriped(offs)], 0, "e4m3"))
    z = sum(f64(gate)[d, :1] * h[:, unstriped(p)] for d, p in enumerate((pos1, pos2)))
    return mxq(f64(w2), 0, "e4m3").T @ mxq(z, 0, "e4m3")

@@ -1,0 +1,186 @@
+from contextlib import ExitStack
+
+import concourse.mybir as mybir
+
+K, T, D, S, V, H, N = 512, 2048, 2, 1024, 512, 512, 128
+FLOPS = 2 * K * H * S + 2 * H * N * V
+
+F32 = mybir.dt.float32
+BF16 = mybir.dt.bfloat16
+U32 = mybir.dt.uint32
+U16 = mybir.dt.uint16
+U8 = mybir.dt.uint8
+FP8X4 = mybir.dt.float8_e4m3fn_x4
+COPY = mybir.ActivationFunctionType.Copy
+SILU = mybir.ActivationFunctionType.Silu
+ADD = mybir.AluOpType.add
+MULT = mybir.AluOpType.mult
+
+P = 128
+J = 4
+
+
+def tile_picked_sage_silu_e_kernel(tc, xT, w1, w2, gate, offs, pos1, pos2, out):
+    nc = tc.nc
+    with ExitStack() as ctx:
+        keep = ctx.enter_context(tc.tile_pool(name="keep", bufs=1))
+        psum = ctx.enter_context(tc.psum_pool(name="psum", bufs=1))
+
+        offs_sb = keep.tile([P, S // 16], U16, name="offs_sb")
+        pos1_sb = keep.tile([P, V // 16], U16, name="pos1_sb")
+        pos2_sb = keep.tile([P, V // 16], U16, name="pos2_sb")
+        gate_sb = keep.tile([P, D, V], F32, name="gate_sb")
+        w1_raw = keep.tile([P, J, H], F32, name="w1_raw")
+        w2_raw = keep.tile([P, J, N], F32, name="w2_raw")
+        w1_c = keep.tile([P, H], U32, name="w1_c", align_bytes=64)
+        w1_s = keep.tile([P, H], U8, name="w1_s", align_bytes=64)
+        w2_c = keep.tile([P, N], U32, name="w2_c", align_bytes=64)
+        w2_s = keep.tile([P, N], U8, name="w2_s", align_bytes=64)
+        xb = [keep.tile([P, T * 2], BF16, name=f"xb{u}", align_bytes=64) for u in range(2)]
+        early = keep.tile([P, S * J + P * J], BF16, name="early", tag="stage", align_bytes=64)
+        grouped = early[:, : S * J]
+        x_c = keep.tile([P, 768], U32, name="x_c", align_bytes=64)
+        x_s = keep.tile([P, S], U8, name="x_s", align_bytes=64)
+        w1_e0 = keep.tile([P, P * J], BF16, name="w1_e0", tag="first", align_bytes=64)
+        h = [keep.tile([P, S], F32, name=f"h{t}", align_bytes=64) for t in range(J)]
+        m = [keep.tile([P, J, V], F32, name=f"m{d}", align_bytes=64) for d in range(D)]
+        z_b = keep.tile([P, V * J], BF16, name="z_b", align_bytes=64)
+        z_c = keep.tile([P, V], U32, name="z_c", align_bytes=64)
+        z_s = keep.tile([P, V], U8, name="z_s", align_bytes=64)
+        o_sb = keep.tile([P, V], F32, name="o_sb", align_bytes=64)
+        warm = keep.tile([P, 1], F32, name="warm")
+
+        nc.vector.memset(warm[:], 0.0)
+        nc.scalar.activation(warm[:], warm[:], SILU)
+
+        x_view = xT.rearrange("(p u e) t -> p u e t", u=2, e=2)
+        chunks = [(0, 0, 1024), (0, 1024, 1024), (1, 0, 1024), (1, 1024, 512), (1, 1536, 512)]
+        raws = []
+        for i, (u, c0, n) in enumerate(chunks):
+            raw = keep.tile([P, 2, n], F32, name=f"x_raw{i}", align_bytes=64)
+            nc.sync.dma_start(out=raw[:], in_=x_view[:, u, :, c0 : c0 + n])
+            raws.append(raw)
+            if i == 0:
+                nc.sync.dma_start(out=offs_sb[:], in_=offs)
+        w1_view = w1.rearrange("(p j) c -> p j c", j=J)
+        for c0 in (0, H // 2):
+            nc.sync.dma_start(out=w1_raw[:, :, c0 : c0 + H // 2], in_=w1_view[:, :, c0 : c0 + H // 2])
+        nc.sync.dma_start(out=pos1_sb[:], in_=pos1)
+        nc.sync.dma_start(out=gate_sb[:], in_=gate.rearrange("d p v -> p d v"))
+        nc.sync.dma_start(out=w2_raw[:], in_=w2.rearrange("(p j) n -> p j n", j=J))
+        nc.sync.dma_start(out=pos2_sb[:], in_=pos2)
+
+        g_words = grouped.bitcast(U32).rearrange("p (s u) -> p s u", u=2)
+
+        def round_cols(i, a, n, on_vector):
+            u, c0 = chunks[i][:2]
+            dst = xb[u][:, 2 * (c0 + a) : 2 * (c0 + a + n)].rearrange("p (t e) -> p t e", e=2)
+            src = raws[i][:, :, a : a + n].rearrange("p e t -> p t e")
+            if on_vector:
+                nc.vector.tensor_copy(out=dst, in_=src)
+            else:
+                nc.scalar.activation(dst, src, COPY)
+
+        def gather(u, s0, n):
+            nc.vector.tensor_copy(
+                out=g_words[:, s0 : s0 + n, u],
+                in_=xb[u][:].bitcast(U32).indirect(offs_sb[:, s0 // 16 : (s0 + n) // 16]),
+            )
+
+        def quantize(codes, scales, src, c0, n, s0=None):
+            s0 = c0 if s0 is None else s0
+            nc.vector.quantize_mx(
+                out=codes[:, c0 : c0 + n].bitcast(FP8X4),
+                scales=scales[:, c0 : c0 + n],
+                in_=src[:, J * s0 : J * (s0 + n)],
+            )
+
+        def split(i, n_vector):
+            n = chunks[i][2]
+            if n_vector:
+                round_cols(i, 0, n_vector, True)
+            round_cols(i, n_vector, n - n_vector, False)
+
+        split(0, 512)
+        split(1, 512)
+        gather(0, 0, S)
+        split(2, 512)
+        split(3, 320)
+        split(4, 320)
+        w1_src = w1_raw[:].rearrange("p j (m t) -> p m t j", t=J)
+        w1_e1 = early[:, S * J :]
+        for t, dst in ((0, w1_e0[:]), (1, w1_e1)):
+            for m0 in (0, P // 2):
+                nc.scalar.activation(
+                    dst.rearrange("p (m j) -> p m j", j=J)[:, m0 : m0 + P // 2], w1_src[:, m0 : m0 + P // 2, t], COPY
+                )
+        gather(1, 0, 768)
+        quantize(x_c, x_s, grouped, 0, 512)
+        quantize(x_c, x_s, grouped, 512, 256)
+        quantize(w1_c, w1_s, w1_e0, 0, P)
+        gather(1, 768, 256)
+        x_c2 = keep.tile([P, 256], U32, name="x_c2", tag="first", align_bytes=64)
+        nc.vector.quantize_mx(
+            out=x_c2[:].bitcast(FP8X4), scales=x_s[:, 768:], in_=grouped[:, 768 * J :]
+        )
+
+        banks = [psum.tile([P, 512], F32, name=f"bank{i}") for i in range(8)]
+
+        def layer1(t):
+            for s0, n in ((0, 512), (512, 256), (768, 256)):
+                codes = x_c[:, s0 : s0 + n] if s0 < 768 else x_c2[:]
+                nc.tensor.matmul_mx(
+                    out=banks[2 * t + s0 // 512][:, s0 % 512 : s0 % 512 + n],
+                    lhsT=w1_c[:, P * t : P * t + P].bitcast(FP8X4),
+                    lhsT_scale=w1_s[:, P * t : P * t + P],
+                    rhs=codes.bitcast(FP8X4),
+                    rhs_scale=x_s[:, s0 : s0 + n],
+                    start=True,
+                    stop=True,
+                )
+            for half in range(2):
+                nc.scalar.activation(h[t][:, half * 512 : half * 512 + 512], banks[2 * t + half][:], SILU)
+
+        layer1(0)
+        quantize(w1_c, w1_s, w1_e1, P, P, 0)
+        late = keep.tile([P, 2 * P * J + N * J], BF16, name="late", tag="stage", align_bytes=64)
+        w1_late = late[:, : 2 * P * J]
+        w2_late = late[:, 2 * P * J :]
+        nc.vector.tensor_copy(out=w1_late.rearrange("p (t m j) -> p m t j", t=2, j=J), in_=w1_src[:, :, 2:])
+        quantize(w1_c, w1_s, w1_late, 2 * P, 2 * P, 0)
+        nc.vector.tensor_copy(out=w2_late.rearrange("p (n j) -> p n j", j=J), in_=w2_raw[:].rearrange("p j n -> p n j"))
+        for t in range(1, J):
+            layer1(t)
+        for t in range(J):
+            for d, pos in enumerate((pos1_sb, pos2_sb)):
+                nc.vector.tensor_tensor(m[d][:, t, :], h[t][:].indirect(pos[:]), gate_sb[:, d, :], MULT)
+
+        def add(v0, n):
+            pat = "p t (c i) -> p c t i"
+            nc.vector.tensor_tensor(
+                z_b[:, J * v0 : J * (v0 + n)].rearrange("p (c i t) -> p c t i", t=J, i=4),
+                m[0][:, :, v0 : v0 + n].rearrange(pat, i=4),
+                m[1][:, :, v0 : v0 + n].rearrange(pat, i=4),
+                ADD,
+            )
+
+        half_v = V // 2
+        quantize(w2_c, w2_s, w2_late, 0, N)
+        add(0, half_v)
+        add(half_v, half_v)
+        for i in range(2):
+            quantize(z_c, z_s, z_b, i * half_v, half_v)
+        for i in range(2):
+            sl = slice(i * half_v, (i + 1) * half_v)
+            acc = banks[i]
+            nc.tensor.matmul_mx(
+                out=acc[:, :half_v],
+                lhsT=w2_c[:].bitcast(FP8X4),
+                lhsT_scale=w2_s[:],
+                rhs=z_c[:, sl].bitcast(FP8X4),
+                rhs_scale=z_s[:, sl],
+                start=True,
+                stop=True,
+            )
+            nc.scalar.copy(o_sb[:, sl], acc[:, :half_v])
+            nc.sync.dma_start(out=out[:, sl], in_=o_sb[:, sl])

@@ -1,6 +1,7 @@
 from contextlib import ExitStack
 
 import concourse.mybir as mybir
+from concourse.masks import make_identity
 
 K, T, D, S, V, H, N = 512, 2048, 2, 1024, 512, 512, 128
 FLOPS = 2 * K * H * S + 2 * H * N * V
@@ -18,6 +19,7 @@ MULT = mybir.AluOpType.mult
 
 P = 128
 J = 4
+BANK = 512
 
 
 def tile_picked_sage_silu_e_kernel(tc, xT, w1, w2, gate, offs, pos1, pos2, out):
@@ -30,28 +32,31 @@ def tile_picked_sage_silu_e_kernel(tc, xT, w1, w2, gate, offs, pos1, pos2, out):
         pos1_sb = keep.tile([P, V // 16], U16, name="pos1_sb")
         pos2_sb = keep.tile([P, V // 16], U16, name="pos2_sb")
         gate_sb = keep.tile([P, D, V], F32, name="gate_sb")
-        w1_raw = keep.tile([P, J, H], F32, name="w1_raw")
+        w1_raw = [keep.tile([P, J, H // 2], F32, name=f"w1_raw{i}") for i in range(2)]
         w2_raw = keep.tile([P, J, N], F32, name="w2_raw")
+        w1_lo = keep.tile([P, 2 * P * J], BF16, name="w1_lo", tag="first", align_bytes=64)
+        w1_hi = keep.tile([P, 2 * P * J], BF16, name="w1_hi", align_bytes=64)
+        w2_b = keep.tile([P, N * J], BF16, name="w2_b", align_bytes=64)
         w1_c = keep.tile([P, H], U32, name="w1_c", align_bytes=64)
         w1_s = keep.tile([P, H], U8, name="w1_s", align_bytes=64)
         w2_c = keep.tile([P, N], U32, name="w2_c", align_bytes=64)
         w2_s = keep.tile([P, N], U8, name="w2_s", align_bytes=64)
         xb = [keep.tile([P, T * 2], BF16, name=f"xb{u}", align_bytes=64) for u in range(2)]
-        early = keep.tile([P, S * J + P * J], BF16, name="early", tag="stage", align_bytes=64)
-        grouped = early[:, : S * J]
-        x_c = keep.tile([P, 768], U32, name="x_c", align_bytes=64)
+        grouped = keep.tile([P, S * J], BF16, name="grouped", align_bytes=64)
         x_s = keep.tile([P, S], U8, name="x_s", align_bytes=64)
-        w1_e0 = keep.tile([P, P * J], BF16, name="w1_e0", tag="first", align_bytes=64)
         h = [keep.tile([P, S], F32, name=f"h{t}", align_bytes=64) for t in range(J)]
         m = [keep.tile([P, J, V], F32, name=f"m{d}", align_bytes=64) for d in range(D)]
         z_b = keep.tile([P, V * J], BF16, name="z_b", align_bytes=64)
+        zt = keep.tile([P, V * 2], BF16, name="zt", align_bytes=64)
         z_c = keep.tile([P, V], U32, name="z_c", align_bytes=64)
         z_s = keep.tile([P, V], U8, name="z_s", align_bytes=64)
         o_sb = keep.tile([P, V], F32, name="o_sb", align_bytes=64)
+        ident = keep.tile([P, P], F32, name="ident", align_bytes=64)
         warm = keep.tile([P, 1], F32, name="warm")
 
         nc.vector.memset(warm[:], 0.0)
         nc.scalar.activation(warm[:], warm[:], SILU)
+        make_identity(nc, ident[:])
 
         x_view = xT.rearrange("(p u e) t -> p u e t", u=2, e=2)
         chunks = [(0, 0, 1024), (0, 1024, 1024), (1, 0, 1024), (1, 1024, 512), (1, 1536, 512)]
@@ -63,14 +68,14 @@ def tile_picked_sage_silu_e_kernel(tc, xT, w1, w2, gate, offs, pos1, pos2, out):
             if i == 0:
                 nc.sync.dma_start(out=offs_sb[:], in_=offs)
         w1_view = w1.rearrange("(p j) c -> p j c", j=J)
-        for c0 in (0, H // 2):
-            nc.sync.dma_start(out=w1_raw[:, :, c0 : c0 + H // 2], in_=w1_view[:, :, c0 : c0 + H // 2])
+        for i in range(2):
+            nc.sync.dma_start(out=w1_raw[i][:], in_=w1_view[:, :, i * H // 2 : (i + 1) * H // 2])
         nc.sync.dma_start(out=pos1_sb[:], in_=pos1)
         nc.sync.dma_start(out=gate_sb[:], in_=gate.rearrange("d p v -> p d v"))
-        nc.sync.dma_start(out=w2_raw[:], in_=w2.rearrange("(p j) n -> p j n", j=J))
         nc.sync.dma_start(out=pos2_sb[:], in_=pos2)
+        nc.sync.dma_start(out=w2_raw[:], in_=w2.rearrange("(p j) n -> p j n", j=J))
 
-        g_words = grouped.bitcast(U32).rearrange("p (s u) -> p s u", u=2)
+        g_words = grouped[:].bitcast(U32).rearrange("p (s u) -> p s u", u=2)
 
         def round_cols(i, a, n, on_vector):
             u, c0 = chunks[i][:2]
@@ -97,90 +102,104 @@ def tile_picked_sage_silu_e_kernel(tc, xT, w1, w2, gate, offs, pos1, pos2, out):
 
         def split(i, n_vector):
             n = chunks[i][2]
-            if n_vector:
-                round_cols(i, 0, n_vector, True)
+            round_cols(i, 0, n_vector, True)
             round_cols(i, n_vector, n - n_vector, False)
 
+        def interleave(dst, raw):
+            nc.scalar.activation(dst.rearrange("p (c j) -> p c j", j=J), raw.rearrange("p j c -> p c j"), COPY)
+
         split(0, 512)
-        split(1, 512)
+        split(1, 672)
         gather(0, 0, S)
-        split(2, 512)
+        split(2, 384)
         split(3, 320)
         split(4, 320)
-        w1_src = w1_raw[:].rearrange("p j (m t) -> p m t j", t=J)
-        w1_e1 = early[:, S * J :]
-        for t, dst in ((0, w1_e0[:]), (1, w1_e1)):
-            for m0 in (0, P // 2):
+        for i in range(2):
+            for u, dst in enumerate((w1_lo, w1_hi)):
                 nc.scalar.activation(
-                    dst.rearrange("p (m j) -> p m j", j=J)[:, m0 : m0 + P // 2], w1_src[:, m0 : m0 + P // 2, t], COPY
+                    dst[:].rearrange("p (e c j) -> p c e j", e=2, j=J)[:, i * P // 2 : (i + 1) * P // 2],
+                    w1_raw[i][:].rearrange("p j (c t) -> p c t j", t=J)[:, :, 2 * u : 2 * u + 2],
+                    COPY,
                 )
-        gather(1, 0, 768)
-        quantize(x_c, x_s, grouped, 0, 512)
-        quantize(x_c, x_s, grouped, 512, 256)
-        quantize(w1_c, w1_s, w1_e0, 0, P)
-        gather(1, 768, 256)
-        x_c2 = keep.tile([P, 256], U32, name="x_c2", tag="first", align_bytes=64)
-        nc.vector.quantize_mx(
-            out=x_c2[:].bitcast(FP8X4), scales=x_s[:, 768:], in_=grouped[:, 768 * J :]
-        )
+        gather(1, 0, S)
+        quantize(w1_c, w1_s, w1_lo, 0, 2 * P)
+        x_c = keep.tile([P, S], U32, name="x_c", tag="first", align_bytes=64)
+        for s0 in range(0, S, 256):
+            quantize(x_c, x_s, grouped, s0, 256)
+        quantize(w1_c, w1_s, w1_hi, 2 * P, 2 * P, 0)
 
-        banks = [psum.tile([P, 512], F32, name=f"bank{i}") for i in range(8)]
+        banks = [psum.tile([P, BANK], F32, name=f"bank{i}") for i in range(8)]
+
+        def mx(acc, w_c, w_s, c0, codes, scales):
+            nc.tensor.matmul_mx(
+                out=acc,
+                lhsT=w_c[:, c0 : c0 + P].bitcast(FP8X4),
+                lhsT_scale=w_s[:, c0 : c0 + P],
+                rhs=codes.bitcast(FP8X4),
+                rhs_scale=scales,
+                start=True,
+                stop=True,
+            )
+
+        layer1_banks = ((0, 1, 2, 3), (4, 5), (6, 7), (0, 1))
 
         def layer1(t):
-            for s0, n in ((0, 512), (512, 256), (768, 256)):
-                codes = x_c[:, s0 : s0 + n] if s0 < 768 else x_c2[:]
-                nc.tensor.matmul_mx(
-                    out=banks[2 * t + s0 // 512][:, s0 % 512 : s0 % 512 + n],
-                    lhsT=w1_c[:, P * t : P * t + P].bitcast(FP8X4),
-                    lhsT_scale=w1_s[:, P * t : P * t + P],
-                    rhs=codes.bitcast(FP8X4),
-                    rhs_scale=x_s[:, s0 : s0 + n],
-                    start=True,
-                    stop=True,
-                )
-            for half in range(2):
-                nc.scalar.activation(h[t][:, half * 512 : half * 512 + 512], banks[2 * t + half][:], SILU)
+            n = S // len(layer1_banks[t])
+            for i, b in enumerate(layer1_banks[t]):
+                s0 = i * n
+                mx(banks[b][:, :n], w1_c, w1_s, P * t, x_c[:, s0 : s0 + n], x_s[:, s0 : s0 + n])
+                nc.scalar.activation(h[t][:, s0 : s0 + n], banks[b][:, :n], SILU)
 
-        layer1(0)
-        quantize(w1_c, w1_s, w1_e1, P, P, 0)
-        late = keep.tile([P, 2 * P * J + N * J], BF16, name="late", tag="stage", align_bytes=64)
-        w1_late = late[:, : 2 * P * J]
-        w2_late = late[:, 2 * P * J :]
-        nc.vector.tensor_copy(out=w1_late.rearrange("p (t m j) -> p m t j", t=2, j=J), in_=w1_src[:, :, 2:])
-        quantize(w1_c, w1_s, w1_late, 2 * P, 2 * P, 0)
-        nc.vector.tensor_copy(out=w2_late.rearrange("p (n j) -> p n j", j=J), in_=w2_raw[:].rearrange("p j n -> p n j"))
-        for t in range(1, J):
+        for t in range(J):
             layer1(t)
+        interleave(w2_b[:], w2_raw[:])
+        quantize(w2_c, w2_s, w2_b, 0, N)
+
         for t in range(J):
             for d, pos in enumerate((pos1_sb, pos2_sb)):
                 nc.vector.tensor_tensor(m[d][:, t, :], h[t][:].indirect(pos[:]), gate_sb[:, d, :], MULT)
 
+        sum_banks = (banks[2], banks[3])
+        for t in range(2):
+            for b in range(V // P):
+                for d in range(D):
+                    c = 2 * t + b % 2
+                    nc.tensor.matmul(
+                        sum_banks[b // 2][:, c * P : (c + 1) * P],
+                        lhsT=m[d][:, t, b * P : (b + 1) * P],
+                        rhs=ident[:],
+                        start=(d == 0),
+                        stop=(d == D - 1),
+                        is_transpose=True,
+                    )
+        back = banks[4]
+        words = zt[:].bitcast(F32)
+        for i in range(2):
+            nc.scalar.copy(
+                zt[:, i * V : (i + 1) * V].rearrange("v (b p e) -> v b p e", b=2, e=2),
+                sum_banks[i][:].rearrange("v (e b p) -> v b p e", e=2, b=2),
+            )
+            for b in (2 * i, 2 * i + 1):
+                nc.tensor.transpose(back[:, b * P : (b + 1) * P], words[:, b * P : (b + 1) * P], ident[:])
+        nc.scalar.copy(z_b[:].bitcast(F32).rearrange("p (v u) -> p v u", u=2)[:, :, 0], back[:])
+
         def add(v0, n):
-            pat = "p t (c i) -> p c t i"
+            pat = "p e (c i) -> p c e i"
             nc.vector.tensor_tensor(
-                z_b[:, J * v0 : J * (v0 + n)].rearrange("p (c i t) -> p c t i", t=J, i=4),
-                m[0][:, :, v0 : v0 + n].rearrange(pat, i=4),
-                m[1][:, :, v0 : v0 + n].rearrange(pat, i=4),
+                z_b[:, J * v0 : J * (v0 + n)].rearrange("p (c i t) -> p c t i", t=J, i=4)[:, :, 2:],
+                m[0][:, 2:, v0 : v0 + n].rearrange(pat, i=4),
+                m[1][:, 2:, v0 : v0 + n].rearrange(pat, i=4),
                 ADD,
             )
 
         half_v = V // 2
-        quantize(w2_c, w2_s, w2_late, 0, N)
         add(0, half_v)
         add(half_v, half_v)
         for i in range(2):
             quantize(z_c, z_s, z_b, i * half_v, half_v)
         for i in range(2):
             sl = slice(i * half_v, (i + 1) * half_v)
-            acc = banks[i]
-            nc.tensor.matmul_mx(
-                out=acc[:, :half_v],
-                lhsT=w2_c[:].bitcast(FP8X4),
-                lhsT_scale=w2_s[:],
-                rhs=z_c[:, sl].bitcast(FP8X4),
-                rhs_scale=z_s[:, sl],
-                start=True,
-                stop=True,
-            )
-            nc.scalar.copy(o_sb[:, sl], acc[:, :half_v])
+            acc = banks[5 + i][:, :half_v]
+            mx(acc, w2_c, w2_s, 0, z_c[:, sl], z_s[:, sl])
+            nc.scalar.copy(o_sb[:, sl], acc)
             nc.sync.dma_start(out=out[:, sl], in_=o_sb[:, sl])

@@ -20,6 +20,7 @@ MULT = mybir.AluOpType.mult
 P = 128
 J = 4
 BANK = 512
+HALF = V // 2
 
 
 def tile_picked_sage_silu_e_kernel(tc, xT, w1, w2, gate, offs, pos1, pos2, out):
@@ -31,24 +32,24 @@ def tile_picked_sage_silu_e_kernel(tc, xT, w1, w2, gate, offs, pos1, pos2, out):
         offs_sb = keep.tile([P, S // 16], U16, name="offs_sb")
         pos1_sb = keep.tile([P, V // 16], U16, name="pos1_sb")
         pos2_sb = keep.tile([P, V // 16], U16, name="pos2_sb")
-        gate_sb = keep.tile([P, D, V], F32, name="gate_sb")
+        gate_sb = keep.tile([P, D, V + HALF], F32, name="gate_sb", align_bytes=64)
         w1_raw = [keep.tile([P, J, H // 2], F32, name=f"w1_raw{i}") for i in range(2)]
         w2_raw = keep.tile([P, J, N], F32, name="w2_raw")
         w1_lo = keep.tile([P, 2 * P * J], BF16, name="w1_lo", tag="first", align_bytes=64)
         w1_hi = keep.tile([P, 2 * P * J], BF16, name="w1_hi", align_bytes=64)
-        w2_b = keep.tile([P, N * J], BF16, name="w2_b", align_bytes=64)
         w1_c = keep.tile([P, H], U32, name="w1_c", align_bytes=64)
         w1_s = keep.tile([P, H], U8, name="w1_s", align_bytes=64)
         w2_c = keep.tile([P, N], U32, name="w2_c", align_bytes=64)
         w2_s = keep.tile([P, N], U8, name="w2_s", align_bytes=64)
         xb = [keep.tile([P, T * 2], BF16, name=f"xb{u}", align_bytes=64) for u in range(2)]
-        grouped = keep.tile([P, S * J], BF16, name="grouped", align_bytes=64)
+        grouped = keep.tile([P, S * J], BF16, name="grouped", tag="stage", align_bytes=64)
         x_s = keep.tile([P, S], U8, name="x_s", align_bytes=64)
         h = [keep.tile([P, S], F32, name=f"h{t}", align_bytes=64) for t in range(J)]
         m = [keep.tile([P, J, V], F32, name=f"m{d}", align_bytes=64) for d in range(D)]
-        z_b = keep.tile([P, V * J], BF16, name="z_b", align_bytes=64)
-        zt = keep.tile([P, V * 2], BF16, name="zt", align_bytes=64)
-        z_c = keep.tile([P, V], U32, name="z_c", align_bytes=64)
+        z_a = keep.tile([P, HALF * J], BF16, name="z_a", tag="za", align_bytes=64)
+        z_b = keep.tile([P, HALF * J], BF16, name="z_b", align_bytes=64)
+        zt = [keep.tile([P, V], BF16, name=f"zt{i}", align_bytes=64) for i in range(3)]
+        za_c = keep.tile([P, HALF], U32, name="za_c", align_bytes=64)
         z_s = keep.tile([P, V], U8, name="z_s", align_bytes=64)
         o_sb = keep.tile([P, V], F32, name="o_sb", align_bytes=64)
         ident = keep.tile([P, P], F32, name="ident", align_bytes=64)
@@ -70,10 +71,10 @@ def tile_picked_sage_silu_e_kernel(tc, xT, w1, w2, gate, offs, pos1, pos2, out):
         w1_view = w1.rearrange("(p j) c -> p j c", j=J)
         for i in range(2):
             nc.sync.dma_start(out=w1_raw[i][:], in_=w1_view[:, :, i * H // 2 : (i + 1) * H // 2])
-        nc.sync.dma_start(out=pos1_sb[:], in_=pos1)
-        nc.sync.dma_start(out=gate_sb[:], in_=gate.rearrange("d p v -> p d v"))
-        nc.sync.dma_start(out=pos2_sb[:], in_=pos2)
         nc.sync.dma_start(out=w2_raw[:], in_=w2.rearrange("(p j) n -> p j n", j=J))
+        nc.sync.dma_start(out=pos1_sb[:], in_=pos1)
+        nc.sync.dma_start(out=gate_sb[:, :, :V], in_=gate.rearrange("d p v -> p d v"))
+        nc.sync.dma_start(out=pos2_sb[:], in_=pos2)
 
         g_words = grouped[:].bitcast(U32).rearrange("p (s u) -> p s u", u=2)
 
@@ -105,9 +106,6 @@ def tile_picked_sage_silu_e_kernel(tc, xT, w1, w2, gate, offs, pos1, pos2, out):
             round_cols(i, 0, n_vector, True)
             round_cols(i, n_vector, n - n_vector, False)
 
-        def interleave(dst, raw):
-            nc.scalar.activation(dst.rearrange("p (c j) -> p c j", j=J), raw.rearrange("p j c -> p c j"), COPY)
-
         split(0, 512)
         split(1, 672)
         gather(0, 0, S)
@@ -124,9 +122,13 @@ def tile_picked_sage_silu_e_kernel(tc, xT, w1, w2, gate, offs, pos1, pos2, out):
         gather(1, 0, S)
         quantize(w1_c, w1_s, w1_lo, 0, 2 * P)
         x_c = keep.tile([P, S], U32, name="x_c", tag="first", align_bytes=64)
-        for s0 in range(0, S, 256):
-            quantize(x_c, x_s, grouped, s0, 256)
+        node_slices = ((0, 256), (256, 256), (512, 256), (768, 128), (896, 128))
+        for s0, n in node_slices:
+            quantize(x_c, x_s, grouped, s0, n)
+        w2_b = keep.tile([P, N * J], BF16, name="w2_b", tag="stage", align_bytes=64)
+        nc.vector.tensor_copy(out=w2_b[:].rearrange("p (n j) -> p n j", j=J), in_=w2_raw[:].rearrange("p j n -> p n j"))
         quantize(w1_c, w1_s, w1_hi, 2 * P, 2 * P, 0)
+        quantize(w2_c, w2_s, w2_b, 0, N)
 
         banks = [psum.tile([P, BANK], F32, name=f"bank{i}") for i in range(8)]
 
@@ -141,65 +143,85 @@ def tile_picked_sage_silu_e_kernel(tc, xT, w1, w2, gate, offs, pos1, pos2, out):
                 stop=True,
             )
 
-        layer1_banks = ((0, 1, 2, 3), (4, 5), (6, 7), (0, 1))
-
-        def layer1(t):
-            n = S // len(layer1_banks[t])
-            for i, b in enumerate(layer1_banks[t]):
-                s0 = i * n
+        layer1_banks = ((0, 1, 2, 3, 4), (3, 4), (5, 6), (7, 0))
+        for t in range(J):
+            pieces = node_slices if t == 0 else ((0, BANK), (BANK, BANK))
+            for (s0, n), b in zip(pieces, layer1_banks[t]):
                 mx(banks[b][:, :n], w1_c, w1_s, P * t, x_c[:, s0 : s0 + n], x_s[:, s0 : s0 + n])
                 nc.scalar.activation(h[t][:, s0 : s0 + n], banks[b][:, :n], SILU)
 
-        for t in range(J):
-            layer1(t)
-        interleave(w2_b[:], w2_raw[:])
-        quantize(w2_c, w2_s, w2_b, 0, N)
-
-        for t in range(J):
+        def fetch(t, v0, n, dst):
             for d, pos in enumerate((pos1_sb, pos2_sb)):
-                nc.vector.tensor_tensor(m[d][:, t, :], h[t][:].indirect(pos[:]), gate_sb[:, d, :], MULT)
+                nc.vector.tensor_tensor(
+                    dst(d), h[t][:].indirect(pos[:, v0 // 16 : (v0 + n) // 16]), gate_sb[:, d, v0 : v0 + n], MULT
+                )
 
-        sum_banks = (banks[2], banks[3])
         for t in range(2):
-            for b in range(V // P):
+            fetch(t, 0, V, lambda d: m[d][:, t, :])
+        for t in (2, 3):
+            fetch(t, 0, HALF, lambda d: m[d][:, t, :HALF])
+        fetch(2, HALF, HALF, lambda d: gate_sb[:, d, :HALF])
+        fetch(3, HALF, HALF, lambda d: gate_sb[:, d, V:])
+
+        def add_turned(t, bank, b0):
+            for b in range(2):
                 for d in range(D):
-                    c = 2 * t + b % 2
+                    c = 2 * (t % 2) + b
                     nc.tensor.matmul(
-                        sum_banks[b // 2][:, c * P : (c + 1) * P],
-                        lhsT=m[d][:, t, b * P : (b + 1) * P],
+                        bank[:, c * P : (c + 1) * P],
+                        lhsT=m[d][:, t, (b0 + b) * P : (b0 + b + 1) * P],
                         rhs=ident[:],
                         start=(d == 0),
                         stop=(d == D - 1),
                         is_transpose=True,
                     )
-        back = banks[4]
-        words = zt[:].bitcast(F32)
-        for i in range(2):
-            nc.scalar.copy(
-                zt[:, i * V : (i + 1) * V].rearrange("v (b p e) -> v b p e", b=2, e=2),
-                sum_banks[i][:].rearrange("v (e b p) -> v b p e", e=2, b=2),
-            )
-            for b in (2 * i, 2 * i + 1):
-                nc.tensor.transpose(back[:, b * P : (b + 1) * P], words[:, b * P : (b + 1) * P], ident[:])
-        nc.scalar.copy(z_b[:].bitcast(F32).rearrange("p (v u) -> p v u", u=2)[:, :, 0], back[:])
 
-        def add(v0, n):
+        def turn_back(pairs, bank, back):
+            nc.scalar.copy(
+                pairs[:].rearrange("v (b p e) -> v b p e", b=2, e=2),
+                bank[:].rearrange("v (e b p) -> v b p e", e=2, b=2),
+            )
+            words = pairs[:].bitcast(F32)
+            for b in range(2):
+                nc.tensor.transpose(back[:, b * P : (b + 1) * P], words[:, b * P : (b + 1) * P], ident[:])
+
+        for t in range(2):
+            for i in range(2):
+                add_turned(t, banks[1 + i], 2 * i)
+        for t in (2, 3):
+            add_turned(t, banks[3], 0)
+        turn_back(zt[0], banks[1], banks[4][:, :HALF])
+        turn_back(zt[1], banks[2], banks[5][:, :HALF])
+        turn_back(zt[2], banks[3], banks[4][:, HALF:])
+        nc.scalar.copy(
+            z_a[:].bitcast(F32).rearrange("p (v u) -> p v u", u=2), banks[4][:].rearrange("p (u v) -> p v u", u=2)
+        )
+        nc.scalar.copy(z_b[:].bitcast(F32).rearrange("p (v u) -> p v u", u=2)[:, :, 0], banks[5][:, :HALF])
+
+        late = [gate_sb[:, d, :].rearrange("p (e v) -> p e v", v=HALF)[:, ::2] for d in range(D)]
+        for v0 in (0, P):
             pat = "p e (c i) -> p c e i"
             nc.vector.tensor_tensor(
-                z_b[:, J * v0 : J * (v0 + n)].rearrange("p (c i t) -> p c t i", t=J, i=4)[:, :, 2:],
-                m[0][:, 2:, v0 : v0 + n].rearrange(pat, i=4),
-                m[1][:, 2:, v0 : v0 + n].rearrange(pat, i=4),
+                z_b[:, J * v0 : J * (v0 + P)].rearrange("p (c i t) -> p c t i", t=J, i=4)[:, :, 2:],
+                late[0][:, :, v0 : v0 + P].rearrange(pat, i=4),
+                late[1][:, :, v0 : v0 + P].rearrange(pat, i=4),
                 ADD,
             )
-
-        half_v = V // 2
-        add(0, half_v)
-        add(half_v, half_v)
-        for i in range(2):
-            quantize(z_c, z_s, z_b, i * half_v, half_v)
-        for i in range(2):
-            sl = slice(i * half_v, (i + 1) * half_v)
-            acc = banks[5 + i][:, :half_v]
-            mx(acc, w2_c, w2_s, 0, z_c[:, sl], z_s[:, sl])
-            nc.scalar.copy(o_sb[:, sl], acc)
+        quantize(za_c, z_s, z_a, 0, HALF)
+        zb_c = keep.tile([P, HALF], U32, name="zb_c", tag="za", align_bytes=64)
+        for v0 in (0, P):
+            nc.vector.quantize_mx(
+                out=zb_c[:, v0 : v0 + P].bitcast(FP8X4),
+                scales=z_s[:, HALF + v0 : HALF + v0 + P],
+                in_=z_b[:, J * v0 : J * (v0 + P)],
+            )
+        pieces = ((0, HALF, za_c[:]), (HALF, P, zb_c[:, :P]), (HALF + P, P, zb_c[:, P:]))
+        for i, (v0, n, codes) in enumerate(pieces):
+            sl = slice(v0, v0 + n)
+            acc = banks[(6 + i) % 8][:, :n]
+            mx(acc, w2_c, w2_s, 0, codes, z_s[:, sl])
+            if i < 2:
+                nc.scalar.copy(o_sb[:, sl], acc)
+            else:
+                nc.vector.tensor_copy(out=o_sb[:, sl], in_=acc)
             nc.sync.dma_start(out=out[:, sl], in_=o_sb[:, sl])

@@ -35,16 +35,15 @@ def tile_picked_sage_silu_e_kernel(tc, xT, w1, w2, gate, offs, pos1, pos2, out):
         gate_sb = keep.tile([P, D, V + HALF], F32, name="gate_sb", align_bytes=64)
         w1_raw = [keep.tile([P, J, H // 2], F32, name=f"w1_raw{i}") for i in range(2)]
         w2_raw = keep.tile([P, J, N], F32, name="w2_raw")
-        w1_lo = keep.tile([P, 2 * P * J], BF16, name="w1_lo", tag="first", align_bytes=64)
+        w1_lo = [keep.tile([P, P * J], BF16, name=f"w1_lo{i}", tag=f"lo{i}", align_bytes=64) for i in range(2)]
         w1_hi = keep.tile([P, 2 * P * J], BF16, name="w1_hi", align_bytes=64)
         w1_c = keep.tile([P, H], U32, name="w1_c", align_bytes=64)
         w1_s = keep.tile([P, H], U8, name="w1_s", align_bytes=64)
-        w2_c = keep.tile([P, N], U32, name="w2_c", align_bytes=64)
         w2_s = keep.tile([P, N], U8, name="w2_s", align_bytes=64)
         xb = [keep.tile([P, T * 2], BF16, name=f"xb{u}", align_bytes=64) for u in range(2)]
-        grouped = keep.tile([P, S * J], BF16, name="grouped", tag="stage", align_bytes=64)
+        grouped = keep.tile([P, S * J], BF16, name="grouped", align_bytes=64)
         x_s = keep.tile([P, S], U8, name="x_s", align_bytes=64)
-        h = [keep.tile([P, S], F32, name=f"h{t}", align_bytes=64) for t in range(J)]
+        h = [keep.tile([P, S], F32, name=f"h{t}", tag=f"h{t}", align_bytes=64) for t in range(J)]
         m = [keep.tile([P, J, V], F32, name=f"m{d}", align_bytes=64) for d in range(D)]
         z_a = keep.tile([P, HALF * J], BF16, name="z_a", tag="za", align_bytes=64)
         z_b = keep.tile([P, HALF * J], BF16, name="z_b", align_bytes=64)
@@ -60,7 +59,7 @@ def tile_picked_sage_silu_e_kernel(tc, xT, w1, w2, gate, offs, pos1, pos2, out):
         make_identity(nc, ident[:])
 
         x_view = xT.rearrange("(p u e) t -> p u e t", u=2, e=2)
-        chunks = [(0, 0, 1024), (0, 1024, 1024), (1, 0, 1024), (1, 1024, 512), (1, 1536, 512)]
+        chunks = [(u, c0, n) for u in range(2) for c0, n in ((0, 1024), (1024, 768), (1792, 256))]
         raws = []
         for i, (u, c0, n) in enumerate(chunks):
             raw = keep.tile([P, 2, n], F32, name=f"x_raw{i}", align_bytes=64)
@@ -71,10 +70,10 @@ def tile_picked_sage_silu_e_kernel(tc, xT, w1, w2, gate, offs, pos1, pos2, out):
         w1_view = w1.rearrange("(p j) c -> p j c", j=J)
         for i in range(2):
             nc.sync.dma_start(out=w1_raw[i][:], in_=w1_view[:, :, i * H // 2 : (i + 1) * H // 2])
-        nc.sync.dma_start(out=w2_raw[:], in_=w2.rearrange("(p j) n -> p j n", j=J))
         nc.sync.dma_start(out=pos1_sb[:], in_=pos1)
         nc.sync.dma_start(out=gate_sb[:, :, :V], in_=gate.rearrange("d p v -> p d v"))
         nc.sync.dma_start(out=pos2_sb[:], in_=pos2)
+        nc.sync.dma_start(out=w2_raw[:], in_=w2.rearrange("(p j) n -> p j n", j=J))
 
         g_words = grouped[:].bitcast(U32).rearrange("p (s u) -> p s u", u=2)
 
@@ -107,28 +106,28 @@ def tile_picked_sage_silu_e_kernel(tc, xT, w1, w2, gate, offs, pos1, pos2, out):
             round_cols(i, n_vector, n - n_vector, False)
 
         split(0, 512)
-        split(1, 672)
+        split(1, 512)
+        split(2, 176)
         gather(0, 0, S)
-        split(2, 384)
         split(3, 320)
-        split(4, 320)
+        split(4, 512)
+        split(5, 176)
         for i in range(2):
-            for u, dst in enumerate((w1_lo, w1_hi)):
-                nc.scalar.activation(
-                    dst[:].rearrange("p (e c j) -> p c e j", e=2, j=J)[:, i * P // 2 : (i + 1) * P // 2],
-                    w1_raw[i][:].rearrange("p j (c t) -> p c t j", t=J)[:, :, 2 * u : 2 * u + 2],
-                    COPY,
-                )
+            src = w1_raw[i][:].rearrange("p j (c t) -> p c t j", t=J)
+            nc.scalar.activation(w1_lo[i][:].rearrange("p (c e j) -> p c e j", e=2, j=J), src[:, :, :2], COPY)
+            nc.scalar.activation(
+                w1_hi[:].rearrange("p (e c j) -> p c e j", e=2, j=J)[:, i * P // 2 : (i + 1) * P // 2],
+                src[:, :, 2:],
+                COPY,
+            )
         gather(1, 0, S)
-        quantize(w1_c, w1_s, w1_lo, 0, 2 * P)
-        x_c = keep.tile([P, S], U32, name="x_c", tag="first", align_bytes=64)
-        node_slices = ((0, 256), (256, 256), (512, 256), (768, 128), (896, 128))
+        quantize(w1_c, w1_s, w1_lo[0], 0, P)
+        x_c = keep.tile([P, S], U32, name="x_c", tag="lo0", align_bytes=64)
+        node_slices = ((0, 128), (128, 256), (384, 256), (640, 256), (896, 128))
         for s0, n in node_slices:
             quantize(x_c, x_s, grouped, s0, n)
-        w2_b = keep.tile([P, N * J], BF16, name="w2_b", tag="stage", align_bytes=64)
-        nc.vector.tensor_copy(out=w2_b[:].rearrange("p (n j) -> p n j", j=J), in_=w2_raw[:].rearrange("p j n -> p n j"))
+        quantize(w1_c, w1_s, w1_lo[1], P, P, 0)
         quantize(w1_c, w1_s, w1_hi, 2 * P, 2 * P, 0)
-        quantize(w2_c, w2_s, w2_b, 0, N)
 
         banks = [psum.tile([P, BANK], F32, name=f"bank{i}") for i in range(8)]
 
@@ -150,6 +149,9 @@ def tile_picked_sage_silu_e_kernel(tc, xT, w1, w2, gate, offs, pos1, pos2, out):
                 mx(banks[b][:, :n], w1_c, w1_s, P * t, x_c[:, s0 : s0 + n], x_s[:, s0 : s0 + n])
                 nc.scalar.activation(h[t][:, s0 : s0 + n], banks[b][:, :n], SILU)
 
+        w2_b = keep.tile([P, N * J], BF16, name="w2_b", tag="lo0", align_bytes=64)
+        nc.scalar.activation(w2_b[:].rearrange("p (n j) -> p n j", j=J), w2_raw[:].rearrange("p j n -> p n j"), COPY)
+
         def fetch(t, v0, n, dst):
             for d, pos in enumerate((pos1_sb, pos2_sb)):
                 nc.vector.tensor_tensor(
@@ -166,7 +168,7 @@ def tile_picked_sage_silu_e_kernel(tc, xT, w1, w2, gate, offs, pos1, pos2, out):
         def add_turned(t, bank, b0):
             for b in range(2):
                 for d in range(D):
-                    c = 2 * (t % 2) + b
+                    c = 2 * b + t if t < 2 else 2 * (t % 2) + b
                     nc.tensor.matmul(
                         bank[:, c * P : (c + 1) * P],
                         lhsT=m[d][:, t, (b0 + b) * P : (b0 + b + 1) * P],
@@ -176,11 +178,8 @@ def tile_picked_sage_silu_e_kernel(tc, xT, w1, w2, gate, offs, pos1, pos2, out):
                         is_transpose=True,
                     )
 
-        def turn_back(pairs, bank, back):
-            nc.scalar.copy(
-                pairs[:].rearrange("v (b p e) -> v b p e", b=2, e=2),
-                bank[:].rearrange("v (e b p) -> v b p e", e=2, b=2),
-            )
+        def turn_back(pairs, sums, back):
+            nc.scalar.copy(pairs[:].rearrange("v (b p e) -> v b p e", b=2, e=2), sums)
             words = pairs[:].bitcast(F32)
             for b in range(2):
                 nc.tensor.transpose(back[:, b * P : (b + 1) * P], words[:, b * P : (b + 1) * P], ident[:])
@@ -190,14 +189,16 @@ def tile_picked_sage_silu_e_kernel(tc, xT, w1, w2, gate, offs, pos1, pos2, out):
                 add_turned(t, banks[1 + i], 2 * i)
         for t in (2, 3):
             add_turned(t, banks[3], 0)
-        turn_back(zt[0], banks[1], banks[4][:, :HALF])
-        turn_back(zt[1], banks[2], banks[5][:, :HALF])
-        turn_back(zt[2], banks[3], banks[4][:, HALF:])
+        turn_back(zt[0], banks[1][:].rearrange("v (b p e) -> v b p e", e=2, b=2), banks[4][:, :HALF])
+        turn_back(zt[1], banks[2][:].rearrange("v (b p e) -> v b p e", e=2, b=2), banks[5][:, :HALF])
+        turn_back(zt[2], banks[3][:].rearrange("v (e b p) -> v b p e", e=2, b=2), banks[4][:, HALF:])
         nc.scalar.copy(
             z_a[:].bitcast(F32).rearrange("p (v u) -> p v u", u=2), banks[4][:].rearrange("p (u v) -> p v u", u=2)
         )
         nc.scalar.copy(z_b[:].bitcast(F32).rearrange("p (v u) -> p v u", u=2)[:, :, 0], banks[5][:, :HALF])
 
+        w2_c = keep.tile([P, N], U32, name="w2_c", tag="h3", align_bytes=64)
+        quantize(w2_c, w2_s, w2_b, 0, N)
         late = [gate_sb[:, d, :].rearrange("p (e v) -> p e v", v=HALF)[:, ::2] for d in range(D)]
         for v0 in (0, P):
             pat = "p e (c i) -> p c e i"

@@ -21,6 +21,7 @@ P = 128
 J = 4
 BANK = 512
 HALF = V // 2
+NV = 256
 
 
 def tile_picked_sage_silu_e_kernel(tc, xT, w1, w2, gate, offs, pos1, pos2, out):
@@ -36,12 +37,15 @@ def tile_picked_sage_silu_e_kernel(tc, xT, w1, w2, gate, offs, pos1, pos2, out):
         w1_raw = [keep.tile([P, J, H // 2], F32, name=f"w1_raw{i}") for i in range(2)]
         w2_raw = keep.tile([P, J, N], F32, name="w2_raw")
         w1_lo = [keep.tile([P, P * J], BF16, name=f"w1_lo{i}", tag=f"lo{i}", align_bytes=64) for i in range(2)]
-        w1_hi = keep.tile([P, 2 * P * J], BF16, name="w1_hi", align_bytes=64)
+        w1_c0 = keep.tile([P, P], U32, name="w1_c0", tag="c0", align_bytes=64)
         w1_c = keep.tile([P, H], U32, name="w1_c", align_bytes=64)
         w1_s = keep.tile([P, H], U8, name="w1_s", align_bytes=64)
         w2_s = keep.tile([P, N], U8, name="w2_s", align_bytes=64)
-        xb = [keep.tile([P, T * 2], BF16, name=f"xb{u}", align_bytes=64) for u in range(2)]
-        grouped = keep.tile([P, S * J], BF16, name="grouped", align_bytes=64)
+        pairs01 = keep.tile([P, T * 2], BF16, name="pairs01", align_bytes=64)
+        row_f = {j: keep.tile([P, T], F32, name=f"row_f{j}", align_bytes=64) for j in (2, 3)}
+        row_b = {j: keep.tile([P, T], BF16, name=f"row_b{j}", align_bytes=64) for j in (2, 3)}
+        picked_v = keep.tile([P, NV * J], BF16, name="picked_v", align_bytes=64)
+        picked_s = keep.tile([P, (S - NV) * J], BF16, name="picked_s", align_bytes=64)
         x_s = keep.tile([P, S], U8, name="x_s", align_bytes=64)
         h = [keep.tile([P, S], F32, name=f"h{t}", tag=f"h{t}", align_bytes=64) for t in range(J)]
         m = [keep.tile([P, J, V], F32, name=f"m{d}", align_bytes=64) for d in range(D)]
@@ -58,15 +62,20 @@ def tile_picked_sage_silu_e_kernel(tc, xT, w1, w2, gate, offs, pos1, pos2, out):
         nc.scalar.activation(warm[:], warm[:], SILU)
         make_identity(nc, ident[:])
 
-        x_view = xT.rearrange("(p u e) t -> p u e t", u=2, e=2)
-        chunks = [(u, c0, n) for u in range(2) for c0, n in ((0, 1024), (1024, 768), (1792, 256))]
-        raws = []
-        for i, (u, c0, n) in enumerate(chunks):
-            raw = keep.tile([P, 2, n], F32, name=f"x_raw{i}", align_bytes=64)
-            nc.sync.dma_start(out=raw[:], in_=x_view[:, u, :, c0 : c0 + n])
-            raws.append(raw)
+        x_view = xT.rearrange("(p j) t -> p j t", j=J)
+        row_chunks = {2: ((0, 1024), (1024, 1024)), 3: ((0, 512), (512, 512), (1024, 512), (1536, 512))}
+        chunks = ((0, 1024), (1024, 768), (1792, 256))
+        for i, (c0, n) in enumerate(row_chunks[2]):
+            nc.sync.dma_start(out=row_f[2][:, c0 : c0 + n], in_=x_view[:, 2, c0 : c0 + n])
             if i == 0:
                 nc.sync.dma_start(out=offs_sb[:], in_=offs)
+        raws = []
+        for i, (c0, n) in enumerate(chunks):
+            raw = keep.tile([P, 2, n], F32, name=f"x_raw{i}", align_bytes=64)
+            nc.sync.dma_start(out=raw[:], in_=x_view[:, :2, c0 : c0 + n])
+            raws.append(raw)
+        for c0, n in row_chunks[3]:
+            nc.sync.dma_start(out=row_f[3][:, c0 : c0 + n], in_=x_view[:, 3, c0 : c0 + n])
         w1_view = w1.rearrange("(p j) c -> p j c", j=J)
         for i in range(2):
             nc.sync.dma_start(out=w1_raw[i][:], in_=w1_view[:, :, i * H // 2 : (i + 1) * H // 2])
@@ -75,21 +84,36 @@ def tile_picked_sage_silu_e_kernel(tc, xT, w1, w2, gate, offs, pos1, pos2, out):
         nc.sync.dma_start(out=pos2_sb[:], in_=pos2)
         nc.sync.dma_start(out=w2_raw[:], in_=w2.rearrange("(p j) n -> p j n", j=J))
 
-        g_words = grouped[:].bitcast(U32).rearrange("p (s u) -> p s u", u=2)
+        def entries(s0, n):
+            return offs_sb[:, s0 // 16 : (s0 + n) // 16]
 
-        def round_cols(i, a, n, on_vector):
-            u, c0 = chunks[i][:2]
-            dst = xb[u][:, 2 * (c0 + a) : 2 * (c0 + a + n)].rearrange("p (t e) -> p t e", e=2)
+        def round_pair(i, a, n, on_vector):
+            c0 = chunks[i][0]
+            dst = pairs01[:, 2 * (c0 + a) : 2 * (c0 + a + n)].rearrange("p (t e) -> p t e", e=2)
             src = raws[i][:, :, a : a + n].rearrange("p e t -> p t e")
             if on_vector:
                 nc.vector.tensor_copy(out=dst, in_=src)
             else:
                 nc.scalar.activation(dst, src, COPY)
 
-        def gather(u, s0, n):
+        def split(i, n_vector):
+            round_pair(i, 0, n_vector, True)
+            round_pair(i, n_vector, chunks[i][1] - n_vector, False)
+
+        def gather_pair(picked, s0, n):
+            words = picked[:].bitcast(U32).rearrange("p (s u) -> p s u", u=2)
+            nc.vector.tensor_copy(out=words[:, :, 0], in_=pairs01[:].bitcast(U32).indirect(entries(s0, n)))
+
+        def gather_row_vector(j):
             nc.vector.tensor_copy(
-                out=g_words[:, s0 : s0 + n, u],
-                in_=xb[u][:].bitcast(U32).indirect(offs_sb[:, s0 // 16 : (s0 + n) // 16]),
+                out=picked_v[:].rearrange("p (s j) -> p s j", j=J)[:, :, j], in_=row_f[j][:].indirect(entries(0, NV))
+            )
+
+        def gather_row_scalar(j, s0, n):
+            nc.scalar.activation(
+                picked_s[:].rearrange("p (s j) -> p s j", j=J)[:, s0 - NV : s0 - NV + n, j],
+                row_b[j][:].indirect(entries(s0, n)),
+                COPY,
             )
 
         def quantize(codes, scales, src, c0, n, s0=None):
@@ -100,34 +124,38 @@ def tile_picked_sage_silu_e_kernel(tc, xT, w1, w2, gate, offs, pos1, pos2, out):
                 in_=src[:, J * s0 : J * (s0 + n)],
             )
 
-        def split(i, n_vector):
-            n = chunks[i][2]
-            round_cols(i, 0, n_vector, True)
-            round_cols(i, n_vector, n - n_vector, False)
-
-        split(0, 512)
+        nc.scalar.activation(row_b[2][:, :1024], row_f[2][:, :1024], COPY)
+        nc.vector.tensor_copy(out=row_b[2][:, 1024:], in_=row_f[2][:, 1024:])
+        gather_row_vector(2)
+        gather_row_scalar(2, NV, S - NV)
+        round_pair(0, 0, 1024, True)
         split(1, 512)
         split(2, 176)
-        gather(0, 0, S)
-        split(3, 320)
-        split(4, 512)
-        split(5, 176)
-        for i in range(2):
-            src = w1_raw[i][:].rearrange("p j (c t) -> p c t j", t=J)
-            nc.scalar.activation(w1_lo[i][:].rearrange("p (c e j) -> p c e j", e=2, j=J), src[:, :, :2], COPY)
-            nc.scalar.activation(
-                w1_hi[:].rearrange("p (e c j) -> p c e j", e=2, j=J)[:, i * P // 2 : (i + 1) * P // 2],
-                src[:, :, 2:],
-                COPY,
+        gather_pair(picked_s, NV, S - NV)
+        gather_pair(picked_v, 0, NV)
+        for c0, n in row_chunks[3]:
+            nc.scalar.activation(row_b[3][:, c0 : c0 + n], row_f[3][:, c0 : c0 + n], COPY)
+        gather_row_vector(3)
+        for s0 in range(NV, S, 256):
+            gather_row_scalar(3, s0, 256)
+        w1_src = [w1_raw[i][:].rearrange("p j (c t) -> p c t j", t=J) for i in range(2)]
+
+        def weave_lo(i):
+            nc.vector.tensor_copy(
+                out=w1_lo[i][:].rearrange("p (c e j) -> p c e j", e=2, j=J), in_=w1_src[i][:, :, :2]
             )
-        gather(1, 0, S)
-        quantize(w1_c, w1_s, w1_lo[0], 0, P)
+
+        weave_lo(0)
+        quantize(w1_c0, w1_s, w1_lo[0], 0, P)
         x_c = keep.tile([P, S], U32, name="x_c", tag="lo0", align_bytes=64)
-        node_slices = ((0, 128), (128, 256), (384, 256), (640, 256), (896, 128))
+        node_slices = ((0, 256), (256, 256), (512, 256), (768, 128), (896, 128))
         for s0, n in node_slices:
-            quantize(x_c, x_s, grouped, s0, n)
+            if s0 < NV:
+                quantize(x_c, x_s, picked_v, s0, n)
+            else:
+                quantize(x_c, x_s, picked_s, s0, n, s0 - NV)
+        weave_lo(1)
         quantize(w1_c, w1_s, w1_lo[1], P, P, 0)
-        quantize(w1_c, w1_s, w1_hi, 2 * P, 2 * P, 0)
 
         banks = [psum.tile([P, BANK], F32, name=f"bank{i}") for i in range(8)]
 
@@ -143,11 +171,25 @@ def tile_picked_sage_silu_e_kernel(tc, xT, w1, w2, gate, offs, pos1, pos2, out):
             )
 
         layer1_banks = ((0, 1, 2, 3, 4), (3, 4), (5, 6), (7, 0))
-        for t in range(J):
+
+        def layer1(t):
             pieces = node_slices if t == 0 else ((0, BANK), (BANK, BANK))
             for (s0, n), b in zip(pieces, layer1_banks[t]):
-                mx(banks[b][:, :n], w1_c, w1_s, P * t, x_c[:, s0 : s0 + n], x_s[:, s0 : s0 + n])
+                w_c = w1_c0 if t == 0 else w1_c
+                mx(banks[b][:, :n], w_c, w1_s, P * t, x_c[:, s0 : s0 + n], x_s[:, s0 : s0 + n])
                 nc.scalar.activation(h[t][:, s0 : s0 + n], banks[b][:, :n], SILU)
+
+        layer1(0)
+        w1_hi = keep.tile([P, 2 * P * J], BF16, name="w1_hi", tag="c0", align_bytes=64)
+        for i in range(2):
+            nc.scalar.activation(
+                w1_hi[:].rearrange("p (e c j) -> p c e j", e=2, j=J)[:, i * P // 2 : (i + 1) * P // 2],
+                w1_src[i][:, :, 2:],
+                COPY,
+            )
+        quantize(w1_c, w1_s, w1_hi, 2 * P, 2 * P, 0)
+        for t in range(1, J):
+            layer1(t)
 
         w2_b = keep.tile([P, N * J], BF16, name="w2_b", tag="lo0", align_bytes=64)
         nc.scalar.activation(w2_b[:].rearrange("p (n j) -> p n j", j=J), w2_raw[:].rearrange("p j n -> p n j"), COPY)

@@ -21,7 +21,7 @@ P = 128
 J = 4
 BANK = 512
 HALF = V // 2
-NV = 256
+NV = 320
 
 
 def tile_picked_sage_silu_e_kernel(tc, xT, w1, w2, gate, offs, pos1, pos2, out):
@@ -37,14 +37,12 @@ def tile_picked_sage_silu_e_kernel(tc, xT, w1, w2, gate, offs, pos1, pos2, out):
         w1_raw = [keep.tile([P, J, H // 2], F32, name=f"w1_raw{i}") for i in range(2)]
         w2_raw = keep.tile([P, J, N], F32, name="w2_raw")
         w1_lo = [keep.tile([P, P * J], BF16, name=f"w1_lo{i}", tag=f"lo{i}", align_bytes=64) for i in range(2)]
-        w1_c0 = keep.tile([P, P], U32, name="w1_c0", tag="c0", align_bytes=64)
         w1_c = keep.tile([P, H], U32, name="w1_c", align_bytes=64)
         w1_s = keep.tile([P, H], U8, name="w1_s", align_bytes=64)
         w2_s = keep.tile([P, N], U8, name="w2_s", align_bytes=64)
-        pairs01 = keep.tile([P, T * 2], BF16, name="pairs01", align_bytes=64)
-        row_f = {j: keep.tile([P, T], F32, name=f"row_f{j}", align_bytes=64) for j in (2, 3)}
-        row_b = {j: keep.tile([P, T], BF16, name=f"row_b{j}", align_bytes=64) for j in (2, 3)}
-        picked_v = keep.tile([P, NV * J], BF16, name="picked_v", align_bytes=64)
+        row_f = {j: keep.tile([P, T], F32, name=f"row_f{j}", align_bytes=64) for j in range(J)}
+        row_b = {j: keep.tile([P, T], BF16, name=f"row_b{j}", align_bytes=64) for j in range(J)}
+        picked_v = keep.tile([P, NV * J], BF16, name="picked_v", tag="pv", align_bytes=64)
         picked_s = keep.tile([P, (S - NV) * J], BF16, name="picked_s", align_bytes=64)
         x_s = keep.tile([P, S], U8, name="x_s", align_bytes=64)
         h = [keep.tile([P, S], F32, name=f"h{t}", tag=f"h{t}", align_bytes=64) for t in range(J)]
@@ -63,19 +61,14 @@ def tile_picked_sage_silu_e_kernel(tc, xT, w1, w2, gate, offs, pos1, pos2, out):
         make_identity(nc, ident[:])
 
         x_view = xT.rearrange("(p j) t -> p j t", j=J)
-        row_chunks = {2: ((0, 1024), (1024, 1024)), 3: ((0, 512), (512, 512), (1024, 512), (1536, 512))}
-        chunks = ((0, 1024), (1024, 768), (1792, 256))
-        for i, (c0, n) in enumerate(row_chunks[2]):
-            nc.sync.dma_start(out=row_f[2][:, c0 : c0 + n], in_=x_view[:, 2, c0 : c0 + n])
-            if i == 0:
-                nc.sync.dma_start(out=offs_sb[:], in_=offs)
-        raws = []
-        for i, (c0, n) in enumerate(chunks):
-            raw = keep.tile([P, 2, n], F32, name=f"x_raw{i}", align_bytes=64)
-            nc.sync.dma_start(out=raw[:], in_=x_view[:, :2, c0 : c0 + n])
-            raws.append(raw)
-        for c0, n in row_chunks[3]:
-            nc.sync.dma_start(out=row_f[3][:, c0 : c0 + n], in_=x_view[:, 3, c0 : c0 + n])
+        halves = ((0, 1024), (1024, 1024))
+        tapered = ((0, 1024), (1024, 768), (1792, 256))
+        row_chunks = (tapered, halves, halves, tapered)
+        for j in range(J):
+            for c0, n in row_chunks[j]:
+                nc.sync.dma_start(out=row_f[j][:, c0 : c0 + n], in_=x_view[:, j, c0 : c0 + n])
+                if j == 0 and c0 == 0:
+                    nc.sync.dma_start(out=offs_sb[:], in_=offs)
         w1_view = w1.rearrange("(p j) c -> p j c", j=J)
         for i in range(2):
             nc.sync.dma_start(out=w1_raw[i][:], in_=w1_view[:, :, i * H // 2 : (i + 1) * H // 2])
@@ -86,23 +79,6 @@ def tile_picked_sage_silu_e_kernel(tc, xT, w1, w2, gate, offs, pos1, pos2, out):
 
         def entries(s0, n):
             return offs_sb[:, s0 // 16 : (s0 + n) // 16]
-
-        def round_pair(i, a, n, on_vector):
-            c0 = chunks[i][0]
-            dst = pairs01[:, 2 * (c0 + a) : 2 * (c0 + a + n)].rearrange("p (t e) -> p t e", e=2)
-            src = raws[i][:, :, a : a + n].rearrange("p e t -> p t e")
-            if on_vector:
-                nc.vector.tensor_copy(out=dst, in_=src)
-            else:
-                nc.scalar.activation(dst, src, COPY)
-
-        def split(i, n_vector):
-            round_pair(i, 0, n_vector, True)
-            round_pair(i, n_vector, chunks[i][1] - n_vector, False)
-
-        def gather_pair(picked, s0, n):
-            words = picked[:].bitcast(U32).rearrange("p (s u) -> p s u", u=2)
-            nc.vector.tensor_copy(out=words[:, :, 0], in_=pairs01[:].bitcast(U32).indirect(entries(s0, n)))
 
         def gather_row_vector(j):
             nc.vector.tensor_copy(
@@ -124,20 +100,15 @@ def tile_picked_sage_silu_e_kernel(tc, xT, w1, w2, gate, offs, pos1, pos2, out):
                 in_=src[:, J * s0 : J * (s0 + n)],
             )
 
-        nc.scalar.activation(row_b[2][:, :1024], row_f[2][:, :1024], COPY)
-        nc.vector.tensor_copy(out=row_b[2][:, 1024:], in_=row_f[2][:, 1024:])
-        gather_row_vector(2)
-        gather_row_scalar(2, NV, S - NV)
-        round_pair(0, 0, 1024, True)
-        split(1, 512)
-        split(2, 176)
-        gather_pair(picked_s, NV, S - NV)
-        gather_pair(picked_v, 0, NV)
-        for c0, n in row_chunks[3]:
-            nc.scalar.activation(row_b[3][:, c0 : c0 + n], row_f[3][:, c0 : c0 + n], COPY)
-        gather_row_vector(3)
-        for s0 in range(NV, S, 256):
-            gather_row_scalar(3, s0, 256)
+        for j in range(J):
+            for c0, n in row_chunks[j]:
+                if j == 0 and n != 768:
+                    nc.scalar.activation(row_b[j][:, c0 : c0 + n], row_f[j][:, c0 : c0 + n], COPY)
+                else:
+                    nc.vector.tensor_copy(out=row_b[j][:, c0 : c0 + n], in_=row_f[j][:, c0 : c0 + n])
+            gather_row_vector(j)
+            for s0, n in ((NV, S - NV),) if j < J - 1 else ((NV, 768 - NV), (768, 256)):
+                gather_row_scalar(j, s0, n)
         w1_src = [w1_raw[i][:].rearrange("p j (c t) -> p c t j", t=J) for i in range(2)]
 
         def weave_lo(i):
@@ -146,16 +117,28 @@ def tile_picked_sage_silu_e_kernel(tc, xT, w1, w2, gate, offs, pos1, pos2, out):
             )
 
         weave_lo(0)
-        quantize(w1_c0, w1_s, w1_lo[0], 0, P)
+        quantize(w1_c, w1_s, w1_lo[0], 0, P)
         x_c = keep.tile([P, S], U32, name="x_c", tag="lo0", align_bytes=64)
-        node_slices = ((0, 256), (256, 256), (512, 256), (768, 128), (896, 128))
-        for s0, n in node_slices:
-            if s0 < NV:
-                quantize(x_c, x_s, picked_v, s0, n)
-            else:
-                quantize(x_c, x_s, picked_s, s0, n, s0 - NV)
+        node_pieces = (((0, 256), (256, 64)), ((320, 256),), ((576, 128), (704, 64)), ((768, 128),), ((896, 128),))
+        for piece in node_pieces:
+            for s0, n in piece:
+                if s0 < NV:
+                    quantize(x_c, x_s, picked_v, s0, n)
+                else:
+                    quantize(x_c, x_s, picked_s, s0, n, s0 - NV)
+        w1_hi = keep.tile([P, 2 * P * J], BF16, name="w1_hi", tag="pv", align_bytes=64)
+
+        def weave_hi(i):
+            nc.vector.tensor_copy(
+                out=w1_hi[:].rearrange("p (e c j) -> p c e j", e=2, j=J)[:, i * P // 2 : (i + 1) * P // 2],
+                in_=w1_src[i][:, :, 2:],
+            )
+
         weave_lo(1)
+        weave_hi(0)
         quantize(w1_c, w1_s, w1_lo[1], P, P, 0)
+        weave_hi(1)
+        quantize(w1_c, w1_s, w1_hi, 2 * P, 2 * P, 0)
 
         banks = [psum.tile([P, BANK], F32, name=f"bank{i}") for i in range(8)]
 
@@ -172,24 +155,14 @@ def tile_picked_sage_silu_e_kernel(tc, xT, w1, w2, gate, offs, pos1, pos2, out):
 
         layer1_banks = ((0, 1, 2, 3, 4), (3, 4), (5, 6), (7, 0))
 
-        def layer1(t):
-            pieces = node_slices if t == 0 else ((0, BANK), (BANK, BANK))
-            for (s0, n), b in zip(pieces, layer1_banks[t]):
-                w_c = w1_c0 if t == 0 else w1_c
-                mx(banks[b][:, :n], w_c, w1_s, P * t, x_c[:, s0 : s0 + n], x_s[:, s0 : s0 + n])
-                nc.scalar.activation(h[t][:, s0 : s0 + n], banks[b][:, :n], SILU)
-
-        layer1(0)
-        w1_hi = keep.tile([P, 2 * P * J], BF16, name="w1_hi", tag="c0", align_bytes=64)
-        for i in range(2):
-            nc.scalar.activation(
-                w1_hi[:].rearrange("p (e c j) -> p c e j", e=2, j=J)[:, i * P // 2 : (i + 1) * P // 2],
-                w1_src[i][:, :, 2:],
-                COPY,
-            )
-        quantize(w1_c, w1_s, w1_hi, 2 * P, 2 * P, 0)
-        for t in range(1, J):
-            layer1(t)
+        for t in range(J):
+            pieces = node_pieces if t == 0 else (((0, BANK),), ((BANK, BANK),))
+            for piece, b in zip(pieces, layer1_banks[t]):
+                first, end = piece[0][0], sum(piece[-1])
+                for s0, n in piece:
+                    acc = banks[b][:, s0 - first : s0 - first + n]
+                    mx(acc, w1_c, w1_s, P * t, x_c[:, s0 : s0 + n], x_s[:, s0 : s0 + n])
+                nc.scalar.activation(h[t][:, first:end], banks[b][:, : end - first], SILU)
 
         w2_b = keep.tile([P, N * J], BF16, name="w2_b", tag="lo0", align_bytes=64)
         nc.scalar.activation(w2_b[:].rearrange("p (n j) -> p n j", j=J), w2_raw[:].rearrange("p j n -> p n j"), COPY)

@@ -61,9 +61,9 @@ def tile_picked_sage_silu_e_kernel(tc, xT, w1, w2, gate, offs, pos1, pos2, out):
         make_identity(nc, ident[:])
 
         x_view = xT.rearrange("(p j) t -> p j t", j=J)
-        halves = ((0, 1024), (1024, 1024))
+        two = ((0, 1280), (1280, 768))
         tapered = ((0, 1024), (1024, 768), (1792, 256))
-        row_chunks = (tapered, halves, halves, tapered)
+        row_chunks = (tapered, two, two, two)
         for j in range(J):
             for c0, n in row_chunks[j]:
                 nc.sync.dma_start(out=row_f[j][:, c0 : c0 + n], in_=x_view[:, j, c0 : c0 + n])
@@ -111,15 +111,18 @@ def tile_picked_sage_silu_e_kernel(tc, xT, w1, w2, gate, offs, pos1, pos2, out):
                 gather_row_scalar(j, s0, n)
         w1_src = [w1_raw[i][:].rearrange("p j (c t) -> p c t j", t=J) for i in range(2)]
 
-        def weave_lo(i):
+        def weave_lo(i, c0=0, n=P // 2):
             nc.vector.tensor_copy(
-                out=w1_lo[i][:].rearrange("p (c e j) -> p c e j", e=2, j=J), in_=w1_src[i][:, :, :2]
+                out=w1_lo[i][:].rearrange("p (c e j) -> p c e j", e=2, j=J)[:, c0 : c0 + n],
+                in_=w1_src[i][:, c0 : c0 + n, :2],
             )
 
-        weave_lo(0)
-        quantize(w1_c, w1_s, w1_lo[0], 0, P)
+        for c0 in (0, P // 4):
+            weave_lo(0, c0, P // 4)
+        for c0 in (0, P // 2):
+            quantize(w1_c, w1_s, w1_lo[0], c0, P // 2)
         x_c = keep.tile([P, S], U32, name="x_c", tag="lo0", align_bytes=64)
-        node_pieces = (((0, 256), (256, 64)), ((320, 256),), ((576, 128), (704, 64)), ((768, 128),), ((896, 128),))
+        node_pieces = (((0, 256), (256, 64)), ((320, 256), (576, 128), (704, 64)), ((768, 256),))
         for piece in node_pieces:
             for s0, n in piece:
                 if s0 < NV:
@@ -136,8 +139,8 @@ def tile_picked_sage_silu_e_kernel(tc, xT, w1, w2, gate, offs, pos1, pos2, out):
 
         weave_lo(1)
         weave_hi(0)
-        quantize(w1_c, w1_s, w1_lo[1], P, P, 0)
         weave_hi(1)
+        quantize(w1_c, w1_s, w1_lo[1], P, P, 0)
         quantize(w1_c, w1_s, w1_hi, 2 * P, 2 * P, 0)
 
         banks = [psum.tile([P, BANK], F32, name=f"bank{i}") for i in range(8)]
@@ -153,7 +156,7 @@ def tile_picked_sage_silu_e_kernel(tc, xT, w1, w2, gate, offs, pos1, pos2, out):
                 stop=True,
             )
 
-        layer1_banks = ((0, 1, 2, 3, 4), (3, 4), (5, 6), (7, 0))
+        layer1_banks = ((0, 3, 4), (3, 4), (5, 6), (7, 0))
 
         for t in range(J):
             pieces = node_pieces if t == 0 else (((0, BANK),), ((BANK, BANK),))

@@ -21,7 +21,7 @@ P = 128
 J = 4
 BANK = 512
 HALF = V // 2
-NV = 320
+NV = 384
 
 
 def tile_picked_sage_silu_e_kernel(tc, xT, w1, w2, gate, offs, pos1, pos2, out):
@@ -122,7 +122,7 @@ def tile_picked_sage_silu_e_kernel(tc, xT, w1, w2, gate, offs, pos1, pos2, out):
         for c0 in (0, P // 2):
             quantize(w1_c, w1_s, w1_lo[0], c0, P // 2)
         x_c = keep.tile([P, S], U32, name="x_c", tag="lo0", align_bytes=64)
-        node_pieces = (((0, 256), (256, 64)), ((320, 256), (576, 128), (704, 64)), ((768, 256),))
+        node_pieces = (((0, 256), (256, 128)), ((384, 256), (640, 128)), ((768, 256),))
         for piece in node_pieces:
             for s0, n in piece:
                 if s0 < NV:

@@ -33,7 +33,7 @@ def tile_picked_sage_silu_e_kernel(tc, xT, w1, w2, gate, offs, pos1, pos2, out):
         offs_sb = keep.tile([P, S // 16], U16, name="offs_sb")
         pos1_sb = keep.tile([P, V // 16], U16, name="pos1_sb")
         pos2_sb = keep.tile([P, V // 16], U16, name="pos2_sb")
-        gate_sb = keep.tile([P, D, V + HALF], F32, name="gate_sb", align_bytes=64)
+        gate_sb = keep.tile([P, D, V], F32, name="gate_sb", align_bytes=64)
         w1_raw = [keep.tile([P, J, H // 2], F32, name=f"w1_raw{i}") for i in range(2)]
         w2_raw = keep.tile([P, J, N], F32, name="w2_raw")
         w1_lo = [keep.tile([P, P * J], BF16, name=f"w1_lo{i}", tag=f"lo{i}", align_bytes=64) for i in range(2)]
@@ -47,10 +47,10 @@ def tile_picked_sage_silu_e_kernel(tc, xT, w1, w2, gate, offs, pos1, pos2, out):
         x_s = keep.tile([P, S], U8, name="x_s", align_bytes=64)
         h = [keep.tile([P, S], F32, name=f"h{t}", tag=f"h{t}", align_bytes=64) for t in range(J)]
         m = [keep.tile([P, J, V], F32, name=f"m{d}", align_bytes=64) for d in range(D)]
-        z_a = keep.tile([P, HALF * J], BF16, name="z_a", tag="za", align_bytes=64)
+        z_a = keep.tile([P, HALF * J], BF16, name="z_a", align_bytes=64)
         z_b = keep.tile([P, HALF * J], BF16, name="z_b", align_bytes=64)
         zt = [keep.tile([P, V], BF16, name=f"zt{i}", align_bytes=64) for i in range(3)]
-        za_c = keep.tile([P, HALF], U32, name="za_c", align_bytes=64)
+        z_c = keep.tile([P, V], U32, name="z_c", align_bytes=64)
         z_s = keep.tile([P, V], U8, name="z_s", align_bytes=64)
         o_sb = keep.tile([P, V], F32, name="o_sb", align_bytes=64)
         ident = keep.tile([P, P], F32, name="ident", align_bytes=64)
@@ -73,7 +73,7 @@ def tile_picked_sage_silu_e_kernel(tc, xT, w1, w2, gate, offs, pos1, pos2, out):
         for i in range(2):
             nc.sync.dma_start(out=w1_raw[i][:], in_=w1_view[:, :, i * H // 2 : (i + 1) * H // 2])
         nc.sync.dma_start(out=pos1_sb[:], in_=pos1)
-        nc.sync.dma_start(out=gate_sb[:, :, :V], in_=gate.rearrange("d p v -> p d v"))
+        nc.sync.dma_start(out=gate_sb[:], in_=gate.rearrange("d p v -> p d v"))
         nc.sync.dma_start(out=pos2_sb[:], in_=pos2)
         nc.sync.dma_start(out=w2_raw[:], in_=w2.rearrange("(p j) n -> p j n", j=J))
 
@@ -176,71 +176,70 @@ def tile_picked_sage_silu_e_kernel(tc, xT, w1, w2, gate, offs, pos1, pos2, out):
                     dst(d), h[t][:].indirect(pos[:, v0 // 16 : (v0 + n) // 16]), gate_sb[:, d, v0 : v0 + n], MULT
                 )
 
-        for t in range(2):
+        for t in range(3):
             fetch(t, 0, V, lambda d: m[d][:, t, :])
-        for t in (2, 3):
-            fetch(t, 0, HALF, lambda d: m[d][:, t, :HALF])
-        fetch(2, HALF, HALF, lambda d: gate_sb[:, d, :HALF])
-        fetch(3, HALF, HALF, lambda d: gate_sb[:, d, V:])
+        for v0 in (0, HALF):
+            fetch(3, v0, HALF, lambda d: m[d][:, 3, v0 : v0 + HALF])
 
-        def add_turned(t, bank, b0):
-            for b in range(2):
-                for d in range(D):
-                    c = 2 * b + t if t < 2 else 2 * (t % 2) + b
-                    nc.tensor.matmul(
-                        bank[:, c * P : (c + 1) * P],
-                        lhsT=m[d][:, t, (b0 + b) * P : (b0 + b + 1) * P],
-                        rhs=ident[:],
-                        start=(d == 0),
-                        stop=(d == D - 1),
-                        is_transpose=True,
-                    )
+        def add_turned(t, dst, b):
+            for d in range(D):
+                nc.tensor.matmul(
+                    dst,
+                    lhsT=m[d][:, t, b * P : (b + 1) * P],
+                    rhs=ident[:],
+                    start=(d == 0),
+                    stop=(d == D - 1),
+                    is_transpose=True,
+                )
 
-        def turn_back(pairs, sums, back):
-            nc.scalar.copy(pairs[:].rearrange("v (b p e) -> v b p e", b=2, e=2), sums)
-            words = pairs[:].bitcast(F32)
-            for b in range(2):
-                nc.tensor.transpose(back[:, b * P : (b + 1) * P], words[:, b * P : (b + 1) * P], ident[:])
-
+        back = (banks[4], banks[6])
         for t in range(2):
-            for i in range(2):
-                add_turned(t, banks[1 + i], 2 * i)
-        for t in (2, 3):
-            add_turned(t, banks[3], 0)
-        turn_back(zt[0], banks[1][:].rearrange("v (b p e) -> v b p e", e=2, b=2), banks[4][:, :HALF])
-        turn_back(zt[1], banks[2][:].rearrange("v (b p e) -> v b p e", e=2, b=2), banks[5][:, :HALF])
-        turn_back(zt[2], banks[3][:].rearrange("v (e b p) -> v b p e", e=2, b=2), banks[4][:, HALF:])
-        nc.scalar.copy(
-            z_a[:].bitcast(F32).rearrange("p (v u) -> p v u", u=2), banks[4][:].rearrange("p (u v) -> p v u", u=2)
-        )
+            for b in range(4):
+                c = 2 * (b % 2) + t
+                add_turned(t, banks[1 + b // 2][:, c * P : (c + 1) * P], b)
+        for i in range(2):
+            nc.scalar.copy(zt[i][:], banks[1 + i][:])
+            words = zt[i][:].bitcast(F32)
+            for b in range(2):
+                dst = back[b][:, :P] if i == 0 else banks[5][:, b * P : (b + 1) * P]
+                nc.tensor.transpose(dst, words[:, b * P : (b + 1) * P], ident[:])
         nc.scalar.copy(z_b[:].bitcast(F32).rearrange("p (v u) -> p v u", u=2)[:, :, 0], banks[5][:, :HALF])
+        turned = (banks[3], banks[7])
+        for t in (2, 3):
+            for b in range(2):
+                add_turned(t, turned[b][:, (t - 2) * P : (t - 1) * P], b)
+        for b in range(2):
+            pairs = zt[2][:, b * HALF : (b + 1) * HALF]
+            nc.scalar.copy(
+                pairs.rearrange("v (p e) -> v p e", e=2), turned[b][:, :HALF].rearrange("v (e p) -> v p e", e=2)
+            )
+            nc.tensor.transpose(back[b][:, P:HALF], pairs.bitcast(F32), ident[:])
+        for b in range(2):
+            nc.scalar.copy(
+                z_a[:, b * BANK : (b + 1) * BANK].bitcast(F32).rearrange("p (v u) -> p v u", u=2),
+                back[b][:, :HALF].rearrange("p (u v) -> p v u", u=2),
+            )
 
         w2_c = keep.tile([P, N], U32, name="w2_c", tag="h3", align_bytes=64)
         quantize(w2_c, w2_s, w2_b, 0, N)
-        late = [gate_sb[:, d, :].rearrange("p (e v) -> p e v", v=HALF)[:, ::2] for d in range(D)]
         for v0 in (0, P):
             pat = "p e (c i) -> p c e i"
             nc.vector.tensor_tensor(
                 z_b[:, J * v0 : J * (v0 + P)].rearrange("p (c i t) -> p c t i", t=J, i=4)[:, :, 2:],
-                late[0][:, :, v0 : v0 + P].rearrange(pat, i=4),
-                late[1][:, :, v0 : v0 + P].rearrange(pat, i=4),
+                m[0][:, 2:, HALF + v0 : HALF + v0 + P].rearrange(pat, i=4),
+                m[1][:, 2:, HALF + v0 : HALF + v0 + P].rearrange(pat, i=4),
                 ADD,
             )
-        quantize(za_c, z_s, z_a, 0, HALF)
-        zb_c = keep.tile([P, HALF], U32, name="zb_c", tag="za", align_bytes=64)
-        for v0 in (0, P):
-            nc.vector.quantize_mx(
-                out=zb_c[:, v0 : v0 + P].bitcast(FP8X4),
-                scales=z_s[:, HALF + v0 : HALF + v0 + P],
-                in_=z_b[:, J * v0 : J * (v0 + P)],
-            )
-        pieces = ((0, HALF, za_c[:]), (HALF, P, zb_c[:, :P]), (HALF + P, P, zb_c[:, P:]))
-        for i, (v0, n, codes) in enumerate(pieces):
-            sl = slice(v0, v0 + n)
-            acc = banks[(6 + i) % 8][:, :n]
-            mx(acc, w2_c, w2_s, 0, codes, z_s[:, sl])
-            if i < 2:
+        for i, b in enumerate((2, 3, 0, 1)):
+            quantize(z_c, z_s, z_b if b >= 2 else z_a, b * P, P, (b % 2) * P)
+        for i, b in enumerate((2, 3, 0, 1)):
+            sl = slice(b * P, (b + 1) * P)
+            acc = banks[i][:, :P]
+            mx(acc, w2_c, w2_s, 0, z_c[:, sl], z_s[:, sl])
+            if i < 3:
                 nc.scalar.copy(o_sb[:, sl], acc)
             else:
                 nc.vector.tensor_copy(out=o_sb[:, sl], in_=acc)
-            nc.sync.dma_start(out=out[:, sl], in_=o_sb[:, sl])
+            if i > 0:
+                sl = slice(HALF, V) if i == 1 else sl
+                nc.sync.dma_start(out=out[:, sl], in_=o_sb[:, sl])

@@ -21,7 +21,7 @@ P = 128
 J = 4
 BANK = 512
 HALF = V // 2
-NV = 384
+NV = (384, 384, 320, 320)
 
 
 def tile_picked_sage_silu_e_kernel(tc, xT, w1, w2, gate, offs, pos1, pos2, out):
@@ -42,8 +42,7 @@ def tile_picked_sage_silu_e_kernel(tc, xT, w1, w2, gate, offs, pos1, pos2, out):
         w2_s = keep.tile([P, N], U8, name="w2_s", align_bytes=64)
         row_f = {j: keep.tile([P, T], F32, name=f"row_f{j}", align_bytes=64) for j in range(J)}
         row_b = {j: keep.tile([P, T], BF16, name=f"row_b{j}", align_bytes=64) for j in range(J)}
-        picked_v = keep.tile([P, NV * J], BF16, name="picked_v", tag="pv", align_bytes=64)
-        picked_s = keep.tile([P, (S - NV) * J], BF16, name="picked_s", align_bytes=64)
+        picked = keep.tile([P, S * J], BF16, name="picked", tag="pv", align_bytes=64)
         x_s = keep.tile([P, S], U8, name="x_s", align_bytes=64)
         h = [keep.tile([P, S], F32, name=f"h{t}", tag=f"h{t}", align_bytes=64) for t in range(J)]
         m = [keep.tile([P, J, V], F32, name=f"m{d}", align_bytes=64) for d in range(D)]
@@ -82,12 +81,13 @@ def tile_picked_sage_silu_e_kernel(tc, xT, w1, w2, gate, offs, pos1, pos2, out):
 
         def gather_row_vector(j):
             nc.vector.tensor_copy(
-                out=picked_v[:].rearrange("p (s j) -> p s j", j=J)[:, :, j], in_=row_f[j][:].indirect(entries(0, NV))
+                out=picked[:].rearrange("p (s j) -> p s j", j=J)[:, : NV[j], j],
+                in_=row_f[j][:].indirect(entries(0, NV[j])),
             )
 
         def gather_row_scalar(j, s0, n):
             nc.scalar.activation(
-                picked_s[:].rearrange("p (s j) -> p s j", j=J)[:, s0 - NV : s0 - NV + n, j],
+                picked[:].rearrange("p (s j) -> p s j", j=J)[:, s0 : s0 + n, j],
                 row_b[j][:].indirect(entries(s0, n)),
                 COPY,
             )
@@ -107,14 +107,14 @@ def tile_picked_sage_silu_e_kernel(tc, xT, w1, w2, gate, offs, pos1, pos2, out):
                 else:
                     nc.vector.tensor_copy(out=row_b[j][:, c0 : c0 + n], in_=row_f[j][:, c0 : c0 + n])
             gather_row_vector(j)
-            for s0, n in ((NV, S - NV),) if j < J - 1 else ((NV, 768 - NV), (768, 256)):
+            for s0, n in ((NV[j], S - NV[j]),) if j < J - 1 else ((NV[j], 768 - NV[j]), (768, 256)):
                 gather_row_scalar(j, s0, n)
-        w1_src = [w1_raw[i][:].rearrange("p j (c t) -> p c t j", t=J) for i in range(2)]
+        w1_src = [w1_raw[i][:].rearrange("p j (c t) -> p c j t", t=J) for i in range(2)]
 
         def weave_lo(i, c0=0, n=P // 2):
             nc.vector.tensor_copy(
-                out=w1_lo[i][:].rearrange("p (c e j) -> p c e j", e=2, j=J)[:, c0 : c0 + n],
-                in_=w1_src[i][:, c0 : c0 + n, :2],
+                out=w1_lo[i][:].rearrange("p (c e j) -> p c j e", e=2, j=J)[:, c0 : c0 + n],
+                in_=w1_src[i][:, c0 : c0 + n, :, :2],
             )
 
         for c0 in (0, P // 4):
@@ -122,19 +122,16 @@ def tile_picked_sage_silu_e_kernel(tc, xT, w1, w2, gate, offs, pos1, pos2, out):
         for c0 in (0, P // 2):
             quantize(w1_c, w1_s, w1_lo[0], c0, P // 2)
         x_c = keep.tile([P, S], U32, name="x_c", tag="lo0", align_bytes=64)
-        node_pieces = (((0, 256), (256, 128)), ((384, 256), (640, 128)), ((768, 256),))
+        node_pieces = (((0, 256),), ((256, 256), (512, 256)), ((768, 256),))
         for piece in node_pieces:
             for s0, n in piece:
-                if s0 < NV:
-                    quantize(x_c, x_s, picked_v, s0, n)
-                else:
-                    quantize(x_c, x_s, picked_s, s0, n, s0 - NV)
+                quantize(x_c, x_s, picked, s0, n)
         w1_hi = keep.tile([P, 2 * P * J], BF16, name="w1_hi", tag="pv", align_bytes=64)
 
         def weave_hi(i):
             nc.vector.tensor_copy(
-                out=w1_hi[:].rearrange("p (e c j) -> p c e j", e=2, j=J)[:, i * P // 2 : (i + 1) * P // 2],
-                in_=w1_src[i][:, :, 2:],
+                out=w1_hi[:].rearrange("p (e c j) -> p c j e", e=2, j=J)[:, i * P // 2 : (i + 1) * P // 2],
+                in_=w1_src[i][:, :, :, 2:],
             )
 
         weave_lo(1)

@@ -42,7 +42,7 @@ def tile_picked_sage_silu_e_kernel(tc, xT, w1, w2, gate, offs, pos1, pos2, out):
         w2_s = keep.tile([P, N], U8, name="w2_s", align_bytes=64)
         row_f = {j: keep.tile([P, T], F32, name=f"row_f{j}", align_bytes=64) for j in range(J)}
         row_b = {j: keep.tile([P, T], BF16, name=f"row_b{j}", align_bytes=64) for j in range(J)}
-        picked = keep.tile([P, S * J], BF16, name="picked", tag="pv", align_bytes=64)
+        picked = keep.tile([P, S * J], BF16, name="picked", align_bytes=64)
         x_s = keep.tile([P, S], U8, name="x_s", align_bytes=64)
         h = [keep.tile([P, S], F32, name=f"h{t}", tag=f"h{t}", align_bytes=64) for t in range(J)]
         m = [keep.tile([P, J, V], F32, name=f"m{d}", align_bytes=64) for d in range(D)]
@@ -111,22 +111,12 @@ def tile_picked_sage_silu_e_kernel(tc, xT, w1, w2, gate, offs, pos1, pos2, out):
                 gather_row_scalar(j, s0, n)
         w1_src = [w1_raw[i][:].rearrange("p j (c t) -> p c j t", t=J) for i in range(2)]
 
-        def weave_lo(i, c0=0, n=P // 2):
-            nc.vector.tensor_copy(
-                out=w1_lo[i][:].rearrange("p (c e j) -> p c j e", e=2, j=J)[:, c0 : c0 + n],
-                in_=w1_src[i][:, c0 : c0 + n, :, :2],
-            )
+        w1_hi = keep.tile([P, 2 * P * J], BF16, name="w1_hi", align_bytes=64)
 
-        for c0 in (0, P // 4):
-            weave_lo(0, c0, P // 4)
-        for c0 in (0, P // 2):
-            quantize(w1_c, w1_s, w1_lo[0], c0, P // 2)
-        x_c = keep.tile([P, S], U32, name="x_c", tag="lo0", align_bytes=64)
-        node_pieces = (((0, 256),), ((256, 256), (512, 256)), ((768, 256),))
-        for piece in node_pieces:
-            for s0, n in piece:
-                quantize(x_c, x_s, picked, s0, n)
-        w1_hi = keep.tile([P, 2 * P * J], BF16, name="w1_hi", tag="pv", align_bytes=64)
+        def weave_lo(i):
+            nc.vector.tensor_copy(
+                out=w1_lo[i][:].rearrange("p (c e j) -> p c j e", e=2, j=J), in_=w1_src[i][:, :, :, :2]
+            )
 
         def weave_hi(i):
             nc.vector.tensor_copy(
@@ -134,8 +124,15 @@ def tile_picked_sage_silu_e_kernel(tc, xT, w1, w2, gate, offs, pos1, pos2, out):
                 in_=w1_src[i][:, :, :, 2:],
             )
 
-        weave_lo(1)
+        weave_lo(0)
         weave_hi(0)
+        quantize(w1_c, w1_s, w1_lo[0], 0, P)
+        x_c = keep.tile([P, S], U32, name="x_c", tag="lo0", align_bytes=64)
+        node_pieces = tuple(((s0, 256),) for s0 in range(0, S, 256))
+        for piece in node_pieces:
+            for s0, n in piece:
+                quantize(x_c, x_s, picked, s0, n)
+        weave_lo(1)
         weave_hi(1)
         quantize(w1_c, w1_s, w1_lo[1], P, P, 0)
         quantize(w1_c, w1_s, w1_hi, 2 * P, 2 * P, 0)
@@ -153,7 +150,7 @@ def tile_picked_sage_silu_e_kernel(tc, xT, w1, w2, gate, offs, pos1, pos2, out):
                 stop=True,
             )
 
-        layer1_banks = ((0, 3, 4), (3, 4), (5, 6), (7, 0))
+        layer1_banks = ((0, 1, 3, 4), (3, 4), (5, 6), (7, 0))
 
         for t in range(J):
             pieces = node_pieces if t == 0 else (((0, BANK),), ((BANK, BANK),))
@@ -222,9 +219,9 @@ def tile_picked_sage_silu_e_kernel(tc, xT, w1, w2, gate, offs, pos1, pos2, out):
         for v0 in (0, P):
             pat = "p e (c i) -> p c e i"
             nc.vector.tensor_tensor(
-                z_b[:, J * v0 : J * (v0 + P)].rearrange("p (c i t) -> p c t i", t=J, i=4)[:, :, 2:],
-                m[0][:, 2:, HALF + v0 : HALF + v0 + P].rearrange(pat, i=4),
-                m[1][:, 2:, HALF + v0 : HALF + v0 + P].rearrange(pat, i=4),
+                z_b[:, J * v0 : J * (v0 + P)].rearrange("p (c i t) -> p c t i", t=J, i=2)[:, :, 2:],
+                m[0][:, 2:, HALF + v0 : HALF + v0 + P].rearrange(pat, i=2),
+                m[1][:, 2:, HALF + v0 : HALF + v0 + P].rearrange(pat, i=2),
                 ADD,
             )
         for i, b in enumerate((2, 3, 0, 1)):

@@ -33,7 +33,8 @@ def tile_picked_sage_silu_e_kernel(tc, xT, w1, w2, gate, offs, pos1, pos2, out):
         offs_sb = keep.tile([P, S // 16], U16, name="offs_sb")
         pos1_sb = keep.tile([P, V // 16], U16, name="pos1_sb")
         pos2_sb = keep.tile([P, V // 16], U16, name="pos2_sb")
-        gate_sb = keep.tile([P, D, V], F32, name="gate_sb", align_bytes=64)
+        gate_lo = [keep.tile([P, 2 * V], F32, name="gate0", align_bytes=64), keep.tile([P, V], F32, name="gate1", align_bytes=64)]
+        gate_sb = [gate_lo[0][:, :V], gate_lo[1][:]]
         w1_raw = [keep.tile([P, J, H // 2], F32, name=f"w1_raw{i}") for i in range(2)]
         w2_raw = keep.tile([P, J, N], F32, name="w2_raw")
         w1_lo = [keep.tile([P, P * J], BF16, name=f"w1_lo{i}", tag=f"lo{i}", align_bytes=64) for i in range(2)]
@@ -72,8 +73,9 @@ def tile_picked_sage_silu_e_kernel(tc, xT, w1, w2, gate, offs, pos1, pos2, out):
         for i in range(2):
             nc.sync.dma_start(out=w1_raw[i][:], in_=w1_view[:, :, i * H // 2 : (i + 1) * H // 2])
         nc.sync.dma_start(out=pos1_sb[:], in_=pos1)
-        nc.sync.dma_start(out=gate_sb[:], in_=gate.rearrange("d p v -> p d v"))
+        nc.sync.dma_start(out=gate_sb[0], in_=gate[0])
         nc.sync.dma_start(out=pos2_sb[:], in_=pos2)
+        nc.sync.dma_start(out=gate_sb[1], in_=gate[1])
         nc.sync.dma_start(out=w2_raw[:], in_=w2.rearrange("(p j) n -> p j n", j=J))
 
         def entries(s0, n):
@@ -128,7 +130,7 @@ def tile_picked_sage_silu_e_kernel(tc, xT, w1, w2, gate, offs, pos1, pos2, out):
         weave_hi(0)
         quantize(w1_c, w1_s, w1_lo[0], 0, P)
         x_c = keep.tile([P, S], U32, name="x_c", tag="lo0", align_bytes=64)
-        node_pieces = tuple(((s0, 256),) for s0 in range(0, S, 256))
+        node_pieces = (((0, 256),), ((256, 256),), ((512, 256),), ((768, 128),), ((896, 128),))
         for piece in node_pieces:
             for s0, n in piece:
                 quantize(x_c, x_s, picked, s0, n)
@@ -150,7 +152,7 @@ def tile_picked_sage_silu_e_kernel(tc, xT, w1, w2, gate, offs, pos1, pos2, out):
                 stop=True,
             )
 
-        layer1_banks = ((0, 1, 3, 4), (3, 4), (5, 6), (7, 0))
+        layer1_banks = ((0, 1, 2, 3, 4), (3, 4), (5, 6), (7, 0))
 
         for t in range(J):
             pieces = node_pieces if t == 0 else (((0, BANK),), ((BANK, BANK),))
@@ -164,16 +166,22 @@ def tile_picked_sage_silu_e_kernel(tc, xT, w1, w2, gate, offs, pos1, pos2, out):
         w2_b = keep.tile([P, N * J], BF16, name="w2_b", tag="lo0", align_bytes=64)
         nc.scalar.activation(w2_b[:].rearrange("p (n j) -> p n j", j=J), w2_raw[:].rearrange("p j n -> p n j"), COPY)
 
-        def fetch(t, v0, n, dst):
-            for d, pos in enumerate((pos1_sb, pos2_sb)):
-                nc.vector.tensor_tensor(
-                    dst(d), h[t][:].indirect(pos[:, v0 // 16 : (v0 + n) // 16]), gate_sb[:, d, v0 : v0 + n], MULT
-                )
+        def fetch(t, d, v0, n, dst):
+            pos = (pos1_sb, pos2_sb)[d]
+            nc.vector.tensor_tensor(
+                dst, h[t][:].indirect(pos[:, v0 // 16 : (v0 + n) // 16]), gate_sb[d][:, v0 : v0 + n], MULT
+            )
 
-        for t in range(3):
-            fetch(t, 0, V, lambda d: m[d][:, t, :])
-        for v0 in (0, HALF):
-            fetch(3, v0, HALF, lambda d: m[d][:, 3, v0 : v0 + HALF])
+        for t in range(2):
+            for d in range(D):
+                fetch(t, d, 0, V, m[d][:, t, :])
+        fetch(2, 0, 0, V, m[0][:, 2, :])
+        fetch(2, 1, 0, HALF, m[1][:, 2, :HALF])
+        for d in range(D):
+            fetch(3, d, 0, HALF, m[d][:, 3, :HALF])
+        fetch(2, 1, HALF, HALF, gate_lo[0][:, :HALF])
+        fetch(3, 0, HALF, HALF, m[0][:, 3, HALF:])
+        fetch(3, 1, HALF, HALF, gate_lo[0][:, 3 * HALF :])
 
         def add_turned(t, dst, b):
             for d in range(D):
@@ -214,14 +222,15 @@ def tile_picked_sage_silu_e_kernel(tc, xT, w1, w2, gate, offs, pos1, pos2, out):
                 back[b][:, :HALF].rearrange("p (u v) -> p v u", u=2),
             )
 
-        w2_c = keep.tile([P, N], U32, name="w2_c", tag="h3", align_bytes=64)
+        w2_c = keep.tile([P, N], U32, name="w2_c", tag="h2", align_bytes=64)
         quantize(w2_c, w2_s, w2_b, 0, N)
+        late = gate_lo[0][:].rearrange("p (e r) -> p e r", r=HALF)[:, ::3]
         for v0 in (0, P):
             pat = "p e (c i) -> p c e i"
             nc.vector.tensor_tensor(
                 z_b[:, J * v0 : J * (v0 + P)].rearrange("p (c i t) -> p c t i", t=J, i=2)[:, :, 2:],
                 m[0][:, 2:, HALF + v0 : HALF + v0 + P].rearrange(pat, i=2),
-                m[1][:, 2:, HALF + v0 : HALF + v0 + P].rearrange(pat, i=2),
+                late[:, :, v0 : v0 + P].rearrange(pat, i=2),
                 ADD,
             )
         for i, b in enumerate((2, 3, 0, 1)):

@@ -35,7 +35,7 @@ def tile_picked_sage_silu_e_kernel(tc, xT, w1, w2, gate, offs, pos1, pos2, out):
         pos2_sb = keep.tile([P, V // 16], U16, name="pos2_sb")
         gate_lo = [keep.tile([P, 2 * V], F32, name="gate0", align_bytes=64), keep.tile([P, V], F32, name="gate1", align_bytes=64)]
         gate_sb = [gate_lo[0][:, :V], gate_lo[1][:]]
-        w1_raw = [keep.tile([P, J, H // 2], F32, name=f"w1_raw{i}") for i in range(2)]
+        w1_raw = [keep.tile([P, J, H // 2], F32, name=f"w1_raw{i}", tag=f"raw{i}", align_bytes=64) for i in range(2)]
         w2_raw = keep.tile([P, J, N], F32, name="w2_raw")
         w1_lo = [keep.tile([P, P * J], BF16, name=f"w1_lo{i}", tag=f"lo{i}", align_bytes=64) for i in range(2)]
         w1_c = keep.tile([P, H], U32, name="w1_c", align_bytes=64)
@@ -62,8 +62,10 @@ def tile_picked_sage_silu_e_kernel(tc, xT, w1, w2, gate, offs, pos1, pos2, out):
 
         x_view = xT.rearrange("(p j) t -> p j t", j=J)
         two = ((0, 1280), (1280, 768))
-        tapered = ((0, 1024), (1024, 768), (1792, 256))
-        row_chunks = (tapered, two, two, two)
+        row_chunks = (two, two, two, two)
+        round_cuts = (((0, 640, False), (640, 640, True), (1280, 512, False), (1792, 256, True)),) + 3 * (
+            tuple((c0, n, False) for c0, n in two),
+        )
         for j in range(J):
             for c0, n in row_chunks[j]:
                 nc.sync.dma_start(out=row_f[j][:, c0 : c0 + n], in_=x_view[:, j, c0 : c0 + n])
@@ -103,8 +105,8 @@ def tile_picked_sage_silu_e_kernel(tc, xT, w1, w2, gate, offs, pos1, pos2, out):
             )
 
         for j in range(J):
-            for c0, n in row_chunks[j]:
-                if j == 0 and n != 768:
+            for c0, n, on_scalar in round_cuts[j]:
+                if on_scalar:
                     nc.scalar.activation(row_b[j][:, c0 : c0 + n], row_f[j][:, c0 : c0 + n], COPY)
                 else:
                     nc.vector.tensor_copy(out=row_b[j][:, c0 : c0 + n], in_=row_f[j][:, c0 : c0 + n])
@@ -129,7 +131,7 @@ def tile_picked_sage_silu_e_kernel(tc, xT, w1, w2, gate, offs, pos1, pos2, out):
         weave_lo(0)
         weave_hi(0)
         quantize(w1_c, w1_s, w1_lo[0], 0, P)
-        x_c = keep.tile([P, S], U32, name="x_c", tag="lo0", align_bytes=64)
+        x_c = keep.tile([P, S], U32, name="x_c", tag="raw0", align_bytes=64)
         node_pieces = (((0, 256),), ((256, 256),), ((512, 256),), ((768, 128),), ((896, 128),))
         for piece in node_pieces:
             for s0, n in piece:
@@ -163,7 +165,7 @@ def tile_picked_sage_silu_e_kernel(tc, xT, w1, w2, gate, offs, pos1, pos2, out):
                     mx(acc, w1_c, w1_s, P * t, x_c[:, s0 : s0 + n], x_s[:, s0 : s0 + n])
                 nc.scalar.activation(h[t][:, first:end], banks[b][:, : end - first], SILU)
 
-        w2_b = keep.tile([P, N * J], BF16, name="w2_b", tag="lo0", align_bytes=64)
+        w2_b = keep.tile([P, N * J], BF16, name="w2_b", tag="raw0", align_bytes=64)
         nc.scalar.activation(w2_b[:].rearrange("p (n j) -> p n j", j=J), w2_raw[:].rearrange("p j n -> p n j"), COPY)
 
         def fetch(t, d, v0, n, dst):

@@ -21,6 +21,7 @@ P = 128
 J = 4
 BANK = 512
 HALF = V // 2
+TURNED = 3 * P
 NV = (384, 384, 320, 320)
 
 
@@ -47,9 +48,9 @@ def tile_picked_sage_silu_e_kernel(tc, xT, w1, w2, gate, offs, pos1, pos2, out):
         x_s = keep.tile([P, S], U8, name="x_s", align_bytes=64)
         h = [keep.tile([P, S], F32, name=f"h{t}", tag=f"h{t}", align_bytes=64) for t in range(J)]
         m = [keep.tile([P, J, V], F32, name=f"m{d}", align_bytes=64) for d in range(D)]
-        z_a = keep.tile([P, HALF * J], BF16, name="z_a", align_bytes=64)
-        z_b = keep.tile([P, HALF * J], BF16, name="z_b", align_bytes=64)
-        zt = [keep.tile([P, V], BF16, name=f"zt{i}", align_bytes=64) for i in range(3)]
+        z = [keep.tile([P, P * J], BF16, name=f"z{b}", align_bytes=64) for b in range(4)]
+        zt = [keep.tile([P, V], BF16, name=f"zt{i}", align_bytes=64) for i in range(2)]
+        pairs = [keep.tile([P, 2 * P], BF16, name=f"pairs{b}", align_bytes=64) for b in range(3)]
         z_c = keep.tile([P, V], U32, name="z_c", align_bytes=64)
         z_s = keep.tile([P, V], U8, name="z_s", align_bytes=64)
         o_sb = keep.tile([P, V], F32, name="o_sb", align_bytes=64)
@@ -177,13 +178,15 @@ def tile_picked_sage_silu_e_kernel(tc, xT, w1, w2, gate, offs, pos1, pos2, out):
         for t in range(2):
             for d in range(D):
                 fetch(t, d, 0, V, m[d][:, t, :])
-        fetch(2, 0, 0, V, m[0][:, 2, :])
-        fetch(2, 1, 0, HALF, m[1][:, 2, :HALF])
         for d in range(D):
-            fetch(3, d, 0, HALF, m[d][:, 3, :HALF])
-        fetch(2, 1, HALF, HALF, gate_lo[0][:, :HALF])
-        fetch(3, 0, HALF, HALF, m[0][:, 3, HALF:])
-        fetch(3, 1, HALF, HALF, gate_lo[0][:, 3 * HALF :])
+            fetch(2, d, 0, TURNED, m[d][:, 2, :TURNED])
+        fetch(3, 0, 0, TURNED, m[0][:, 3, :TURNED])
+        fetch(3, 1, 0, HALF, m[1][:, 3, :HALF])
+        fetch(3, 1, HALF, P, m[1][:, 3, HALF:TURNED])
+        late = gate_lo[0][:].rearrange("p (e d r) -> p e d r", e=2, r=P)
+        for t in (2, 3):
+            for d in range(D):
+                fetch(t, d, TURNED, P, late[:, t - 2, d, :])
 
         def add_turned(t, dst, b):
             for d in range(D):
@@ -196,7 +199,7 @@ def tile_picked_sage_silu_e_kernel(tc, xT, w1, w2, gate, offs, pos1, pos2, out):
                     is_transpose=True,
                 )
 
-        back = (banks[4], banks[6])
+        back = (banks[4], banks[6], banks[5])
         for t in range(2):
             for b in range(4):
                 c = 2 * (b % 2) + t
@@ -204,47 +207,49 @@ def tile_picked_sage_silu_e_kernel(tc, xT, w1, w2, gate, offs, pos1, pos2, out):
         for i in range(2):
             nc.scalar.copy(zt[i][:], banks[1 + i][:])
             words = zt[i][:].bitcast(F32)
-            for b in range(2):
-                dst = back[b][:, :P] if i == 0 else banks[5][:, b * P : (b + 1) * P]
-                nc.tensor.transpose(dst, words[:, b * P : (b + 1) * P], ident[:])
-        nc.scalar.copy(z_b[:].bitcast(F32).rearrange("p (v u) -> p v u", u=2)[:, :, 0], banks[5][:, :HALF])
-        turned = (banks[3], banks[7])
-        for t in (2, 3):
-            for b in range(2):
-                add_turned(t, turned[b][:, (t - 2) * P : (t - 1) * P], b)
-        for b in range(2):
-            pairs = zt[2][:, b * HALF : (b + 1) * HALF]
+            for b in (2 * i, 2 * i + 1):
+                dst = back[b][:, :P] if b < 3 else back[2][:, HALF:TURNED]
+                nc.tensor.transpose(dst, words[:, (b % 2) * P : (b % 2 + 1) * P], ident[:])
+        nc.scalar.copy(z[3][:].bitcast(F32).rearrange("p (v u) -> p v u", u=2)[:, :, 0], back[2][:, HALF:TURNED])
+        pair_views = [pairs[b][:].rearrange("v (p e) -> v p e", e=2) for b in range(3)]
+        for b in range(3):
+            add_turned(2, banks[3][:, b * P : (b + 1) * P], b)
+        for b in range(3):
+            nc.scalar.copy(pair_views[b][:, :, 0], banks[3][:, b * P : (b + 1) * P])
+        turned = (banks[7], banks[0], banks[1])
+        for b in range(3):
+            add_turned(3, turned[b][:, :P], b)
+        for b in range(3):
+            nc.scalar.copy(pair_views[b][:, :, 1], turned[b][:, :P])
+            nc.tensor.transpose(back[b][:, P:HALF], pairs[b][:].bitcast(F32), ident[:])
+        for b in range(3):
             nc.scalar.copy(
-                pairs.rearrange("v (p e) -> v p e", e=2), turned[b][:, :HALF].rearrange("v (e p) -> v p e", e=2)
-            )
-            nc.tensor.transpose(back[b][:, P:HALF], pairs.bitcast(F32), ident[:])
-        for b in range(2):
-            nc.scalar.copy(
-                z_a[:, b * BANK : (b + 1) * BANK].bitcast(F32).rearrange("p (v u) -> p v u", u=2),
+                z[b][:].bitcast(F32).rearrange("p (v u) -> p v u", u=2),
                 back[b][:, :HALF].rearrange("p (u v) -> p v u", u=2),
             )
 
         w2_c = keep.tile([P, N], U32, name="w2_c", tag="h2", align_bytes=64)
         quantize(w2_c, w2_s, w2_b, 0, N)
-        late = gate_lo[0][:].rearrange("p (e r) -> p e r", r=HALF)[:, ::3]
-        for v0 in (0, P):
-            pat = "p e (c i) -> p c e i"
+        pat = "p e (c i) -> p c e i"
+        for v0 in (0, P // 2):
             nc.vector.tensor_tensor(
-                z_b[:, J * v0 : J * (v0 + P)].rearrange("p (c i t) -> p c t i", t=J, i=2)[:, :, 2:],
-                m[0][:, 2:, HALF + v0 : HALF + v0 + P].rearrange(pat, i=2),
-                late[:, :, v0 : v0 + P].rearrange(pat, i=2),
+                z[3][:, J * v0 : J * (v0 + P // 2)].rearrange("p (c i t) -> p c t i", t=J, i=2)[:, :, 2:],
+                late[:, :, 0, v0 : v0 + P // 2].rearrange(pat, i=2),
+                late[:, :, 1, v0 : v0 + P // 2].rearrange(pat, i=2),
                 ADD,
             )
-        for i, b in enumerate((2, 3, 0, 1)):
-            quantize(z_c, z_s, z_b if b >= 2 else z_a, b * P, P, (b % 2) * P)
-        for i, b in enumerate((2, 3, 0, 1)):
+        for v0 in (0, P // 2):
+            quantize(z_c, z_s, z[3], TURNED + v0, P // 2, v0)
+        for b in range(3):
+            quantize(z_c, z_s, z[b], b * P, P, 0)
+        for i, b in enumerate((3, 0, 1, 2)):
             sl = slice(b * P, (b + 1) * P)
-            acc = banks[i][:, :P]
+            acc = banks[(6, 3, 7, 0)[i]][:, :P]
             mx(acc, w2_c, w2_s, 0, z_c[:, sl], z_s[:, sl])
             if i < 3:
                 nc.scalar.copy(o_sb[:, sl], acc)
             else:
                 nc.vector.tensor_copy(out=o_sb[:, sl], in_=acc)
-            if i > 0:
-                sl = slice(HALF, V) if i == 1 else sl
+            if i != 2:
+                sl = slice(P, TURNED) if i == 3 else sl
                 nc.sync.dma_start(out=out[:, sl], in_=o_sb[:, sl])

@@ -18,11 +18,16 @@ ADD = mybir.AluOpType.add
 MULT = mybir.AluOpType.mult
 
 P = 128
-J = 4
+QUAD = 4
 BANK = 512
-HALF = V // 2
-TURNED = 3 * P
-NV = (384, 384, 320, 320)
+PER_COLUMN = 16
+LAST = V // P - 1
+TURNED = LAST * P
+
+ROW_CHUNKS = (((0, 1024), (1024, 768), (1792, 256)),) + 3 * (((0, 1280), (1280, 768)),)
+VECTOR_NODES = (384, 384, 320, 320)
+NODE_PIECES = ((0, 256), (256, 256), (512, 256), (768, 128), (896, 128))
+LAST_GATHER = 768
 
 
 def tile_picked_sage_silu_e_kernel(tc, xT, w1, w2, gate, offs, pos1, pos2, out):
@@ -31,29 +36,29 @@ def tile_picked_sage_silu_e_kernel(tc, xT, w1, w2, gate, offs, pos1, pos2, out):
         keep = ctx.enter_context(tc.tile_pool(name="keep", bufs=1))
         psum = ctx.enter_context(tc.psum_pool(name="psum", bufs=1))
 
-        offs_sb = keep.tile([P, S // 16], U16, name="offs_sb")
-        pos1_sb = keep.tile([P, V // 16], U16, name="pos1_sb")
-        pos2_sb = keep.tile([P, V // 16], U16, name="pos2_sb")
-        gate_lo = [keep.tile([P, 2 * V], F32, name="gate0", align_bytes=64), keep.tile([P, V], F32, name="gate1", align_bytes=64)]
-        gate_sb = [gate_lo[0][:, :V], gate_lo[1][:]]
-        w1_raw = [keep.tile([P, J, H // 2], F32, name=f"w1_raw{i}", tag=f"raw{i}", align_bytes=64) for i in range(2)]
-        w2_raw = keep.tile([P, J, N], F32, name="w2_raw")
-        w1_lo = [keep.tile([P, P * J], BF16, name=f"w1_lo{i}", tag=f"lo{i}", align_bytes=64) for i in range(2)]
-        w1_c = keep.tile([P, H], U32, name="w1_c", align_bytes=64)
-        w1_s = keep.tile([P, H], U8, name="w1_s", align_bytes=64)
-        w2_s = keep.tile([P, N], U8, name="w2_s", align_bytes=64)
-        row_f = {j: keep.tile([P, T], F32, name=f"row_f{j}", align_bytes=64) for j in range(J)}
-        row_b = {j: keep.tile([P, T], BF16, name=f"row_b{j}", align_bytes=64) for j in range(J)}
-        picked = keep.tile([P, S * J], BF16, name="picked", align_bytes=64)
-        x_s = keep.tile([P, S], U8, name="x_s", align_bytes=64)
-        h = [keep.tile([P, S], F32, name=f"h{t}", tag=f"h{t}", align_bytes=64) for t in range(J)]
-        m = [keep.tile([P, J, V], F32, name=f"m{d}", align_bytes=64) for d in range(D)]
-        z = [keep.tile([P, P * J], BF16, name=f"z{b}", align_bytes=64) for b in range(4)]
-        zt = [keep.tile([P, V], BF16, name=f"zt{i}", align_bytes=64) for i in range(2)]
-        pairs = [keep.tile([P, 2 * P], BF16, name=f"pairs{b}", align_bytes=64) for b in range(3)]
-        z_c = keep.tile([P, V], U32, name="z_c", align_bytes=64)
-        z_s = keep.tile([P, V], U8, name="z_s", align_bytes=64)
-        o_sb = keep.tile([P, V], F32, name="o_sb", align_bytes=64)
+        offs_sb = keep.tile([P, S // PER_COLUMN], U16, name="offs_sb")
+        pos1_sb = keep.tile([P, V // PER_COLUMN], U16, name="pos1_sb")
+        pos2_sb = keep.tile([P, V // PER_COLUMN], U16, name="pos2_sb")
+        gate0_tile = keep.tile([P, 2 * V], F32, name="gate0", align_bytes=64)
+        gate1_tile = keep.tile([P, V], F32, name="gate1", align_bytes=64)
+        gate_sb = (gate0_tile[:, :V], gate1_tile[:])
+        w1_raw = [keep.tile([P, QUAD, H // 2], F32, name=f"w1_raw{i}", tag=f"raw{i}", align_bytes=64) for i in range(2)]
+        w2_raw = keep.tile([P, QUAD, N], F32, name="w2_raw")
+        w1_lo = [keep.tile([P, P * QUAD], BF16, name=f"w1_lo{i}", align_bytes=64) for i in range(2)]
+        w1_codes = keep.tile([P, H], U32, name="w1_codes", align_bytes=64)
+        w1_scales = keep.tile([P, H], U8, name="w1_scales", align_bytes=64)
+        w2_scales = keep.tile([P, N], U8, name="w2_scales", align_bytes=64)
+        row_f32 = [keep.tile([P, T], F32, name=f"row_f32_{j}", align_bytes=64) for j in range(QUAD)]
+        row_bf16 = [keep.tile([P, T], BF16, name=f"row_bf16_{j}", align_bytes=64) for j in range(QUAD)]
+        picked = keep.tile([P, S * QUAD], BF16, name="picked", align_bytes=64)
+        x_scales = keep.tile([P, S], U8, name="x_scales", align_bytes=64)
+        h = [keep.tile([P, S], F32, name=f"h{t}", tag=f"h{t}", align_bytes=64) for t in range(QUAD)]
+        gated = [keep.tile([P, QUAD, V], F32, name=f"gated{d}", align_bytes=64) for d in range(D)]
+        z = [keep.tile([P, P * QUAD], BF16, name=f"z{b}", tag=f"z{b}", align_bytes=64) for b in range(LAST + 1)]
+        low = [keep.tile([P, 2 * P], BF16, name=f"low{b}", align_bytes=64) for b in range(LAST + 1)]
+        high = [keep.tile([P, 2 * P], BF16, name=f"high{b}", align_bytes=64) for b in range(LAST)]
+        z_scales = keep.tile([P, V], U8, name="z_scales", align_bytes=64)
+        result = keep.tile([P, V], F32, name="result", align_bytes=64)
         ident = keep.tile([P, P], F32, name="ident", align_bytes=64)
         warm = keep.tile([P, 1], F32, name="warm")
 
@@ -61,94 +66,69 @@ def tile_picked_sage_silu_e_kernel(tc, xT, w1, w2, gate, offs, pos1, pos2, out):
         nc.scalar.activation(warm[:], warm[:], SILU)
         make_identity(nc, ident[:])
 
-        x_view = xT.rearrange("(p j) t -> p j t", j=J)
-        two = ((0, 1280), (1280, 768))
-        row_chunks = (two, two, two, two)
-        round_cuts = (((0, 640, False), (640, 640, True), (1280, 512, False), (1792, 256, True)),) + 3 * (
-            tuple((c0, n, False) for c0, n in two),
-        )
-        for j in range(J):
-            for c0, n in row_chunks[j]:
-                nc.sync.dma_start(out=row_f[j][:, c0 : c0 + n], in_=x_view[:, j, c0 : c0 + n])
+        x_view = xT.rearrange("(p j) t -> p j t", j=QUAD)
+        for j in range(QUAD):
+            for c0, n in ROW_CHUNKS[j]:
+                nc.sync.dma_start(out=row_f32[j][:, c0 : c0 + n], in_=x_view[:, j, c0 : c0 + n])
                 if j == 0 and c0 == 0:
                     nc.sync.dma_start(out=offs_sb[:], in_=offs)
-        w1_view = w1.rearrange("(p j) c -> p j c", j=J)
+        w1_view = w1.rearrange("(p j) c -> p j c", j=QUAD)
         for i in range(2):
             nc.sync.dma_start(out=w1_raw[i][:], in_=w1_view[:, :, i * H // 2 : (i + 1) * H // 2])
-        nc.sync.dma_start(out=pos1_sb[:], in_=pos1)
-        nc.sync.dma_start(out=gate_sb[0], in_=gate[0])
-        nc.sync.dma_start(out=pos2_sb[:], in_=pos2)
-        nc.sync.dma_start(out=gate_sb[1], in_=gate[1])
-        nc.sync.dma_start(out=w2_raw[:], in_=w2.rearrange("(p j) n -> p j n", j=J))
+        for d, (pos_sb, pos) in enumerate(((pos1_sb, pos1), (pos2_sb, pos2))):
+            nc.sync.dma_start(out=pos_sb[:], in_=pos)
+            nc.sync.dma_start(out=gate_sb[d], in_=gate[d])
+        nc.sync.dma_start(out=w2_raw[:], in_=w2.rearrange("(p j) n -> p j n", j=QUAD))
 
-        def entries(s0, n):
-            return offs_sb[:, s0 // 16 : (s0 + n) // 16]
+        def entries(list_sb, first, n):
+            return list_sb[:, first // PER_COLUMN : (first + n) // PER_COLUMN]
 
-        def gather_row_vector(j):
-            nc.vector.tensor_copy(
-                out=picked[:].rearrange("p (s j) -> p s j", j=J)[:, : NV[j], j],
-                in_=row_f[j][:].indirect(entries(0, NV[j])),
-            )
+        def quantize(codes, scales, quads):
+            nc.vector.quantize_mx(out=codes.bitcast(FP8X4), scales=scales, in_=quads)
 
-        def gather_row_scalar(j, s0, n):
-            nc.scalar.activation(
-                picked[:].rearrange("p (s j) -> p s j", j=J)[:, s0 : s0 + n, j],
-                row_b[j][:].indirect(entries(s0, n)),
-                COPY,
-            )
-
-        def quantize(codes, scales, src, c0, n, s0=None):
-            s0 = c0 if s0 is None else s0
-            nc.vector.quantize_mx(
-                out=codes[:, c0 : c0 + n].bitcast(FP8X4),
-                scales=scales[:, c0 : c0 + n],
-                in_=src[:, J * s0 : J * (s0 + n)],
-            )
-
-        for j in range(J):
-            for c0, n, on_scalar in round_cuts[j]:
-                if on_scalar:
-                    nc.scalar.activation(row_b[j][:, c0 : c0 + n], row_f[j][:, c0 : c0 + n], COPY)
+        picked_quads = picked[:].rearrange("p (s j) -> p s j", j=QUAD)
+        for j in range(QUAD):
+            for i, (c0, n) in enumerate(ROW_CHUNKS[j]):
+                if j == 0 and i != 1:
+                    nc.scalar.activation(row_bf16[j][:, c0 : c0 + n], row_f32[j][:, c0 : c0 + n], COPY)
                 else:
-                    nc.vector.tensor_copy(out=row_b[j][:, c0 : c0 + n], in_=row_f[j][:, c0 : c0 + n])
-            gather_row_vector(j)
-            for s0, n in ((NV[j], S - NV[j]),) if j < J - 1 else ((NV[j], 768 - NV[j]), (768, 256)):
-                gather_row_scalar(j, s0, n)
-        w1_src = [w1_raw[i][:].rearrange("p j (c t) -> p c j t", t=J) for i in range(2)]
+                    nc.vector.tensor_copy(out=row_bf16[j][:, c0 : c0 + n], in_=row_f32[j][:, c0 : c0 + n])
+            split = VECTOR_NODES[j]
+            nc.vector.tensor_copy(out=picked_quads[:, :split, j], in_=row_f32[j][:].indirect(entries(offs_sb, 0, split)))
+            cuts = (split, S) if j < QUAD - 1 else (split, LAST_GATHER, S)
+            for s0, s1 in zip(cuts, cuts[1:]):
+                nc.scalar.activation(
+                    picked_quads[:, s0:s1, j], row_bf16[j][:].indirect(entries(offs_sb, s0, s1 - s0)), COPY
+                )
 
-        w1_hi = keep.tile([P, 2 * P * J], BF16, name="w1_hi", align_bytes=64)
+        w1_src = [w1_raw[i][:].rearrange("p j (c t) -> p c j t", t=QUAD) for i in range(2)]
+        w1_hi = keep.tile([P, 2 * P * QUAD], BF16, name="w1_hi", align_bytes=64)
 
-        def weave_lo(i):
+        def weave_w1_half(i):
             nc.vector.tensor_copy(
-                out=w1_lo[i][:].rearrange("p (c e j) -> p c j e", e=2, j=J), in_=w1_src[i][:, :, :, :2]
+                out=w1_lo[i][:].rearrange("p (c e j) -> p c j e", e=2, j=QUAD), in_=w1_src[i][:, :, :, :2]
             )
-
-        def weave_hi(i):
             nc.vector.tensor_copy(
-                out=w1_hi[:].rearrange("p (e c j) -> p c j e", e=2, j=J)[:, i * P // 2 : (i + 1) * P // 2],
+                out=w1_hi[:].rearrange("p (e c j) -> p c j e", e=2, j=QUAD)[:, i * P // 2 : (i + 1) * P // 2],
                 in_=w1_src[i][:, :, :, 2:],
             )
 
-        weave_lo(0)
-        weave_hi(0)
-        quantize(w1_c, w1_s, w1_lo[0], 0, P)
-        x_c = keep.tile([P, S], U32, name="x_c", tag="raw0", align_bytes=64)
-        node_pieces = (((0, 256),), ((256, 256),), ((512, 256),), ((768, 128),), ((896, 128),))
-        for piece in node_pieces:
-            for s0, n in piece:
-                quantize(x_c, x_s, picked, s0, n)
-        weave_lo(1)
-        weave_hi(1)
-        quantize(w1_c, w1_s, w1_lo[1], P, P, 0)
-        quantize(w1_c, w1_s, w1_hi, 2 * P, 2 * P, 0)
+        weave_w1_half(0)
+        quantize(w1_codes[:, :P], w1_scales[:, :P], w1_lo[0][:])
+        x_codes = keep.tile([P, S], U32, name="x_codes", tag="raw0", align_bytes=64)
+        for s0, n in NODE_PIECES:
+            quantize(x_codes[:, s0 : s0 + n], x_scales[:, s0 : s0 + n], picked[:, QUAD * s0 : QUAD * (s0 + n)])
+        weave_w1_half(1)
+        quantize(w1_codes[:, P : 2 * P], w1_scales[:, P : 2 * P], w1_lo[1][:])
+        quantize(w1_codes[:, 2 * P :], w1_scales[:, 2 * P :], w1_hi[:])
 
         banks = [psum.tile([P, BANK], F32, name=f"bank{i}") for i in range(8)]
 
-        def mx(acc, w_c, w_s, c0, codes, scales):
+        def product(acc, w_codes, w_scales, codes, scales):
             nc.tensor.matmul_mx(
                 out=acc,
-                lhsT=w_c[:, c0 : c0 + P].bitcast(FP8X4),
-                lhsT_scale=w_s[:, c0 : c0 + P],
+                lhsT=w_codes.bitcast(FP8X4),
+                lhsT_scale=w_scales,
                 rhs=codes.bitcast(FP8X4),
                 rhs_scale=scales,
                 start=True,
@@ -156,100 +136,92 @@ def tile_picked_sage_silu_e_kernel(tc, xT, w1, w2, gate, offs, pos1, pos2, out):
             )
 
         layer1_banks = ((0, 1, 2, 3, 4), (3, 4), (5, 6), (7, 0))
+        for t in range(QUAD):
+            cols = slice(t * P, (t + 1) * P)
+            for (s0, n), bank in zip(NODE_PIECES if t == 0 else ((0, BANK), (BANK, BANK)), layer1_banks[t]):
+                nodes = slice(s0, s0 + n)
+                product(banks[bank][:, :n], w1_codes[:, cols], w1_scales[:, cols], x_codes[:, nodes], x_scales[:, nodes])
+                nc.scalar.activation(h[t][:, nodes], banks[bank][:, :n], SILU)
 
-        for t in range(J):
-            pieces = node_pieces if t == 0 else (((0, BANK),), ((BANK, BANK),))
-            for piece, b in zip(pieces, layer1_banks[t]):
-                first, end = piece[0][0], sum(piece[-1])
-                for s0, n in piece:
-                    acc = banks[b][:, s0 - first : s0 - first + n]
-                    mx(acc, w1_c, w1_s, P * t, x_c[:, s0 : s0 + n], x_s[:, s0 : s0 + n])
-                nc.scalar.activation(h[t][:, first:end], banks[b][:, : end - first], SILU)
-
-        w2_b = keep.tile([P, N * J], BF16, name="w2_b", tag="raw0", align_bytes=64)
-        nc.scalar.activation(w2_b[:].rearrange("p (n j) -> p n j", j=J), w2_raw[:].rearrange("p j n -> p n j"), COPY)
+        w2_quads = keep.tile([P, N * QUAD], BF16, name="w2_quads", tag="raw0", align_bytes=64)
+        nc.scalar.activation(
+            w2_quads[:].rearrange("p (n j) -> p n j", j=QUAD), w2_raw[:].rearrange("p j n -> p n j"), COPY
+        )
 
         def fetch(t, d, v0, n, dst):
-            pos = (pos1_sb, pos2_sb)[d]
-            nc.vector.tensor_tensor(
-                dst, h[t][:].indirect(pos[:, v0 // 16 : (v0 + n) // 16]), gate_sb[d][:, v0 : v0 + n], MULT
-            )
+            offsets = entries((pos1_sb, pos2_sb)[d], v0, n)
+            nc.vector.tensor_tensor(dst, h[t][:].indirect(offsets), gate_sb[d][:, v0 : v0 + n], MULT)
 
         for t in range(2):
             for d in range(D):
-                fetch(t, d, 0, V, m[d][:, t, :])
+                fetch(t, d, 0, V, gated[d][:, t, :])
         for d in range(D):
-            fetch(2, d, 0, TURNED, m[d][:, 2, :TURNED])
-        fetch(3, 0, 0, TURNED, m[0][:, 3, :TURNED])
-        fetch(3, 1, 0, HALF, m[1][:, 3, :HALF])
-        fetch(3, 1, HALF, P, m[1][:, 3, HALF:TURNED])
-        late = gate_lo[0][:].rearrange("p (e d r) -> p e d r", e=2, r=P)
+            fetch(2, d, 0, TURNED, gated[d][:, 2, :TURNED])
+        fetch(3, 0, 0, TURNED, gated[0][:, 3, :TURNED])
+        fetch(3, 1, 0, 2 * P, gated[1][:, 3, : 2 * P])
+        fetch(3, 1, 2 * P, P, gated[1][:, 3, 2 * P : TURNED])
+        late = gate0_tile[:].rearrange("p (e d r) -> p e d r", e=2, r=P)
         for t in (2, 3):
             for d in range(D):
                 fetch(t, d, TURNED, P, late[:, t - 2, d, :])
 
-        def add_turned(t, dst, b):
+        def add_turned(t, b):
             for d in range(D):
                 nc.tensor.matmul(
-                    dst,
-                    lhsT=m[d][:, t, b * P : (b + 1) * P],
+                    banks[1 + b][:, t % 2 * P : (t % 2 + 1) * P],
+                    lhsT=gated[d][:, t, b * P : (b + 1) * P],
                     rhs=ident[:],
                     start=(d == 0),
                     stop=(d == D - 1),
                     is_transpose=True,
                 )
 
-        back = (banks[4], banks[6], banks[5])
+        back = banks[5:8]
+        last_first = (LAST,) + tuple(range(LAST))
+        last_low_words = banks[1 + LAST][:, 2 * P : 3 * P]
         for t in range(2):
-            for b in range(4):
-                c = 2 * (b % 2) + t
-                add_turned(t, banks[1 + b // 2][:, c * P : (c + 1) * P], b)
-        for i in range(2):
-            nc.scalar.copy(zt[i][:], banks[1 + i][:])
-            words = zt[i][:].bitcast(F32)
-            for b in (2 * i, 2 * i + 1):
-                dst = back[b][:, :P] if b < 3 else back[2][:, HALF:TURNED]
-                nc.tensor.transpose(dst, words[:, (b % 2) * P : (b % 2 + 1) * P], ident[:])
-        nc.scalar.copy(z[3][:].bitcast(F32).rearrange("p (v u) -> p v u", u=2)[:, :, 0], back[2][:, HALF:TURNED])
-        pair_views = [pairs[b][:].rearrange("v (p e) -> v p e", e=2) for b in range(3)]
-        for b in range(3):
-            add_turned(2, banks[3][:, b * P : (b + 1) * P], b)
-        for b in range(3):
-            nc.scalar.copy(pair_views[b][:, :, 0], banks[3][:, b * P : (b + 1) * P])
-        turned = (banks[7], banks[0], banks[1])
-        for b in range(3):
-            add_turned(3, turned[b][:, :P], b)
-        for b in range(3):
-            nc.scalar.copy(pair_views[b][:, :, 1], turned[b][:, :P])
-            nc.tensor.transpose(back[b][:, P:HALF], pairs[b][:].bitcast(F32), ident[:])
-        for b in range(3):
+            for b in last_first:
+                add_turned(t, b)
+        for b in last_first:
+            nc.scalar.copy(low[b][:], banks[1 + b][:, : 2 * P])
+            nc.tensor.transpose(back[b][:, :P] if b < LAST else last_low_words, low[b][:].bitcast(F32), ident[:])
+        z_words = [z[b][:].bitcast(F32).rearrange("p (v u) -> p v u", u=2) for b in range(LAST + 1)]
+        nc.scalar.copy(z_words[LAST][:, :, 0], last_low_words)
+        for t in (2, 3):
+            for b in range(LAST):
+                add_turned(t, b)
+        for b in range(LAST):
             nc.scalar.copy(
-                z[b][:].bitcast(F32).rearrange("p (v u) -> p v u", u=2),
-                back[b][:, :HALF].rearrange("p (u v) -> p v u", u=2),
+                high[b][:].rearrange("v (p e) -> v p e", e=2),
+                banks[1 + b][:, : 2 * P].rearrange("v (e p) -> v p e", e=2),
             )
+            nc.tensor.transpose(back[b][:, P : 2 * P], high[b][:].bitcast(F32), ident[:])
+        for b in range(LAST):
+            nc.scalar.copy(z_words[b], back[b][:, : 2 * P].rearrange("p (u v) -> p v u", u=2))
 
-        w2_c = keep.tile([P, N], U32, name="w2_c", tag="h2", align_bytes=64)
-        quantize(w2_c, w2_s, w2_b, 0, N)
-        pat = "p e (c i) -> p c e i"
-        for v0 in (0, P // 2):
-            nc.vector.tensor_tensor(
-                z[3][:, J * v0 : J * (v0 + P // 2)].rearrange("p (c i t) -> p c t i", t=J, i=2)[:, :, 2:],
-                late[:, :, 0, v0 : v0 + P // 2].rearrange(pat, i=2),
-                late[:, :, 1, v0 : v0 + P // 2].rearrange(pat, i=2),
-                ADD,
-            )
-        for v0 in (0, P // 2):
-            quantize(z_c, z_s, z[3], TURNED + v0, P // 2, v0)
-        for b in range(3):
-            quantize(z_c, z_s, z[b], b * P, P, 0)
-        for i, b in enumerate((3, 0, 1, 2)):
-            sl = slice(b * P, (b + 1) * P)
-            acc = banks[(6, 3, 7, 0)[i]][:, :P]
-            mx(acc, w2_c, w2_s, 0, z_c[:, sl], z_s[:, sl])
-            if i < 3:
-                nc.scalar.copy(o_sb[:, sl], acc)
+        w2_codes = keep.tile([P, N], U32, name="w2_codes", tag="h2", align_bytes=64)
+        quantize(w2_codes[:], w2_scales[:], w2_quads[:])
+        by_two_targets = "p e (c i) -> p c e i"
+        nc.vector.tensor_tensor(
+            z[LAST][:].rearrange("p (c i t) -> p c t i", t=QUAD, i=2)[:, :, 2:],
+            late[:, :, 0, :].rearrange(by_two_targets, i=2),
+            late[:, :, 1, :].rearrange(by_two_targets, i=2),
+            ADD,
+        )
+
+        order = (0, 1, LAST, 2)
+        z_codes = {}
+        for b in order:
+            tag = "z0" if b == LAST else f"z_codes{b}"
+            z_codes[b] = keep.tile([P, P], U32, name=f"z_codes{b}", tag=tag, align_bytes=64)
+            quantize(z_codes[b][:], z_scales[:, b * P : (b + 1) * P], z[b][:])
+        layer2_banks = {0: 0, 1: 4, LAST: 3, 2: 1}
+        for b in order:
+            cols = slice(b * P, (b + 1) * P)
+            acc = banks[layer2_banks[b]][:, :P]
+            product(acc, w2_codes[:], w2_scales[:], z_codes[b][:], z_scales[:, cols])
+            if b != order[-1]:
+                nc.scalar.copy(result[:, cols], acc)
             else:
-                nc.vector.tensor_copy(out=o_sb[:, sl], in_=acc)
-            if i != 2:
-                sl = slice(P, TURNED) if i == 3 else sl
-                nc.sync.dma_start(out=out[:, sl], in_=o_sb[:, sl])
+                nc.vector.tensor_copy(out=result[:, cols], in_=acc)
+            nc.sync.dma_start(out=out[:, cols], in_=result[:, cols])

@@ -24,8 +24,8 @@ PER_COLUMN = 16
 LAST = V // P - 1
 TURNED = LAST * P
 
-ROW_CHUNKS = (((0, 1024), (1024, 768), (1792, 256)),) + 3 * (((0, 1280), (1280, 768)),)
-VECTOR_NODES = (384, 384, 320, 320)
+ROW_CHUNKS = (((0, 1024), (1024, 768), (1792, 256)),) + 3 * (((0, 1024), (1024, 1024)),)
+VECTOR_NODES = (576, 448, 448, 320)
 NODE_PIECES = ((0, 256), (256, 256), (512, 256), (768, 128), (896, 128))
 LAST_GATHER = 768
 
@@ -91,6 +91,10 @@ def tile_picked_sage_silu_e_kernel(tc, xT, w1, w2, gate, offs, pos1, pos2, out):
             for i, (c0, n) in enumerate(ROW_CHUNKS[j]):
                 if j == 0 and i != 1:
                     nc.scalar.activation(row_bf16[j][:, c0 : c0 + n], row_f32[j][:, c0 : c0 + n], COPY)
+                elif j > 0 and i == 0:
+                    nc.gpsimd.tensor_scalar(
+                        row_bf16[j][:, c0 : c0 + n], row_f32[j][:, c0 : c0 + n], 1.0, 0.0, MULT, ADD
+                    )
                 else:
                     nc.vector.tensor_copy(out=row_bf16[j][:, c0 : c0 + n], in_=row_f32[j][:, c0 : c0 + n])
             split = VECTOR_NODES[j]

@@ -24,8 +24,14 @@ PER_COLUMN = 16
 LAST = V // P - 1
 TURNED = LAST * P
 
-ROW_CHUNKS = (((0, 1024), (1024, 768), (1792, 256)),) + 3 * (((0, 1024), (1024, 1024)),)
-VECTOR_NODES = (576, 448, 448, 320)
+ROW_LOADS = ((T,), (1024, 1024), (1024, 1024), (768, 896, 384))
+ROW_ROUNDS = (
+    (("scalar", 1088), ("gpsimd", 960)),
+    (("gpsimd", 1024), ("vector", 1024)),
+    (("gpsimd", 1024), ("vector", 1024)),
+    (("gpsimd", 768), ("vector", 896), ("vector", 384)),
+)
+VECTOR_NODES = (576, 448, 384, 320)
 NODE_PIECES = ((0, 256), (256, 256), (512, 256), (768, 128), (896, 128))
 LAST_GATHER = 768
 
@@ -68,10 +74,12 @@ def tile_picked_sage_silu_e_kernel(tc, xT, w1, w2, gate, offs, pos1, pos2, out):
 
         x_view = xT.rearrange("(p j) t -> p j t", j=QUAD)
         for j in range(QUAD):
-            for c0, n in ROW_CHUNKS[j]:
+            c0 = 0
+            for n in ROW_LOADS[j]:
                 nc.sync.dma_start(out=row_f32[j][:, c0 : c0 + n], in_=x_view[:, j, c0 : c0 + n])
-                if j == 0 and c0 == 0:
-                    nc.sync.dma_start(out=offs_sb[:], in_=offs)
+                c0 = c0 + n
+            if j == 0:
+                nc.sync.dma_start(out=offs_sb[:], in_=offs)
         w1_view = w1.rearrange("(p j) c -> p j c", j=QUAD)
         for i in range(2):
             nc.sync.dma_start(out=w1_raw[i][:], in_=w1_view[:, :, i * H // 2 : (i + 1) * H // 2])
@@ -88,15 +96,16 @@ def tile_picked_sage_silu_e_kernel(tc, xT, w1, w2, gate, offs, pos1, pos2, out):
 
         picked_quads = picked[:].rearrange("p (s j) -> p s j", j=QUAD)
         for j in range(QUAD):
-            for i, (c0, n) in enumerate(ROW_CHUNKS[j]):
-                if j == 0 and i != 1:
-                    nc.scalar.activation(row_bf16[j][:, c0 : c0 + n], row_f32[j][:, c0 : c0 + n], COPY)
-                elif j > 0 and i == 0:
-                    nc.gpsimd.tensor_scalar(
-                        row_bf16[j][:, c0 : c0 + n], row_f32[j][:, c0 : c0 + n], 1.0, 0.0, MULT, ADD
-                    )
+            c0 = 0
+            for engine, n in ROW_ROUNDS[j]:
+                dst, src = row_bf16[j][:, c0 : c0 + n], row_f32[j][:, c0 : c0 + n]
+                if engine == "scalar":
+                    nc.scalar.activation(dst, src, COPY)
+                elif engine == "gpsimd":
+                    nc.gpsimd.tensor_scalar(dst, src, 1.0, 0.0, MULT, ADD)
                 else:
-                    nc.vector.tensor_copy(out=row_bf16[j][:, c0 : c0 + n], in_=row_f32[j][:, c0 : c0 + n])
+                    nc.vector.tensor_copy(out=dst, in_=src)
+                c0 = c0 + n
             split = VECTOR_NODES[j]
             nc.vector.tensor_copy(out=picked_quads[:, :split, j], in_=row_f32[j][:].indirect(entries(offs_sb, 0, split)))
             cuts = (split, S) if j < QUAD - 1 else (split, LAST_GATHER, S)

@@ -102,7 +102,7 @@ def tile_picked_sage_silu_e_kernel(tc, xT, w1, w2, gate, offs, pos1, pos2, out):
                 if engine == "scalar":
                     nc.scalar.activation(dst, src, COPY)
                 elif engine == "gpsimd":
-                    nc.gpsimd.tensor_scalar(dst, src, 1.0, 0.0, MULT, ADD)
+                    nc.gpsimd.tensor_copy(out=dst, in_=src)
                 else:
                     nc.vector.tensor_copy(out=dst, in_=src)
                 c0 = c0 + n

@@ -29,9 +29,9 @@ ROW_ROUNDS = (
     (("scalar", 1088), ("gpsimd", 960)),
     (("gpsimd", 1024), ("vector", 1024)),
     (("gpsimd", 1024), ("vector", 1024)),
-    (("gpsimd", 768), ("vector", 896), ("vector", 384)),
+    (("gpsimd", 768), ("vector", 896), ("gpsimd", 384)),
 )
-VECTOR_NODES = (576, 448, 384, 320)
+VECTOR_NODES = (576, 448, 384, 352)
 NODE_PIECES = ((0, 256), (256, 256), (512, 256), (768, 128), (896, 128))
 LAST_GATHER = 768
 

@@ -31,7 +31,7 @@ ROW_ROUNDS = (
     (("gpsimd", 1024), ("vector", 1024)),
     (("gpsimd", 768), ("vector", 896), ("gpsimd", 384)),
 )
-VECTOR_NODES = (576, 448, 384, 352)
+VECTOR_NODES = (576, 448, 384, 384)
 NODE_PIECES = ((0, 256), (256, 256), (512, 256), (768, 128), (896, 128))
 LAST_GATHER = 768
 
@@ -178,31 +178,34 @@ def tile_picked_sage_silu_e_kernel(tc, xT, w1, w2, gate, offs, pos1, pos2, out):
             for d in range(D):
                 fetch(t, d, TURNED, P, late[:, t - 2, d, :])
 
-        def add_turned(t, b):
-            for d in range(D):
-                nc.tensor.matmul(
-                    banks[1 + b][:, t % 2 * P : (t % 2 + 1) * P],
-                    lhsT=gated[d][:, t, b * P : (b + 1) * P],
-                    rhs=ident[:],
-                    start=(d == 0),
-                    stop=(d == D - 1),
-                    is_transpose=True,
-                )
+        def add_turned(t, b, d):
+            nc.tensor.matmul(
+                banks[1 + b][:, t % 2 * P : (t % 2 + 1) * P],
+                lhsT=gated[d][:, t, b * P : (b + 1) * P],
+                rhs=ident[:],
+                start=(d == 0),
+                stop=(d == D - 1),
+                is_transpose=True,
+            )
 
         back = banks[5:8]
         last_first = (LAST,) + tuple(range(LAST))
         last_low_words = banks[1 + LAST][:, 2 * P : 3 * P]
         for t in range(2):
             for b in last_first:
-                add_turned(t, b)
+                for d in range(D):
+                    add_turned(t, b, d)
         for b in last_first:
             nc.scalar.copy(low[b][:], banks[1 + b][:, : 2 * P])
             nc.tensor.transpose(back[b][:, :P] if b < LAST else last_low_words, low[b][:].bitcast(F32), ident[:])
         z_words = [z[b][:].bitcast(F32).rearrange("p (v u) -> p v u", u=2) for b in range(LAST + 1)]
         nc.scalar.copy(z_words[LAST][:, :, 0], last_low_words)
-        for t in (2, 3):
+        for b in range(LAST):
+            for d in range(D):
+                add_turned(2, b, d)
+        for d in range(D):
             for b in range(LAST):
-                add_turned(t, b)
+                add_turned(3, b, d)
         for b in range(LAST):
             nc.scalar.copy(
                 high[b][:].rearrange("v (p e) -> v p e", e=2),

@@ -31,7 +31,7 @@ ROW_ROUNDS = (
     (("gpsimd", 1024), ("vector", 1024)),
     (("gpsimd", 768), ("vector", 896), ("gpsimd", 384)),
 )
-VECTOR_NODES = (576, 448, 384, 384)
+VECTOR_NODES = (512, 384, 384, 384)
 NODE_PIECES = ((0, 256), (256, 256), (512, 256), (768, 128), (896, 128))
 LAST_GATHER = 768
 

@@ -21,19 +21,11 @@ P = 128
 QUAD = 4
 BANK = 512
 PER_COLUMN = 16
-LAST = V // P - 1
-TURNED = LAST * P
-
-ROW_LOADS = ((T,), (1024, 1024), (1024, 1024), (768, 896, 384))
-ROW_ROUNDS = (
-    (("scalar", 1088), ("gpsimd", 960)),
-    (("gpsimd", 1024), ("vector", 1024)),
-    (("gpsimd", 1024), ("vector", 1024)),
-    (("gpsimd", 768), ("vector", 896), ("gpsimd", 384)),
-)
-VECTOR_NODES = (512, 384, 384, 384)
-NODE_PIECES = ((0, 256), (256, 256), (512, 256), (768, 128), (896, 128))
-LAST_GATHER = 768
+BLOCKS = V // P
+TURNED = 2
+SPLIT = 448
+LAST_ROW_CUTS = (SPLIT, 768, S)
+NODE_PIECE = 256
 
 
 def tile_picked_sage_silu_e_kernel(tc, xT, w1, w2, gate, offs, pos1, pos2, out):
@@ -43,30 +35,31 @@ def tile_picked_sage_silu_e_kernel(tc, xT, w1, w2, gate, offs, pos1, pos2, out):
         psum = ctx.enter_context(tc.psum_pool(name="psum", bufs=1))
 
         offs_sb = keep.tile([P, S // PER_COLUMN], U16, name="offs_sb")
-        pos1_sb = keep.tile([P, V // PER_COLUMN], U16, name="pos1_sb")
-        pos2_sb = keep.tile([P, V // PER_COLUMN], U16, name="pos2_sb")
-        gate0_tile = keep.tile([P, 2 * V], F32, name="gate0", align_bytes=64)
-        gate1_tile = keep.tile([P, V], F32, name="gate1", align_bytes=64)
-        gate_sb = (gate0_tile[:, :V], gate1_tile[:])
-        w1_raw = [keep.tile([P, QUAD, H // 2], F32, name=f"w1_raw{i}", tag=f"raw{i}", align_bytes=64) for i in range(2)]
-        w2_raw = keep.tile([P, QUAD, N], F32, name="w2_raw")
-        w1_lo = [keep.tile([P, P * QUAD], BF16, name=f"w1_lo{i}", align_bytes=64) for i in range(2)]
-        w1_codes = keep.tile([P, H], U32, name="w1_codes", align_bytes=64)
-        w1_scales = keep.tile([P, H], U8, name="w1_scales", align_bytes=64)
-        w2_scales = keep.tile([P, N], U8, name="w2_scales", align_bytes=64)
-        row_f32 = [keep.tile([P, T], F32, name=f"row_f32_{j}", align_bytes=64) for j in range(QUAD)]
-        row_bf16 = [keep.tile([P, T], BF16, name=f"row_bf16_{j}", align_bytes=64) for j in range(QUAD)]
-        picked = keep.tile([P, S * QUAD], BF16, name="picked", align_bytes=64)
+        pos_sb = [keep.tile([P, V // PER_COLUMN], U16, name=f"pos_sb{d}") for d in range(D)]
+        gate_sb = [keep.tile([P, V], F32, name=f"gate{d}", align_bytes=64) for d in range(D)]
+        gate_col = [keep.tile([P, TURNED], F32, name=f"gate_col{d}", align_bytes=64) for d in range(D)]
+        rows = [keep.tile([P, T], F32, name=f"row{j}", align_bytes=64) for j in range(QUAD)]
+        planes = [keep.tile([P, 2, S - SPLIT], BF16, name=f"planes{u}", align_bytes=64) for u in range(2)]
+        picked = keep.tile([P, S * QUAD], BF16, name="picked", tag="picked", align_bytes=64)
         x_scales = keep.tile([P, S], U8, name="x_scales", align_bytes=64)
+        w1_raw = [keep.tile([P, QUAD, H // 2], F32, name=f"w1_raw{i}", tag=f"raw{i}", align_bytes=64) for i in range(2)]
+        w1_quads = [keep.tile([P, 2 * P * QUAD], BF16, name=f"w1_quads{u}", align_bytes=64) for u in range(2)]
+        w1_codes = {0: keep.tile([P, P], U32, name="codes0", align_bytes=64)[:]}
+        codes_hi = keep.tile([P, 2 * P], U32, name="codes_hi", align_bytes=64)
+        w1_scales = keep.tile([P, H], U8, name="w1_scales", align_bytes=64)
+        w2_raw = keep.tile([P, QUAD, N], F32, name="w2_raw")
+        w2_codes = keep.tile([P, N], U32, name="w2_codes", align_bytes=64)
+        w2_scales = keep.tile([P, N], U8, name="w2_scales", align_bytes=64)
         h = [keep.tile([P, S], F32, name=f"h{t}", tag=f"h{t}", align_bytes=64) for t in range(QUAD)]
         gated = [keep.tile([P, QUAD, V], F32, name=f"gated{d}", align_bytes=64) for d in range(D)]
-        z = [keep.tile([P, P * QUAD], BF16, name=f"z{b}", tag=f"z{b}", align_bytes=64) for b in range(LAST + 1)]
-        low = [keep.tile([P, 2 * P], BF16, name=f"low{b}", align_bytes=64) for b in range(LAST + 1)]
-        high = [keep.tile([P, 2 * P], BF16, name=f"high{b}", align_bytes=64) for b in range(LAST)]
+        scaled = [keep.tile([P, 2 * P], F32, name=f"scaled{b}", tag=f"scaled{b}", align_bytes=64) for b in range(TURNED)]
+        pairs = [keep.tile([P, 2, 2 * P], BF16, name=f"pairs{b}", align_bytes=64) for b in range(TURNED)]
+        z_codes = keep.tile([P, V], U32, name="z_codes", align_bytes=64)
         z_scales = keep.tile([P, V], U8, name="z_scales", align_bytes=64)
         result = keep.tile([P, V], F32, name="result", align_bytes=64)
         ident = keep.tile([P, P], F32, name="ident", align_bytes=64)
         warm = keep.tile([P, 1], F32, name="warm")
+        banks = [psum.tile([P, BANK], F32, name=f"bank{i}") for i in range(8)]
 
         nc.vector.memset(warm[:], 0.0)
         nc.scalar.activation(warm[:], warm[:], SILU)
@@ -74,68 +67,25 @@ def tile_picked_sage_silu_e_kernel(tc, xT, w1, w2, gate, offs, pos1, pos2, out):
 
         x_view = xT.rearrange("(p j) t -> p j t", j=QUAD)
         for j in range(QUAD):
-            c0 = 0
-            for n in ROW_LOADS[j]:
-                nc.sync.dma_start(out=row_f32[j][:, c0 : c0 + n], in_=x_view[:, j, c0 : c0 + n])
-                c0 = c0 + n
+            nc.sync.dma_start(out=rows[j][:], in_=x_view[:, j, :])
             if j == 0:
                 nc.sync.dma_start(out=offs_sb[:], in_=offs)
         w1_view = w1.rearrange("(p j) c -> p j c", j=QUAD)
         for i in range(2):
             nc.sync.dma_start(out=w1_raw[i][:], in_=w1_view[:, :, i * H // 2 : (i + 1) * H // 2])
-        for d, (pos_sb, pos) in enumerate(((pos1_sb, pos1), (pos2_sb, pos2))):
-            nc.sync.dma_start(out=pos_sb[:], in_=pos)
-            nc.sync.dma_start(out=gate_sb[d], in_=gate[d])
+        for d, pos in enumerate((pos1, pos2)):
+            nc.sync.dma_start(out=pos_sb[d][:], in_=pos)
+            nc.sync.dma_start(out=gate_sb[d][:], in_=gate[d])
         nc.sync.dma_start(out=w2_raw[:], in_=w2.rearrange("(p j) n -> p j n", j=QUAD))
+        with nc.allow_non_contiguous_dma(reason="one gate weight a partition"):
+            for d in range(D):
+                nc.sync.dma_start(out=gate_col[d][:], in_=gate[d, 0, : TURNED * P].rearrange("(b p) -> p b", p=P))
 
         def entries(list_sb, first, n):
             return list_sb[:, first // PER_COLUMN : (first + n) // PER_COLUMN]
 
         def quantize(codes, scales, quads):
             nc.vector.quantize_mx(out=codes.bitcast(FP8X4), scales=scales, in_=quads)
-
-        picked_quads = picked[:].rearrange("p (s j) -> p s j", j=QUAD)
-        for j in range(QUAD):
-            c0 = 0
-            for engine, n in ROW_ROUNDS[j]:
-                dst, src = row_bf16[j][:, c0 : c0 + n], row_f32[j][:, c0 : c0 + n]
-                if engine == "scalar":
-                    nc.scalar.activation(dst, src, COPY)
-                elif engine == "gpsimd":
-                    nc.gpsimd.tensor_copy(out=dst, in_=src)
-                else:
-                    nc.vector.tensor_copy(out=dst, in_=src)
-                c0 = c0 + n
-            split = VECTOR_NODES[j]
-            nc.vector.tensor_copy(out=picked_quads[:, :split, j], in_=row_f32[j][:].indirect(entries(offs_sb, 0, split)))
-            cuts = (split, S) if j < QUAD - 1 else (split, LAST_GATHER, S)
-            for s0, s1 in zip(cuts, cuts[1:]):
-                nc.scalar.activation(
-                    picked_quads[:, s0:s1, j], row_bf16[j][:].indirect(entries(offs_sb, s0, s1 - s0)), COPY
-                )
-
-        w1_src = [w1_raw[i][:].rearrange("p j (c t) -> p c j t", t=QUAD) for i in range(2)]
-        w1_hi = keep.tile([P, 2 * P * QUAD], BF16, name="w1_hi", align_bytes=64)
-
-        def weave_w1_half(i):
-            nc.vector.tensor_copy(
-                out=w1_lo[i][:].rearrange("p (c e j) -> p c j e", e=2, j=QUAD), in_=w1_src[i][:, :, :, :2]
-            )
-            nc.vector.tensor_copy(
-                out=w1_hi[:].rearrange("p (e c j) -> p c j e", e=2, j=QUAD)[:, i * P // 2 : (i + 1) * P // 2],
-                in_=w1_src[i][:, :, :, 2:],
-            )
-
-        weave_w1_half(0)
-        quantize(w1_codes[:, :P], w1_scales[:, :P], w1_lo[0][:])
-        x_codes = keep.tile([P, S], U32, name="x_codes", tag="raw0", align_bytes=64)
-        for s0, n in NODE_PIECES:
-            quantize(x_codes[:, s0 : s0 + n], x_scales[:, s0 : s0 + n], picked[:, QUAD * s0 : QUAD * (s0 + n)])
-        weave_w1_half(1)
-        quantize(w1_codes[:, P : 2 * P], w1_scales[:, P : 2 * P], w1_lo[1][:])
-        quantize(w1_codes[:, 2 * P :], w1_scales[:, 2 * P :], w1_hi[:])
-
-        banks = [psum.tile([P, BANK], F32, name=f"bank{i}") for i in range(8)]
 
         def product(acc, w_codes, w_scales, codes, scales):
             nc.tensor.matmul_mx(
@@ -148,94 +98,135 @@ def tile_picked_sage_silu_e_kernel(tc, xT, w1, w2, gate, offs, pos1, pos2, out):
                 stop=True,
             )
 
-        layer1_banks = ((0, 1, 2, 3, 4), (3, 4), (5, 6), (7, 0))
-        for t in range(QUAD):
+        picked_quads = picked[:].rearrange("p (s j) -> p s j", j=QUAD)
+        for j in range(QUAD):
+            u, e = divmod(j, 2)
+            nc.vector.tensor_copy(out=picked_quads[:, :SPLIT, j], in_=rows[j][:].indirect(entries(offs_sb, 0, SPLIT)))
+            nc.scalar.activation(planes[u][:, e, :], rows[j][:].indirect(entries(offs_sb, SPLIT, S - SPLIT)), COPY)
+            if j == 1:
+                nc.gpsimd.tensor_copy(out=picked_quads[:, SPLIT:, :2], in_=planes[0][:].rearrange("p e s -> p s e"))
+        for s0, s1 in zip(LAST_ROW_CUTS, LAST_ROW_CUTS[1:]):
+            pairs_of_rows = planes[1][:, :, s0 - SPLIT : s1 - SPLIT].rearrange("p e s -> p s e")
+            nc.scalar.copy(picked_quads[:, s0:s1, 2:], pairs_of_rows)
+
+        w1_src = [w1_raw[i][:].rearrange("p j (c t) -> p c j t", t=QUAD) for i in range(2)]
+
+        def weave_w1(i, u):
+            dst = w1_quads[u][:].rearrange("p (e c j) -> p c j e", e=2, j=QUAD)[:, i * P // 2 : (i + 1) * P // 2]
+            nc.vector.tensor_copy(dst, w1_src[i][:, :, :, 2 * u : 2 * u + 2])
+
+        def node_codes(s0, n):
+            return first_codes[:, s0 : s0 + n] if s0 < NODE_PIECE else other_codes[:, s0 - NODE_PIECE : s0 - NODE_PIECE + n]
+
+        def quantize_nodes(i):
+            s0, s1 = i * NODE_PIECE, (i + 1) * NODE_PIECE
+            quantize(node_codes(s0, NODE_PIECE), x_scales[:, s0:s1], picked[:, QUAD * s0 : QUAD * s1])
+
+        for u in range(2):
+            weave_w1(0, u)
+        first_codes = keep.tile([P, NODE_PIECE], U32, name="first_codes", tag="raw0", align_bytes=64)
+        quantize_nodes(0)
+        for u in range(2):
+            weave_w1(1, u)
+        other_codes = keep.tile([P, S - NODE_PIECE], U32, name="other_codes", tag="raw1", align_bytes=64)
+        quantize(w1_codes[0], w1_scales[:, :P], w1_quads[0][:, : P * QUAD])
+        for i in range(1, S // NODE_PIECE):
+            quantize_nodes(i)
+        quantize(codes_hi[:], w1_scales[:, 2 * P :], w1_quads[1][:])
+        w1_codes[2], w1_codes[3] = codes_hi[:, :P], codes_hi[:, P:]
+        w1_codes[1] = keep.tile([P, P], U32, name="codes1", tag="picked", align_bytes=64)[:]
+        quantize(w1_codes[1], w1_scales[:, P : 2 * P], w1_quads[0][:, P * QUAD :])
+
+        bank_of = {0: (0, 1, 2, 3), 2: (4, 5), 3: (6, 7), 1: (3, 2)}
+        for t in bank_of:
             cols = slice(t * P, (t + 1) * P)
-            for (s0, n), bank in zip(NODE_PIECES if t == 0 else ((0, BANK), (BANK, BANK)), layer1_banks[t]):
-                nodes = slice(s0, s0 + n)
-                product(banks[bank][:, :n], w1_codes[:, cols], w1_scales[:, cols], x_codes[:, nodes], x_scales[:, nodes])
+            n = S // len(bank_of[t])
+            for i, bank in enumerate(bank_of[t]):
+                nodes = slice(i * n, (i + 1) * n)
+                width = NODE_PIECE if i == 0 else n
+                for s0 in range(i * n, (i + 1) * n, width):
+                    acc = banks[bank][:, s0 - i * n : s0 - i * n + width]
+                    product(acc, w1_codes[t], w1_scales[:, cols], node_codes(s0, width), x_scales[:, s0 : s0 + width])
                 nc.scalar.activation(h[t][:, nodes], banks[bank][:, :n], SILU)
 
-        w2_quads = keep.tile([P, N * QUAD], BF16, name="w2_quads", tag="raw0", align_bytes=64)
+        def window(t, d, v0, n):
+            return h[t][:].indirect(entries(pos_sb[d], v0, n))
+
+        def fetch(t, d, v0, n):
+            nc.vector.tensor_tensor(gated[d][:, t, v0 : v0 + n], window(t, d, v0, n), gate_sb[d][:, v0 : v0 + n], MULT)
+
+        def turn(dst, src, start=True, stop=True):
+            nc.tensor.matmul(dst, lhsT=src, rhs=ident[:], start=start, stop=stop, is_transpose=True)
+
+        def add_turned(t):
+            for b in range(TURNED):
+                for d in range(D):
+                    src = gated[d][:, t, b * P : (b + 1) * P]
+                    turn(banks[b][:, t * P : (t + 1) * P], src, d == 0, d == D - 1)
+
+        half = TURNED * P
+        for d in range(D):
+            fetch(0, d, 0, V)
+        add_turned(0)
+        for t in (2, 3):
+            for d in range(D):
+                fetch(t, d, half, V - half)
+        for d in range(D):
+            for t in (2, 3):
+                nc.scalar.activation(gated[d][:, t, :half], window(t, d, 0, half), COPY)
+                for b in range(TURNED):
+                    place = (2 * b + t - 2) * P
+                    turn(banks[4 + d][:, place : place + P], gated[d][:, t, b * P : (b + 1) * P])
+        for v0 in (0, half):
+            for d in range(D):
+                fetch(1, d, v0, half)
+        add_turned(1)
+
+        def by_pairs(bank, b):
+            return bank[:, 2 * b * P : 2 * (b + 1) * P].rearrange("v (e p) -> v p e", e=2)
+
+        for b in range(TURNED):
+            nc.scalar.activation(
+                scaled[b][:].rearrange("v (p e) -> v p e", e=2), by_pairs(banks[4], b), COPY, scale=gate_col[0][:, b : b + 1]
+            )
+        for b in range(TURNED):
+            nc.scalar.copy(pairs[b][:, 0, :].rearrange("v (p e) -> v p e", e=2), by_pairs(banks[b], 0))
+            nc.tensor.transpose(banks[6 + b][:, :P], pairs[b][:, 0, :].bitcast(F32), ident[:])
+        w2_quads = keep.tile([P, N * QUAD], BF16, name="w2_quads", tag="raw1", align_bytes=64)
         nc.scalar.activation(
             w2_quads[:].rearrange("p (n j) -> p n j", j=QUAD), w2_raw[:].rearrange("p j n -> p n j"), COPY
         )
-
-        def fetch(t, d, v0, n, dst):
-            offsets = entries((pos1_sb, pos2_sb)[d], v0, n)
-            nc.vector.tensor_tensor(dst, h[t][:].indirect(offsets), gate_sb[d][:, v0 : v0 + n], MULT)
-
-        for t in range(2):
-            for d in range(D):
-                fetch(t, d, 0, V, gated[d][:, t, :])
-        for d in range(D):
-            fetch(2, d, 0, TURNED, gated[d][:, 2, :TURNED])
-        fetch(3, 0, 0, TURNED, gated[0][:, 3, :TURNED])
-        fetch(3, 1, 0, 2 * P, gated[1][:, 3, : 2 * P])
-        fetch(3, 1, 2 * P, P, gated[1][:, 3, 2 * P : TURNED])
-        late = gate0_tile[:].rearrange("p (e d r) -> p e d r", e=2, r=P)
-        for t in (2, 3):
-            for d in range(D):
-                fetch(t, d, TURNED, P, late[:, t - 2, d, :])
-
-        def add_turned(t, b, d):
-            nc.tensor.matmul(
-                banks[1 + b][:, t % 2 * P : (t % 2 + 1) * P],
-                lhsT=gated[d][:, t, b * P : (b + 1) * P],
-                rhs=ident[:],
-                start=(d == 0),
-                stop=(d == D - 1),
-                is_transpose=True,
+        for b in range(TURNED):
+            nc.vector.scalar_tensor_tensor(
+                pairs[b][:, 1, :].rearrange("v (p e) -> v p e", e=2),
+                by_pairs(banks[5], b),
+                gate_col[1][:, b : b + 1],
+                scaled[b][:].rearrange("v (p e) -> v p e", e=2),
+                MULT,
+                ADD,
             )
-
-        back = banks[5:8]
-        last_first = (LAST,) + tuple(range(LAST))
-        last_low_words = banks[1 + LAST][:, 2 * P : 3 * P]
-        for t in range(2):
-            for b in last_first:
-                for d in range(D):
-                    add_turned(t, b, d)
-        for b in last_first:
-            nc.scalar.copy(low[b][:], banks[1 + b][:, : 2 * P])
-            nc.tensor.transpose(back[b][:, :P] if b < LAST else last_low_words, low[b][:].bitcast(F32), ident[:])
-        z_words = [z[b][:].bitcast(F32).rearrange("p (v u) -> p v u", u=2) for b in range(LAST + 1)]
-        nc.scalar.copy(z_words[LAST][:, :, 0], last_low_words)
-        for b in range(LAST):
-            for d in range(D):
-                add_turned(2, b, d)
-        for d in range(D):
-            for b in range(LAST):
-                add_turned(3, b, d)
-        for b in range(LAST):
+            nc.tensor.transpose(banks[6 + b][:, P : 2 * P], pairs[b][:, 1, :].bitcast(F32), ident[:])
+        z = {}
+        for b in range(TURNED):
+            z[b] = keep.tile([P, P * QUAD], BF16, name=f"z{b}", align_bytes=64)
             nc.scalar.copy(
-                high[b][:].rearrange("v (p e) -> v p e", e=2),
-                banks[1 + b][:, : 2 * P].rearrange("v (e p) -> v p e", e=2),
+                z[b][:].bitcast(F32).rearrange("p (v u) -> p v u", u=2),
+                banks[6 + b][:, : 2 * P].rearrange("p (u v) -> p v u", u=2),
             )
-            nc.tensor.transpose(back[b][:, P : 2 * P], high[b][:].bitcast(F32), ident[:])
-        for b in range(LAST):
-            nc.scalar.copy(z_words[b], back[b][:, : 2 * P].rearrange("p (u v) -> p v u", u=2))
+        for b in range(TURNED, BLOCKS):
+            z[b] = keep.tile([P, P * QUAD], BF16, name=f"z{b}", tag=f"scaled{b - TURNED}", align_bytes=64)
+            both = [gated[d][:, :, b * P : (b + 1) * P].rearrange("p t (c i) -> p c t i", i=2) for d in range(D)]
+            nc.vector.tensor_tensor(z[b][:].rearrange("p (c i t) -> p c t i", t=QUAD, i=2), both[0], both[1], ADD)
 
-        w2_codes = keep.tile([P, N], U32, name="w2_codes", tag="h2", align_bytes=64)
         quantize(w2_codes[:], w2_scales[:], w2_quads[:])
-        by_two_targets = "p e (c i) -> p c e i"
-        nc.vector.tensor_tensor(
-            z[LAST][:].rearrange("p (c i t) -> p c t i", t=QUAD, i=2)[:, :, 2:],
-            late[:, :, 0, :].rearrange(by_two_targets, i=2),
-            late[:, :, 1, :].rearrange(by_two_targets, i=2),
-            ADD,
-        )
-
-        order = (0, 1, LAST, 2)
-        z_codes = {}
-        for b in order:
-            tag = "z0" if b == LAST else f"z_codes{b}"
-            z_codes[b] = keep.tile([P, P], U32, name=f"z_codes{b}", tag=tag, align_bytes=64)
-            quantize(z_codes[b][:], z_scales[:, b * P : (b + 1) * P], z[b][:])
-        layer2_banks = {0: 0, 1: 4, LAST: 3, 2: 1}
+        order = (2, 3, 0, 1)
         for b in order:
             cols = slice(b * P, (b + 1) * P)
-            acc = banks[layer2_banks[b]][:, :P]
-            product(acc, w2_codes[:], w2_scales[:], z_codes[b][:], z_scales[:, cols])
+            quantize(z_codes[:, cols], z_scales[:, cols], z[b][:])
+        for b in order:
+            cols = slice(b * P, (b + 1) * P)
+            acc = banks[2 + b][:, :P]
+            product(acc, w2_codes[:], w2_scales[:], z_codes[:, cols], z_scales[:, cols])
             if b != order[-1]:
                 nc.scalar.copy(result[:, cols], acc)
             else:

@@ -23,9 +23,10 @@ BANK = 512
 PER_COLUMN = 16
 BLOCKS = V // P
 TURNED = 2
-SPLIT = 448
-LAST_ROW_CUTS = (SPLIT, 768, S)
-NODE_PIECE = 256
+SPLITS = (448, 448)
+GPSIMD_END = 576
+LAST_ROW_CUTS = (GPSIMD_END, 768, S)
+NODE_PIECES = ((0, 256), (256, 256), (512, 256), (768, 128), (896, 128))
 
 
 def tile_picked_sage_silu_e_kernel(tc, xT, w1, w2, gate, offs, pos1, pos2, out):
@@ -37,24 +38,23 @@ def tile_picked_sage_silu_e_kernel(tc, xT, w1, w2, gate, offs, pos1, pos2, out):
         offs_sb = keep.tile([P, S // PER_COLUMN], U16, name="offs_sb")
         pos_sb = [keep.tile([P, V // PER_COLUMN], U16, name=f"pos_sb{d}") for d in range(D)]
         gate_sb = [keep.tile([P, V], F32, name=f"gate{d}", align_bytes=64) for d in range(D)]
-        gate_col = [keep.tile([P, TURNED], F32, name=f"gate_col{d}", align_bytes=64) for d in range(D)]
+        gate_col = [keep.tile([P, TURNED], F32, name=f"gate_col{d}", tag=f"gate_col{d}", align_bytes=64) for d in range(D)]
         rows = [keep.tile([P, T], F32, name=f"row{j}", align_bytes=64) for j in range(QUAD)]
-        planes = [keep.tile([P, 2, S - SPLIT], BF16, name=f"planes{u}", align_bytes=64) for u in range(2)]
-        picked = keep.tile([P, S * QUAD], BF16, name="picked", tag="picked", align_bytes=64)
+        planes = [keep.tile([P, 2, S - SPLITS[u]], BF16, name=f"planes{u}", align_bytes=64) for u in range(2)]
+        picked = keep.tile([P, S * QUAD], BF16, name="picked", align_bytes=64)
         x_scales = keep.tile([P, S], U8, name="x_scales", align_bytes=64)
         w1_raw = [keep.tile([P, QUAD, H // 2], F32, name=f"w1_raw{i}", tag=f"raw{i}", align_bytes=64) for i in range(2)]
-        w1_quads = [keep.tile([P, 2 * P * QUAD], BF16, name=f"w1_quads{u}", align_bytes=64) for u in range(2)]
-        w1_codes = {0: keep.tile([P, P], U32, name="codes0", align_bytes=64)[:]}
-        codes_hi = keep.tile([P, 2 * P], U32, name="codes_hi", align_bytes=64)
+        w1_lo = [keep.tile([P, P * QUAD], BF16, name=f"w1_lo{i}", align_bytes=64) for i in range(2)]
+        w1_hi = keep.tile([P, 2 * P * QUAD], BF16, name="w1_hi", align_bytes=64)
+        w1_codes = keep.tile([P, H], U32, name="w1_codes", align_bytes=64)
         w1_scales = keep.tile([P, H], U8, name="w1_scales", align_bytes=64)
         w2_raw = keep.tile([P, QUAD, N], F32, name="w2_raw")
         w2_codes = keep.tile([P, N], U32, name="w2_codes", align_bytes=64)
         w2_scales = keep.tile([P, N], U8, name="w2_scales", align_bytes=64)
         h = [keep.tile([P, S], F32, name=f"h{t}", tag=f"h{t}", align_bytes=64) for t in range(QUAD)]
-        gated = [keep.tile([P, QUAD, V], F32, name=f"gated{d}", align_bytes=64) for d in range(D)]
-        scaled = [keep.tile([P, 2 * P], F32, name=f"scaled{b}", tag=f"scaled{b}", align_bytes=64) for b in range(TURNED)]
-        pairs = [keep.tile([P, 2, 2 * P], BF16, name=f"pairs{b}", align_bytes=64) for b in range(TURNED)]
-        z_codes = keep.tile([P, V], U32, name="z_codes", align_bytes=64)
+        gated = [keep.tile([P, QUAD + 1, V], F32, name=f"gated{d}", tag=f"gated{d}", align_bytes=64) for d in range(D)]
+        high = keep.tile([P, TURNED, 2 * P], BF16, name="high", align_bytes=64)
+        added_codes = keep.tile([P, V // 2], U32, name="added_codes", align_bytes=64)
         z_scales = keep.tile([P, V], U8, name="z_scales", align_bytes=64)
         result = keep.tile([P, V], F32, name="result", align_bytes=64)
         ident = keep.tile([P, P], F32, name="ident", align_bytes=64)
@@ -99,61 +99,63 @@ def tile_picked_sage_silu_e_kernel(tc, xT, w1, w2, gate, offs, pos1, pos2, out):
             )
 
         picked_quads = picked[:].rearrange("p (s j) -> p s j", j=QUAD)
+
+        def lay(copy, u, s0, s1):
+            src = planes[u][:, :, s0 - SPLITS[u] : s1 - SPLITS[u]].rearrange("p e s -> p s e")
+            copy(picked_quads[:, s0:s1, 2 * u : 2 * u + 2], src)
+
         for j in range(QUAD):
             u, e = divmod(j, 2)
-            nc.vector.tensor_copy(out=picked_quads[:, :SPLIT, j], in_=rows[j][:].indirect(entries(offs_sb, 0, SPLIT)))
-            nc.scalar.activation(planes[u][:, e, :], rows[j][:].indirect(entries(offs_sb, SPLIT, S - SPLIT)), COPY)
+            split = SPLITS[u]
+            nc.vector.tensor_copy(out=picked_quads[:, :split, j], in_=rows[j][:].indirect(entries(offs_sb, 0, split)))
+            cuts = (split, GPSIMD_END, S) if j == QUAD - 1 else (split, S)
+            for s0, s1 in zip(cuts, cuts[1:]):
+                plane = planes[u][:, e, s0 - split : s1 - split]
+                nc.scalar.activation(plane, rows[j][:].indirect(entries(offs_sb, s0, s1 - s0)), COPY)
             if j == 1:
-                nc.gpsimd.tensor_copy(out=picked_quads[:, SPLIT:, :2], in_=planes[0][:].rearrange("p e s -> p s e"))
+                lay(nc.gpsimd.tensor_copy, 0, split, S)
+        lay(nc.gpsimd.tensor_copy, 1, SPLITS[1], GPSIMD_END)
         for s0, s1 in zip(LAST_ROW_CUTS, LAST_ROW_CUTS[1:]):
-            pairs_of_rows = planes[1][:, :, s0 - SPLIT : s1 - SPLIT].rearrange("p e s -> p s e")
-            nc.scalar.copy(picked_quads[:, s0:s1, 2:], pairs_of_rows)
+            lay(nc.scalar.copy, 1, s0, s1)
 
         w1_src = [w1_raw[i][:].rearrange("p j (c t) -> p c j t", t=QUAD) for i in range(2)]
+        by_column = "p (e c j) -> p c j e"
 
-        def weave_w1(i, u):
-            dst = w1_quads[u][:].rearrange("p (e c j) -> p c j e", e=2, j=QUAD)[:, i * P // 2 : (i + 1) * P // 2]
-            nc.vector.tensor_copy(dst, w1_src[i][:, :, :, 2 * u : 2 * u + 2])
+        def weave_w1_half(i):
+            nc.vector.tensor_copy(w1_lo[i][:].rearrange(by_column, e=2, j=QUAD), w1_src[i][:, :, :, :2])
+            upper = w1_hi[:].rearrange(by_column, e=2, j=QUAD)[:, i * P // 2 : (i + 1) * P // 2]
+            nc.vector.tensor_copy(upper, w1_src[i][:, :, :, 2:])
 
-        def node_codes(s0, n):
-            return first_codes[:, s0 : s0 + n] if s0 < NODE_PIECE else other_codes[:, s0 - NODE_PIECE : s0 - NODE_PIECE + n]
+        weave_w1_half(0)
+        quantize(w1_codes[:, :P], w1_scales[:, :P], w1_lo[0][:])
+        x_codes = keep.tile([P, S], U32, name="x_codes", tag="raw0", align_bytes=64)
+        for s0, n in NODE_PIECES:
+            quantize(x_codes[:, s0 : s0 + n], x_scales[:, s0 : s0 + n], picked[:, QUAD * s0 : QUAD * (s0 + n)])
+        weave_w1_half(1)
+        quantize(w1_codes[:, P : 2 * P], w1_scales[:, P : 2 * P], w1_lo[1][:])
+        quantize(w1_codes[:, 2 * P :], w1_scales[:, 2 * P :], w1_hi[:])
 
-        def quantize_nodes(i):
-            s0, s1 = i * NODE_PIECE, (i + 1) * NODE_PIECE
-            quantize(node_codes(s0, NODE_PIECE), x_scales[:, s0:s1], picked[:, QUAD * s0 : QUAD * s1])
-
-        for u in range(2):
-            weave_w1(0, u)
-        first_codes = keep.tile([P, NODE_PIECE], U32, name="first_codes", tag="raw0", align_bytes=64)
-        quantize_nodes(0)
-        for u in range(2):
-            weave_w1(1, u)
-        other_codes = keep.tile([P, S - NODE_PIECE], U32, name="other_codes", tag="raw1", align_bytes=64)
-        quantize(w1_codes[0], w1_scales[:, :P], w1_quads[0][:, : P * QUAD])
-        for i in range(1, S // NODE_PIECE):
-            quantize_nodes(i)
-        quantize(codes_hi[:], w1_scales[:, 2 * P :], w1_quads[1][:])
-        w1_codes[2], w1_codes[3] = codes_hi[:, :P], codes_hi[:, P:]
-        w1_codes[1] = keep.tile([P, P], U32, name="codes1", tag="picked", align_bytes=64)[:]
-        quantize(w1_codes[1], w1_scales[:, P : 2 * P], w1_quads[0][:, P * QUAD :])
-
-        bank_of = {0: (0, 1, 2, 3), 2: (4, 5), 3: (6, 7), 1: (3, 2)}
-        for t in bank_of:
+        layer1_banks = ((0, 1, 2, 3, 4), (3, 4), (5, 6), (7, 0))
+        for t in range(QUAD):
             cols = slice(t * P, (t + 1) * P)
-            n = S // len(bank_of[t])
-            for i, bank in enumerate(bank_of[t]):
-                nodes = slice(i * n, (i + 1) * n)
-                width = NODE_PIECE if i == 0 else n
-                for s0 in range(i * n, (i + 1) * n, width):
-                    acc = banks[bank][:, s0 - i * n : s0 - i * n + width]
-                    product(acc, w1_codes[t], w1_scales[:, cols], node_codes(s0, width), x_scales[:, s0 : s0 + width])
+            for (s0, n), bank in zip(NODE_PIECES if t == 0 else ((0, BANK), (BANK, BANK)), layer1_banks[t]):
+                nodes = slice(s0, s0 + n)
+                product(banks[bank][:, :n], w1_codes[:, cols], w1_scales[:, cols], x_codes[:, nodes], x_scales[:, nodes])
                 nc.scalar.activation(h[t][:, nodes], banks[bank][:, :n], SILU)
+            if t == 0:
+                w2_quads = keep.tile([P, N * QUAD], BF16, name="w2_quads", tag="raw1", align_bytes=64)
+                nc.scalar.activation(
+                    w2_quads[:].rearrange("p (n j) -> p n j", j=QUAD), w2_raw[:].rearrange("p j n -> p n j"), COPY
+                )
+
+        place_of = (0, QUAD, 2, 3)
 
         def window(t, d, v0, n):
             return h[t][:].indirect(entries(pos_sb[d], v0, n))
 
         def fetch(t, d, v0, n):
-            nc.vector.tensor_tensor(gated[d][:, t, v0 : v0 + n], window(t, d, v0, n), gate_sb[d][:, v0 : v0 + n], MULT)
+            dst = gated[d][:, place_of[t], v0 : v0 + n]
+            nc.vector.tensor_tensor(dst, window(t, d, v0, n), gate_sb[d][:, v0 : v0 + n], MULT)
 
         def turn(dst, src, start=True, stop=True):
             nc.tensor.matmul(dst, lhsT=src, rhs=ident[:], start=start, stop=stop, is_transpose=True)
@@ -161,72 +163,85 @@ def tile_picked_sage_silu_e_kernel(tc, xT, w1, w2, gate, offs, pos1, pos2, out):
         def add_turned(t):
             for b in range(TURNED):
                 for d in range(D):
-                    src = gated[d][:, t, b * P : (b + 1) * P]
-                    turn(banks[b][:, t * P : (t + 1) * P], src, d == 0, d == D - 1)
+                    src = gated[d][:, place_of[t], b * P : (b + 1) * P]
+                    turn(banks[1 + b][:, t * P : (t + 1) * P], src, d == 0, d == D - 1)
 
         half = TURNED * P
+        lower, upper = slice(0, P // 2), slice(P // 2, P)
         for d in range(D):
             fetch(0, d, 0, V)
+            nc.sync.dma_start(out=gated[d][lower, 1, half:], in_=gated[d][upper, 0, half:])
         add_turned(0)
-        for t in (2, 3):
-            for d in range(D):
-                fetch(t, d, half, V - half)
         for d in range(D):
-            for t in (2, 3):
+            fetch(1, d, half, V - half)
+            nc.sync.dma_start(out=gated[d][upper, 0, half:], in_=gated[d][lower, QUAD, half:])
+            nc.sync.dma_start(out=gated[d][upper, 1, half:], in_=gated[d][upper, QUAD, half:])
+        for d in range(D):
+            fetch(1, d, 0, half)
+        add_turned(1)
+        for d in range(D):
+            fetch(2, d, half, V - half)
+        fetch(3, 0, half, V - half)
+        for b in range(TURNED, BLOCKS):
+            fetch(3, 1, b * P, P)
+        for d in range(D):
+            for t in (3, 2):
                 nc.scalar.activation(gated[d][:, t, :half], window(t, d, 0, half), COPY)
                 for b in range(TURNED):
                     place = (2 * b + t - 2) * P
-                    turn(banks[4 + d][:, place : place + P], gated[d][:, t, b * P : (b + 1) * P])
-        for v0 in (0, half):
-            for d in range(D):
-                fetch(1, d, v0, half)
-        add_turned(1)
+                    turn(banks[3 + d][:, place : place + P], gated[d][:, t, b * P : (b + 1) * P])
 
         def by_pairs(bank, b):
             return bank[:, 2 * b * P : 2 * (b + 1) * P].rearrange("v (e p) -> v p e", e=2)
 
+        scaled = keep.tile([P, TURNED, 2 * P], F32, name="scaled", tag="h2", align_bytes=64)
         for b in range(TURNED):
             nc.scalar.activation(
-                scaled[b][:].rearrange("v (p e) -> v p e", e=2), by_pairs(banks[4], b), COPY, scale=gate_col[0][:, b : b + 1]
+                scaled[:, b, :].rearrange("v (p e) -> v p e", e=2), by_pairs(banks[3], b), COPY, scale=gate_col[0][:, b : b + 1]
             )
+        low = keep.tile([P, TURNED, 2 * P], BF16, name="low", tag="gate_col0", align_bytes=64)
         for b in range(TURNED):
-            nc.scalar.copy(pairs[b][:, 0, :].rearrange("v (p e) -> v p e", e=2), by_pairs(banks[b], 0))
-            nc.tensor.transpose(banks[6 + b][:, :P], pairs[b][:, 0, :].bitcast(F32), ident[:])
-        w2_quads = keep.tile([P, N * QUAD], BF16, name="w2_quads", tag="raw1", align_bytes=64)
-        nc.scalar.activation(
-            w2_quads[:].rearrange("p (n j) -> p n j", j=QUAD), w2_raw[:].rearrange("p j n -> p n j"), COPY
-        )
+            nc.scalar.copy(
+                low[:, b, :].rearrange("v (i c e) -> v i c e", i=2, e=2),
+                banks[1 + b][:, : 2 * P].rearrange("v (i e c) -> v i c e", i=2, e=2),
+            )
+            nc.tensor.transpose(banks[5 + b][:, :P], low[:, b, :].bitcast(F32), ident[:])
+        quantize(w2_codes[:], w2_scales[:], w2_quads[:])
+        z = {}
+
+        def add_block(b, tag):
+            z[b] = keep.tile([P, P * QUAD], BF16, name=f"z{b}", tag=tag, align_bytes=64)
+            both = [gated[d][:, :QUAD, b * P : (b + 1) * P].rearrange("p t (c i) -> p c t i", i=2) for d in range(D)]
+            nc.vector.tensor_tensor(z[b][:].rearrange("p (c i t) -> p c t i", t=QUAD, i=2), both[0], both[1], ADD)
+
+        add_block(2, "z2")
         for b in range(TURNED):
             nc.vector.scalar_tensor_tensor(
-                pairs[b][:, 1, :].rearrange("v (p e) -> v p e", e=2),
-                by_pairs(banks[5], b),
+                high[:, b, :].rearrange("v (p e) -> v p e", e=2),
+                by_pairs(banks[4], b),
                 gate_col[1][:, b : b + 1],
-                scaled[b][:].rearrange("v (p e) -> v p e", e=2),
+                scaled[:, b, :].rearrange("v (p e) -> v p e", e=2),
                 MULT,
                 ADD,
             )
-            nc.tensor.transpose(banks[6 + b][:, P : 2 * P], pairs[b][:, 1, :].bitcast(F32), ident[:])
-        z = {}
+            nc.tensor.transpose(banks[5 + b][:, P : 2 * P], high[:, b, :].bitcast(F32), ident[:])
         for b in range(TURNED):
             z[b] = keep.tile([P, P * QUAD], BF16, name=f"z{b}", align_bytes=64)
             nc.scalar.copy(
                 z[b][:].bitcast(F32).rearrange("p (v u) -> p v u", u=2),
-                banks[6 + b][:, : 2 * P].rearrange("p (u v) -> p v u", u=2),
+                banks[5 + b][:, : 2 * P].rearrange("p (u v) -> p v u", u=2),
             )
-        for b in range(TURNED, BLOCKS):
-            z[b] = keep.tile([P, P * QUAD], BF16, name=f"z{b}", tag=f"scaled{b - TURNED}", align_bytes=64)
-            both = [gated[d][:, :, b * P : (b + 1) * P].rearrange("p t (c i) -> p c t i", i=2) for d in range(D)]
-            nc.vector.tensor_tensor(z[b][:].rearrange("p (c i t) -> p c t i", t=QUAD, i=2), both[0], both[1], ADD)
 
-        quantize(w2_codes[:], w2_scales[:], w2_quads[:])
+        add_block(3, "h2")
         order = (2, 3, 0, 1)
+        turned_codes = keep.tile([P, V // 2], U32, name="turned_codes", tag="gated0", align_bytes=64)
+        z_codes = (turned_codes[:, :P], turned_codes[:, P:], added_codes[:, :P], added_codes[:, P:])
+        for b in order:
+            quantize(z_codes[b], z_scales[:, b * P : (b + 1) * P], z[b][:])
         for b in order:
             cols = slice(b * P, (b + 1) * P)
-            quantize(z_codes[:, cols], z_scales[:, cols], z[b][:])
-        for b in order:
-            cols = slice(b * P, (b + 1) * P)
-            acc = banks[2 + b][:, :P]
-            product(acc, w2_codes[:], w2_scales[:], z_codes[:, cols], z_scales[:, cols])
+            acc = banks[(1, 2, 7, 0)[b]][:, :P]
+            product(acc, w2_codes[:], w2_scales[:], z_codes[b], z_scales[:, cols])
             if b != order[-1]:
                 nc.scalar.copy(result[:, cols], acc)
             else:

@@ -23,9 +23,9 @@ BANK = 512
 PER_COLUMN = 16
 BLOCKS = V // P
 TURNED = 2
-SPLITS = (448, 448)
-GPSIMD_END = 576
-LAST_ROW_CUTS = (GPSIMD_END, 768, S)
+SPLITS = (512, 448)
+GPSIMD_END = 640
+SCALAR_LAYS = ((SPLITS[1], SPLITS[0]), (GPSIMD_END, 768), (768, S))
 NODE_PIECES = ((0, 256), (256, 256), (512, 256), (768, 128), (896, 128))
 
 
@@ -108,14 +108,14 @@ def tile_picked_sage_silu_e_kernel(tc, xT, w1, w2, gate, offs, pos1, pos2, out):
             u, e = divmod(j, 2)
             split = SPLITS[u]
             nc.vector.tensor_copy(out=picked_quads[:, :split, j], in_=rows[j][:].indirect(entries(offs_sb, 0, split)))
-            cuts = (split, GPSIMD_END, S) if j == QUAD - 1 else (split, S)
-            for s0, s1 in zip(cuts, cuts[1:]):
+            last_row = ((SPLITS[0], GPSIMD_END), (split, SPLITS[0]), (GPSIMD_END, S))
+            for s0, s1 in last_row if j == QUAD - 1 else ((split, S),):
                 plane = planes[u][:, e, s0 - split : s1 - split]
                 nc.scalar.activation(plane, rows[j][:].indirect(entries(offs_sb, s0, s1 - s0)), COPY)
             if j == 1:
                 lay(nc.gpsimd.tensor_copy, 0, split, S)
-        lay(nc.gpsimd.tensor_copy, 1, SPLITS[1], GPSIMD_END)
-        for s0, s1 in zip(LAST_ROW_CUTS, LAST_ROW_CUTS[1:]):
+        lay(nc.gpsimd.tensor_copy, 1, SPLITS[0], GPSIMD_END)
+        for s0, s1 in SCALAR_LAYS:
             lay(nc.scalar.copy, 1, s0, s1)
 
         w1_src = [w1_raw[i][:].rearrange("p j (c t) -> p c j t", t=QUAD) for i in range(2)]
@@ -184,20 +184,20 @@ def tile_picked_sage_silu_e_kernel(tc, xT, w1, w2, gate, offs, pos1, pos2, out):
         fetch(3, 0, half, V - half)
         for b in range(TURNED, BLOCKS):
             fetch(3, 1, b * P, P)
+        plain = ((banks[3][:, : 2 * P], banks[3][:, 2 * P :]), (banks[4][:, : 2 * P], banks[7][:, : 2 * P]))
         for d in range(D):
             for t in (3, 2):
                 nc.scalar.activation(gated[d][:, t, :half], window(t, d, 0, half), COPY)
                 for b in range(TURNED):
-                    place = (2 * b + t - 2) * P
-                    turn(banks[3 + d][:, place : place + P], gated[d][:, t, b * P : (b + 1) * P])
+                    turn(plain[d][b][:, (t - 2) * P : (t - 1) * P], gated[d][:, t, b * P : (b + 1) * P])
 
-        def by_pairs(bank, b):
-            return bank[:, 2 * b * P : 2 * (b + 1) * P].rearrange("v (e p) -> v p e", e=2)
+        def by_pairs(sums):
+            return sums.rearrange("v (e p) -> v p e", e=2)
 
         scaled = keep.tile([P, TURNED, 2 * P], F32, name="scaled", tag="h2", align_bytes=64)
         for b in range(TURNED):
             nc.scalar.activation(
-                scaled[:, b, :].rearrange("v (p e) -> v p e", e=2), by_pairs(banks[3], b), COPY, scale=gate_col[0][:, b : b + 1]
+                scaled[:, b, :].rearrange("v (p e) -> v p e", e=2), by_pairs(plain[0][b]), COPY, scale=gate_col[0][:, b : b + 1]
             )
         low = keep.tile([P, TURNED, 2 * P], BF16, name="low", tag="gate_col0", align_bytes=64)
         for b in range(TURNED):
@@ -218,7 +218,7 @@ def tile_picked_sage_silu_e_kernel(tc, xT, w1, w2, gate, offs, pos1, pos2, out):
         for b in range(TURNED):
             nc.vector.scalar_tensor_tensor(
                 high[:, b, :].rearrange("v (p e) -> v p e", e=2),
-                by_pairs(banks[4], b),
+                by_pairs(plain[1][b]),
                 gate_col[1][:, b : b + 1],
                 scaled[:, b, :].rearrange("v (p e) -> v p e", e=2),
                 MULT,
@@ -240,7 +240,7 @@ def tile_picked_sage_silu_e_kernel(tc, xT, w1, w2, gate, offs, pos1, pos2, out):
             quantize(z_codes[b], z_scales[:, b * P : (b + 1) * P], z[b][:])
         for b in order:
             cols = slice(b * P, (b + 1) * P)
-            acc = banks[(1, 2, 7, 0)[b]][:, :P]
+            acc = banks[(1, 2, 3, 0)[b]][:, :P]
             product(acc, w2_codes[:], w2_scales[:], z_codes[b], z_scales[:, cols])
             if b != order[-1]:
                 nc.scalar.copy(result[:, cols], acc)

from contextlib import ExitStack

import concourse.mybir as mybir
from concourse.masks import make_identity

K, T, D, S, V, H, N = 512, 2048, 2, 1024, 512, 512, 128
FLOPS = 2 * K * H * S + 2 * H * N * V

F32 = mybir.dt.float32
BF16 = mybir.dt.bfloat16
U32 = mybir.dt.uint32
U16 = mybir.dt.uint16
U8 = mybir.dt.uint8
FP8X4 = mybir.dt.float8_e4m3fn_x4
COPY = mybir.ActivationFunctionType.Copy
SILU = mybir.ActivationFunctionType.Silu
ADD = mybir.AluOpType.add
MULT = mybir.AluOpType.mult

P = 128
QUAD = 4
BANK = 512
PER_COLUMN = 16
BLOCKS = V // P
TURNED = 2
SPLITS = (512, 448)
GPSIMD_END = 640
SCALAR_LAYS = ((SPLITS[1], SPLITS[0]), (GPSIMD_END, 768), (768, S))
NODE_PIECES = ((0, 256), (256, 256), (512, 256), (768, 128), (896, 128))


def tile_picked_sage_silu_e_kernel(tc, xT, w1, w2, gate, offs, pos1, pos2, out):
    nc = tc.nc
    with ExitStack() as ctx:
        keep = ctx.enter_context(tc.tile_pool(name="keep", bufs=1))
        psum = ctx.enter_context(tc.psum_pool(name="psum", bufs=1))

        offs_sb = keep.tile([P, S // PER_COLUMN], U16, name="offs_sb")
        pos_sb = [keep.tile([P, V // PER_COLUMN], U16, name=f"pos_sb{d}") for d in range(D)]
        gate_sb = [keep.tile([P, V], F32, name=f"gate{d}", align_bytes=64) for d in range(D)]
        gate_col = [keep.tile([P, TURNED], F32, name=f"gate_col{d}", tag=f"gate_col{d}", align_bytes=64) for d in range(D)]
        rows = [keep.tile([P, T], F32, name=f"row{j}", align_bytes=64) for j in range(QUAD)]
        planes = [keep.tile([P, 2, S - SPLITS[u]], BF16, name=f"planes{u}", align_bytes=64) for u in range(2)]
        picked = keep.tile([P, S * QUAD], BF16, name="picked", align_bytes=64)
        x_scales = keep.tile([P, S], U8, name="x_scales", align_bytes=64)
        w1_raw = [keep.tile([P, QUAD, H // 2], F32, name=f"w1_raw{i}", tag=f"raw{i}", align_bytes=64) for i in range(2)]
        w1_lo = [keep.tile([P, P * QUAD], BF16, name=f"w1_lo{i}", align_bytes=64) for i in range(2)]
        w1_hi = keep.tile([P, 2 * P * QUAD], BF16, name="w1_hi", align_bytes=64)
        w1_codes = keep.tile([P, H], U32, name="w1_codes", align_bytes=64)
        w1_scales = keep.tile([P, H], U8, name="w1_scales", align_bytes=64)
        w2_raw = keep.tile([P, QUAD, N], F32, name="w2_raw")
        w2_codes = keep.tile([P, N], U32, name="w2_codes", align_bytes=64)
        w2_scales = keep.tile([P, N], U8, name="w2_scales", align_bytes=64)
        h = [keep.tile([P, S], F32, name=f"h{t}", tag=f"h{t}", align_bytes=64) for t in range(QUAD)]
        gated = [keep.tile([P, QUAD + 1, V], F32, name=f"gated{d}", tag=f"gated{d}", align_bytes=64) for d in range(D)]
        high = keep.tile([P, TURNED, 2 * P], BF16, name="high", align_bytes=64)
        added_codes = keep.tile([P, V // 2], U32, name="added_codes", align_bytes=64)
        z_scales = keep.tile([P, V], U8, name="z_scales", align_bytes=64)
        result = keep.tile([P, V], F32, name="result", align_bytes=64)
        ident = keep.tile([P, P], F32, name="ident", align_bytes=64)
        warm = keep.tile([P, 1], F32, name="warm")
        banks = [psum.tile([P, BANK], F32, name=f"bank{i}") for i in range(8)]

        nc.vector.memset(warm[:], 0.0)
        nc.scalar.activation(warm[:], warm[:], SILU)
        make_identity(nc, ident[:])

        x_view = xT.rearrange("(p j) t -> p j t", j=QUAD)
        for j in range(QUAD):
            nc.sync.dma_start(out=rows[j][:], in_=x_view[:, j, :])
            if j == 0:
                nc.sync.dma_start(out=offs_sb[:], in_=offs)
        w1_view = w1.rearrange("(p j) c -> p j c", j=QUAD)
        for i in range(2):
            nc.sync.dma_start(out=w1_raw[i][:], in_=w1_view[:, :, i * H // 2 : (i + 1) * H // 2])
        for d, pos in enumerate((pos1, pos2)):
            nc.sync.dma_start(out=pos_sb[d][:], in_=pos)
            nc.sync.dma_start(out=gate_sb[d][:], in_=gate[d])
        nc.sync.dma_start(out=w2_raw[:], in_=w2.rearrange("(p j) n -> p j n", j=QUAD))
        with nc.allow_non_contiguous_dma(reason="one gate weight a partition"):
            for d in range(D):
                nc.sync.dma_start(out=gate_col[d][:], in_=gate[d, 0, : TURNED * P].rearrange("(b p) -> p b", p=P))

        def entries(list_sb, first, n):
            return list_sb[:, first // PER_COLUMN : (first + n) // PER_COLUMN]

        def quantize(codes, scales, quads):
            nc.vector.quantize_mx(out=codes.bitcast(FP8X4), scales=scales, in_=quads)

        def product(acc, w_codes, w_scales, codes, scales):
            nc.tensor.matmul_mx(
                out=acc,
                lhsT=w_codes.bitcast(FP8X4),
                lhsT_scale=w_scales,
                rhs=codes.bitcast(FP8X4),
                rhs_scale=scales,
                start=True,
                stop=True,
            )

        picked_quads = picked[:].rearrange("p (s j) -> p s j", j=QUAD)

        def lay(copy, u, s0, s1):
            src = planes[u][:, :, s0 - SPLITS[u] : s1 - SPLITS[u]].rearrange("p e s -> p s e")
            copy(picked_quads[:, s0:s1, 2 * u : 2 * u + 2], src)

        for j in range(QUAD):
            u, e = divmod(j, 2)
            split = SPLITS[u]
            nc.vector.tensor_copy(out=picked_quads[:, :split, j], in_=rows[j][:].indirect(entries(offs_sb, 0, split)))
            last_row = ((SPLITS[0], GPSIMD_END), (split, SPLITS[0]), (GPSIMD_END, S))
            for s0, s1 in last_row if j == QUAD - 1 else ((split, S),):
                plane = planes[u][:, e, s0 - split : s1 - split]
                nc.scalar.activation(plane, rows[j][:].indirect(entries(offs_sb, s0, s1 - s0)), COPY)
            if j == 1:
                lay(nc.gpsimd.tensor_copy, 0, split, S)
        lay(nc.gpsimd.tensor_copy, 1, SPLITS[0], GPSIMD_END)
        for s0, s1 in SCALAR_LAYS:
            lay(nc.scalar.copy, 1, s0, s1)

        w1_src = [w1_raw[i][:].rearrange("p j (c t) -> p c j t", t=QUAD) for i in range(2)]
        by_column = "p (e c j) -> p c j e"

        def weave_w1_half(i):
            nc.vector.tensor_copy(w1_lo[i][:].rearrange(by_column, e=2, j=QUAD), w1_src[i][:, :, :, :2])
            upper = w1_hi[:].rearrange(by_column, e=2, j=QUAD)[:, i * P // 2 : (i + 1) * P // 2]
            nc.vector.tensor_copy(upper, w1_src[i][:, :, :, 2:])

        weave_w1_half(0)
        quantize(w1_codes[:, :P], w1_scales[:, :P], w1_lo[0][:])
        x_codes = keep.tile([P, S], U32, name="x_codes", tag="raw0", align_bytes=64)
        for s0, n in NODE_PIECES:
            quantize(x_codes[:, s0 : s0 + n], x_scales[:, s0 : s0 + n], picked[:, QUAD * s0 : QUAD * (s0 + n)])
        weave_w1_half(1)
        quantize(w1_codes[:, P : 2 * P], w1_scales[:, P : 2 * P], w1_lo[1][:])
        quantize(w1_codes[:, 2 * P :], w1_scales[:, 2 * P :], w1_hi[:])

        layer1_banks = ((0, 1, 2, 3, 4), (3, 4), (5, 6), (7, 0))
        for t in range(QUAD):
            cols = slice(t * P, (t + 1) * P)
            for (s0, n), bank in zip(NODE_PIECES if t == 0 else ((0, BANK), (BANK, BANK)), layer1_banks[t]):
                nodes = slice(s0, s0 + n)
                product(banks[bank][:, :n], w1_codes[:, cols], w1_scales[:, cols], x_codes[:, nodes], x_scales[:, nodes])
                nc.scalar.activation(h[t][:, nodes], banks[bank][:, :n], SILU)
            if t == 0:
                w2_quads = keep.tile([P, N * QUAD], BF16, name="w2_quads", tag="raw1", align_bytes=64)
                nc.scalar.activation(
                    w2_quads[:].rearrange("p (n j) -> p n j", j=QUAD), w2_raw[:].rearrange("p j n -> p n j"), COPY
                )

        place_of = (0, QUAD, 2, 3)

        def window(t, d, v0, n):
            return h[t][:].indirect(entries(pos_sb[d], v0, n))

        def fetch(t, d, v0, n):
            dst = gated[d][:, place_of[t], v0 : v0 + n]
            nc.vector.tensor_tensor(dst, window(t, d, v0, n), gate_sb[d][:, v0 : v0 + n], MULT)

        def turn(dst, src, start=True, stop=True):
            nc.tensor.matmul(dst, lhsT=src, rhs=ident[:], start=start, stop=stop, is_transpose=True)

        def add_turned(t):
            for b in range(TURNED):
                for d in range(D):
                    src = gated[d][:, place_of[t], b * P : (b + 1) * P]
                    turn(banks[1 + b][:, t * P : (t + 1) * P], src, d == 0, d == D - 1)

        half = TURNED * P
        lower, upper = slice(0, P // 2), slice(P // 2, P)
        for d in range(D):
            fetch(0, d, 0, V)
            nc.sync.dma_start(out=gated[d][lower, 1, half:], in_=gated[d][upper, 0, half:])
        add_turned(0)
        for d in range(D):
            fetch(1, d, half, V - half)
            nc.sync.dma_start(out=gated[d][upper, 0, half:], in_=gated[d][lower, QUAD, half:])
            nc.sync.dma_start(out=gated[d][upper, 1, half:], in_=gated[d][upper, QUAD, half:])
        for d in range(D):
            fetch(1, d, 0, half)
        add_turned(1)
        for d in range(D):
            fetch(2, d, half, V - half)
        fetch(3, 0, half, V - half)
        for b in range(TURNED, BLOCKS):
            fetch(3, 1, b * P, P)
        plain = ((banks[3][:, : 2 * P], banks[3][:, 2 * P :]), (banks[4][:, : 2 * P], banks[7][:, : 2 * P]))
        for d in range(D):
            for t in (3, 2):
                nc.scalar.activation(gated[d][:, t, :half], window(t, d, 0, half), COPY)
                for b in range(TURNED):
                    turn(plain[d][b][:, (t - 2) * P : (t - 1) * P], gated[d][:, t, b * P : (b + 1) * P])

        def by_pairs(sums):
            return sums.rearrange("v (e p) -> v p e", e=2)

        scaled = keep.tile([P, TURNED, 2 * P], F32, name="scaled", tag="h2", align_bytes=64)
        for b in range(TURNED):
            nc.scalar.activation(
                scaled[:, b, :].rearrange("v (p e) -> v p e", e=2), by_pairs(plain[0][b]), COPY, scale=gate_col[0][:, b : b + 1]
            )
        low = keep.tile([P, TURNED, 2 * P], BF16, name="low", tag="gate_col0", align_bytes=64)
        for b in range(TURNED):
            nc.scalar.copy(
                low[:, b, :].rearrange("v (i c e) -> v i c e", i=2, e=2),
                banks[1 + b][:, : 2 * P].rearrange("v (i e c) -> v i c e", i=2, e=2),
            )
            nc.tensor.transpose(banks[5 + b][:, :P], low[:, b, :].bitcast(F32), ident[:])
        quantize(w2_codes[:], w2_scales[:], w2_quads[:])
        z = {}

        def add_block(b, tag):
            z[b] = keep.tile([P, P * QUAD], BF16, name=f"z{b}", tag=tag, align_bytes=64)
            both = [gated[d][:, :QUAD, b * P : (b + 1) * P].rearrange("p t (c i) -> p c t i", i=2) for d in range(D)]
            nc.vector.tensor_tensor(z[b][:].rearrange("p (c i t) -> p c t i", t=QUAD, i=2), both[0], both[1], ADD)

        add_block(2, "z2")
        for b in range(TURNED):
            nc.vector.scalar_tensor_tensor(
                high[:, b, :].rearrange("v (p e) -> v p e", e=2),
                by_pairs(plain[1][b]),
                gate_col[1][:, b : b + 1],
                scaled[:, b, :].rearrange("v (p e) -> v p e", e=2),
                MULT,
                ADD,
            )
            nc.tensor.transpose(banks[5 + b][:, P : 2 * P], high[:, b, :].bitcast(F32), ident[:])
        for b in range(TURNED):
            z[b] = keep.tile([P, P * QUAD], BF16, name=f"z{b}", align_bytes=64)
            nc.scalar.copy(
                z[b][:].bitcast(F32).rearrange("p (v u) -> p v u", u=2),
                banks[5 + b][:, : 2 * P].rearrange("p (u v) -> p v u", u=2),
            )

        add_block(3, "h2")
        order = (2, 3, 0, 1)
        turned_codes = keep.tile([P, V // 2], U32, name="turned_codes", tag="gated0", align_bytes=64)
        z_codes = (turned_codes[:, :P], turned_codes[:, P:], added_codes[:, :P], added_codes[:, P:])
        for b in order:
            quantize(z_codes[b], z_scales[:, b * P : (b + 1) * P], z[b][:])
        for b in order:
            cols = slice(b * P, (b + 1) * P)
            acc = banks[(1, 2, 3, 0)[b]][:, :P]
            product(acc, w2_codes[:], w2_scales[:], z_codes[b], z_scales[:, cols])
            if b != order[-1]:
                nc.scalar.copy(result[:, cols], acc)
            else:
                nc.vector.tensor_copy(out=result[:, cols], in_=acc)
            nc.sync.dma_start(out=out[:, cols], in_=result[:, cols])
